import numpy as np
import ml_dtypes


def mxq(x, axis, fmt="e4m3"):
    dtype, down = {"e4m3": (ml_dtypes.float8_e4m3fn, 7), "e5m2": (ml_dtypes.float8_e5m2, 14)}[fmt]
    v = np.moveaxis(np.asarray(x, np.float32).astype(ml_dtypes.bfloat16).astype(np.float64), axis, -1)
    blocks = v.reshape(v.shape[:-1] + (-1, 32))
    amax = np.abs(blocks).max(-1, keepdims=True)
    byte = np.maximum(np.where(amax > 0, np.frexp(amax)[1] - 1 + 127, 0) - down, 1)
    scale = np.exp2(byte - 127.0)
    codes = (blocks / scale).astype(np.float32).astype(dtype).astype(np.float64)
    return np.moveaxis((codes * scale).reshape(v.shape), -1, axis)


WIDE = False


def mx_kscale(k):
    if not WIDE:
        return np.ones(k)
    levels = np.array([10, -10, 5, -5, 0])
    if k % 512:
        return np.exp2(np.random.permutation(np.resize(levels, k // 32))).repeat(32)
    a = np.empty((k // 512, 16))
    for p in range(k // 512):
        a[p, :8] = np.random.permutation(np.resize(levels, 8))
        for g in range(8):
            far = levels[np.abs(levels - a[p, g]) >= 10]
            a[p, g + 8] = far[np.random.randint(len(far))]
    return np.exp2(a.ravel()).repeat(32)


def f64(x):
    return np.asarray(x).astype(np.float64)


def striped(idx):
    return np.tile(idx.reshape(-1, 16).T, (8, 1)).astype(np.uint16)


def unstriped(offs):
    return offs[:16].T.reshape(-1).astype(np.int64)


E2M1 = np.array([0.0, 0.5, 1.0, 1.5, 2.0, 3.0, 4.0, 6.0, -0.0, -0.5, -1.0, -1.5, -2.0, -3.0, -4.0, -6.0])


def pack_weight(w, fmt):
    k, n = w.shape
    w = f64(np.asarray(w, np.float32).astype(ml_dtypes.bfloat16)).reshape(k // 32, 32, n)
    amax = np.abs(w).max(1)
    if fmt == "e4m3":
        byte = np.frexp(amax)[1] - 1 + 127 - 7
    else:
        mant, ex = np.frexp(amax / 6.0)
        byte = np.where(mant > 0.5, ex, ex - 1) + 127
    byte = np.clip(np.where(amax > 0, byte, 1), 1, 254)
    scaled = (w * np.exp2(127.0 - byte)[:, None, :]).reshape(k, n).astype(np.float32)
    by_word = np.ascontiguousarray(scaled.reshape(k // 512, 128, 4, n).transpose(0, 1, 3, 2))
    if fmt == "e4m3":
        words = by_word.astype(ml_dtypes.float8_e4m3fn).view(np.uint8)
    else:
        c = by_word.astype(ml_dtypes.float4_e2m1fn).view(np.uint8) & 0xF
        words = (c[..., 0::2] | (c[..., 1::2] << 4)).reshape(k // 512, 128, 2 * n)
    return np.ascontiguousarray(words), np.ascontiguousarray(byte.astype(np.uint8).reshape(k // 512, 16, n))


def unpack_weight(words, scales, fmt):
    g, _, n = scales.shape
    words = np.ascontiguousarray(words).reshape(g, 128, n, -1)
    if fmt == "e4m3":
        vals = words.view(ml_dtypes.float8_e4m3fn).astype(np.float64)
    else:
        nib = np.empty((g, 128, n, 4), np.uint8)
        nib[..., 0::2] = words & 0xF
        nib[..., 1::2] = words >> 4
        vals = E2M1[nib]
    vals = vals * np.repeat(np.exp2(scales.astype(np.float64) - 127.0), 8, axis=1)[..., None]
    return vals.transpose(0, 1, 3, 2).reshape(g * 512, n)


def gelu(v):
    return 0.5 * v * (1.0 + np.tanh(np.sqrt(2.0 / np.pi) * (v + 0.044715 * v**3)))


def pack_table4(v):
    words, scales = pack_weight(v, "e2m1")
    g, t = words.shape[0] // 2, v.shape[1]
    words = words.reshape(g, 2, 128, t, 2).transpose(0, 2, 3, 1, 4)
    return np.concatenate([words.reshape(g, -1), scales.reshape(g, -1)], axis=1)


def unpack_table4(tab):
    g, t = tab.shape[0], tab.shape[1] // 544
    words = tab[:, :512 * t].reshape(g, 128, t, 2, 2).transpose(0, 3, 1, 2, 4).reshape(2 * g, 128, 2 * t)
    return unpack_weight(words, tab[:, 512 * t:].reshape(2 * g, 16, t), "e2m1")


K, T, S, H, N = 1024, 2048, 1024, 512, 512

def setup_inputs():
    n = np.random.standard_normal
    s = mx_kscale(K)[:, None]
    u = mx_kscale(H)[:, None]
    tab = pack_table4(n((K, T)) * s)
    offs = striped(np.random.permutation(T)[:S])
    wg = (n((K, H)) / np.sqrt(K) / s).astype(np.float32)
    wa = (n((K, H)) / np.sqrt(K) / s * u.T).astype(np.float32)
    wb_words, wb_scales = pack_weight(n((K, H)) / np.sqrt(K) / s * u.T, "e2m1")
    wo_words, wo_scales = pack_weight(n((H, N)) / np.sqrt(H) / u, "e4m3")
    bo = (0.5 * n(N)).astype(np.float32)
    return {"tab": tab, "offs": offs, "wg": wg, "wa": wa,
            "wb_words": wb_words, "wb_scales": wb_scales,
            "wo_words": wo_words, "wo_scales": wo_scales, "bo": bo}

def reference(tab, offs, wg, wa, wb_words, wb_scales, wo_words, wo_scales, bo):
    v = unpack_table4(tab)[:, unstriped(offs)]
    wb = unpack_weight(wb_words, wb_scales, "e2m1")
    wo = unpack_weight(wo_words, wo_scales, "e4m3")
    p = mxq(f64(wg), 0, "e4m3").T @ v
    a = mxq(f64(wa), 0, "e4m3").T @ v
    b = wb.T @ v
    g = 1.0 / (1.0 + np.exp(-p))
    h = b + g * (a - b)
    y = wo.T @ mxq(h, 0, "e4m3")
    return y + f64(bo)[:, None]

@@ -1,0 +1,247 @@
+from contextlib import ExitStack
+
+import concourse.mybir as mybir
+
+K, T, S, H, N = 1024, 2048, 1024, 512, 512
+FLOPS = 2 * K * H * S * 3 + 2 * H * N * S
+
+F32 = mybir.dt.float32
+BF16 = mybir.dt.bfloat16
+I32 = mybir.dt.int32
+U32 = mybir.dt.uint32
+U16 = mybir.dt.uint16
+U8 = mybir.dt.uint8
+FP8X4 = mybir.dt.float8_e4m3fn_x4
+FP4X4 = mybir.dt.float4_e2m1fn_x4
+ALU = mybir.AluOpType
+ACT = mybir.ActivationFunctionType
+
+P = 128
+PACK = 4
+PASSES = K // (P * PACK)
+TOK = 128
+TILES = S // TOK
+HALF = S // 2
+VECTOR_SHARE = (32, 64, 64, 48)
+CHUNKS = (256, 256, 256, 128, 128)
+
+
+def tile_list_session_memory_blend_kernel(
+    tc, tab, offs, wg, wa, wb_words, wb_scales, wo_words, wo_scales, bo, out
+):
+    nc = tc.nc
+    with ExitStack() as ctx:
+        keep = ctx.enter_context(tc.tile_pool(name="keep", bufs=1))
+        ring = ctx.enter_context(tc.tile_pool(name="ring", bufs=3))
+        psum = ctx.enter_context(tc.psum_pool(name="psum", bufs=1))
+
+        offsets = keep.tile([P, S // 16], U16, name="offsets")
+        tab_words = keep.tile([P, T], I32, name="tab_words", align_bytes=64)
+        tab_scales = keep.tile([P, T], U8, name="tab_scales", align_bytes=64)
+        wb_raw = keep.tile([P, PASSES * H // 2], I32, name="wb_raw", align_bytes=64)
+        wb_scales_raw = keep.tile([P, PASSES * H], U8, name="wb_scales_raw", align_bytes=64)
+        v_scales0 = keep.tile([P, S], U8, name="v_scales0", align_bytes=64)
+        v_scales1 = keep.tile([P, S], U8, name="v_scales1", align_bytes=64)
+        wo_codes = keep.tile([P, N], I32, name="wo_codes", align_bytes=64)
+        wo_sc = keep.tile([P, N], U8, name="wo_sc", align_bytes=64)
+        warm = keep.tile([P, 2], F32, name="warm")
+
+        nc.gpsimd.memset(tab_scales[:].bitcast(I32), 0)
+        nc.gpsimd.memset(warm[:], 0.0)
+        nc.gpsimd.memset(wb_scales_raw[:].bitcast(I32), 0)
+        nc.gpsimd.memset(v_scales1[:].bitcast(I32), 0)
+        nc.gpsimd.memset(wo_sc[:].bitcast(I32), 0)
+        nc.scalar.activation(warm[:, 1:2], warm[:, 0:1], ACT.Sigmoid)
+
+        nc.sync.dma_start(offsets[:], offs)
+        nc.sync.dma_start(
+            wb_raw[:].rearrange("p (a w) -> p a w", a=PASSES),
+            wb_words.bitcast(I32).rearrange("a p w -> p a w"),
+        )
+        scale_rows = tab[0, 512 * T :].bitcast(I32).rearrange("(a quad r w) -> r quad a w", a=PASSES, quad=4, r=4)
+        for r in range(4):
+            nc.sync.dma_start(tab_scales[r:P:16, :].bitcast(I32), scale_rows[r])
+        raw = []
+
+        def load_weight(w, a):
+            r = keep.tile([P, PACK, H], F32, name="raw%d" % len(raw), tag="raw%d" % len(raw))
+            nc.sync.dma_start(r[:], w[512 * a : 512 * (a + 1), :].rearrange("(p j) c -> p j c", j=PACK))
+            raw.append(r)
+
+        nc.sync.dma_start(tab_words[:], tab[0, : 512 * T].rearrange("(p b) -> p b", p=P).bitcast(I32))
+        wb_rows = wb_scales.bitcast(I32).rearrange("a q w -> q a w")
+        for quad in range(4):
+            nc.sync.dma_start(
+                wb_scales_raw[32 * quad : 32 * quad + 4, :].bitcast(I32).rearrange("q (a w) -> q a w", a=PASSES),
+                wb_rows[4 * quad : 4 * quad + 4],
+            )
+        load_weight(wg, 0)
+        load_weight(wg, 1)
+        load_weight(wa, 0)
+        load_weight(wa, 1)
+
+        nc.sync.dma_start(wo_codes[:], wo_words[0].rearrange("p c i -> p (c i)").bitcast(I32))
+        for quad in range(4):
+            nc.sync.dma_start(
+                wo_sc[32 * quad : 32 * quad + 4, :].bitcast(I32),
+                wo_scales[0, 4 * quad : 4 * quad + 4, :].bitcast(I32),
+            )
+
+        wb_codes = keep.tile([P, PASSES * H], U16, name="wb_codes", align_bytes=64)
+        wb_sc = keep.tile([P, PASSES * H], U8, name="wb_sc", align_bytes=64)
+        nc.vector.tensor_copy(
+            wb_codes[:].rearrange("p (a t m) -> p a t m", a=PASSES, t=PACK),
+            wb_raw[:].bitcast(U16).rearrange("p (a m t) -> p a t m", a=PASSES, t=PACK),
+        )
+
+        nc.vector.tensor_copy(v_scales0[:], tab_scales[:].indirect(offsets[:]))
+        nc.scalar.dma_start(v_scales1[: P - 16, :].bitcast(I32), v_scales0[16:, :].bitcast(I32))
+        v_scales = (v_scales0, v_scales1)
+        v_codes = []
+
+        def gather_words(half):
+            picked = keep.tile([P, HALF], U32, name="picked%d" % half, tag="picked", align_bytes=64)
+            cols = HALF // 16
+            nc.vector.tensor_copy(
+                picked[:], tab_words[:].bitcast(U32).indirect(offsets[:, half * cols : (half + 1) * cols])
+            )
+            parted = keep.tile([P, PASSES * HALF], U16, name="parted%d" % half, align_bytes=64)
+            nc.vector.tensor_copy(
+                parted[:].rearrange("p (a s) -> p a s", a=PASSES),
+                picked[:].bitcast(U16).rearrange("p (s a) -> p a s", a=PASSES),
+            )
+            v_codes.append(parted)
+
+        gather_words(0)
+        nc.vector.tensor_copy(
+            wb_sc[:].rearrange("p (a t m) -> p a t m", a=PASSES, t=PACK),
+            wb_scales_raw[:].rearrange("p (a m t) -> p a t m", a=PASSES, t=PACK),
+        )
+
+        w_codes, w_scales = [], []
+
+        def quantise_weight(n):
+            grouped = keep.tile([P, H * PACK], BF16, name="grouped%d" % n, align_bytes=64)
+            dst = grouped[:].rearrange("p (t m j) -> p m t j", t=PACK, j=PACK)
+            src = raw[n][:].rearrange("p j (m t) -> p m t j", t=PACK)
+            cut = VECTOR_SHARE[n]
+            nc.scalar.copy(dst[:, cut:], src[:, cut:])
+            nc.vector.tensor_copy(dst[:, :cut], src[:, :cut])
+            codes = keep.tile([P, H], U32, name="w_codes%d" % n, align_bytes=64)
+            scales = keep.tile([P, H], U8, name="w_scales%d" % n, align_bytes=64)
+            nc.vector.quantize_mx(out=codes[:].bitcast(FP8X4), scales=scales[:], in_=grouped[:])
+            w_codes.append(codes)
+            w_scales.append(scales)
+
+        def first_product(kind, i, bank):
+            acc = psum.tile([P, PACK, TOK], F32, name="acc_%s%d" % (kind, i), tag="bank%d" % bank)
+            half, first = divmod(i * TOK, HALF)
+            for t in range(PACK):
+                for a in range(PASSES):
+                    if kind == "b":
+                        cols = slice(a * H + t * P, a * H + (t + 1) * P)
+                        lhs, lhs_scale = wb_codes[:, cols].bitcast(FP4X4), wb_sc[:, cols]
+                    else:
+                        n = a if kind == "p" else PASSES + a
+                        cols = slice(t * P, (t + 1) * P)
+                        lhs, lhs_scale = w_codes[n][:, cols].bitcast(FP8X4), w_scales[n][:, cols]
+                    nc.tensor.matmul_mx(
+                        out=acc[:, t, :],
+                        lhsT=lhs,
+                        lhsT_scale=lhs_scale,
+                        rhs=v_codes[half][:, a * HALF + first : a * HALF + first + TOK].bitcast(FP4X4),
+                        rhs_scale=v_scales[a][:, i * TOK : (i + 1) * TOK],
+                        start=(a == 0),
+                        stop=(a == PASSES - 1),
+                    )
+            return acc[:].rearrange("p t s -> p s t")
+
+        def by_token(tile):
+            return tile[:].rearrange("p (s t) -> p s t", t=PACK)
+
+        gates, rests, b_acc = {}, {}, {}
+
+        def gate(i, bank):
+            acc = first_product("p", i, bank)
+            g = keep.tile([P, TOK * PACK], F32, name="gate%d" % i)
+            nc.scalar.activation(by_token(g), acc, ACT.Sigmoid)
+            gates[i] = g
+
+        def rest(i):
+            r = keep.tile([P, TOK * PACK], F32, name="rest%d" % i)
+            nc.vector.scalar_tensor_tensor(by_token(r), by_token(gates[i]), 1.0, b_acc[i], ALU.subtract, ALU.mult)
+            rests[i] = r
+
+        h_codes = keep.tile([P, S], U32, name="h_codes", align_bytes=64)
+        h_scales = keep.tile([P, S], U8, name="h_scales", align_bytes=64)
+        out_rows = out.rearrange("(c p) s -> p c s", p=P)
+
+        def second_product(first, width, bank):
+            cols = slice(first, first + width)
+            last = first + width == S
+            for pair in range(2):
+                staged = ring.tile([P, 2, width], F32, name="staged", tag="staged%d" % pair)
+                acc = psum.tile([P, 2, width], F32, name="acc_y", tag="bank%d" % (bank + pair))
+                for e in range(2):
+                    c = 2 * pair + e
+                    nc.tensor.matmul_mx(
+                        out=acc[:, e, :],
+                        lhsT=wo_codes[:, c * P : (c + 1) * P].bitcast(FP8X4),
+                        lhsT_scale=wo_sc[:, c * P : (c + 1) * P],
+                        rhs=h_codes[:, cols].bitcast(FP8X4),
+                        rhs_scale=h_scales[:, cols],
+                        start=True,
+                        stop=True,
+                    )
+                for e in range(2):
+                    c = 2 * pair + e
+                    if last and pair == 1:
+                        nc.vector.tensor_scalar_add(staged[:, e, :], acc[:, e, :], bias[:, c : c + 1])
+                    else:
+                        nc.scalar.activation(staged[:, e, :], acc[:, e, :], ACT.Identity, bias=bias[:, c : c + 1])
+                nc.sync.dma_start(out_rows[:, 2 * pair : 2 * pair + 2, cols], staged[:])
+
+        quantise_weight(0)
+        quantise_weight(1)
+        bias = keep.tile([P, N // P], F32, name="bias", tag="raw0")
+        with nc.allow_non_contiguous_dma(reason="one bias value for each partition and block of 128 outputs"):
+            nc.sync.dma_start(bias[:], bo.rearrange("(c p) -> p c", p=P))
+        gather_words(1)
+        for i in range(4):
+            b_acc[i] = first_product("b", i, i)
+        for i in range(4):
+            gate(i, 4 + i)
+            rest(i)
+        quantise_weight(2)
+        quantise_weight(3)
+
+        ends = {}
+        done = 0
+        for n, width in enumerate(CHUNKS):
+            ends[(done + width) // TOK - 1] = (done, width, (6, 4, 0)[n % 3])
+            done = done + width
+
+        blended = {}
+
+        def quantise_h(i):
+            cols = slice(i * TOK, (i + 1) * TOK)
+            nc.vector.quantize_mx(out=h_codes[:, cols].bitcast(FP8X4), scales=h_scales[:, cols], in_=blended[i][:])
+            if i in ends:
+                second_product(*ends[i])
+
+        for i in range(TILES):
+            ahead = i + 4
+            a_acc = first_product("a", i, 2 + i % 2)
+            if ahead < TILES:
+                b_acc[ahead] = first_product("b", ahead, ahead % 2)
+                gate(ahead, 4 + ahead % 2)
+            gated = ring.tile([P, TOK * PACK], F32, name="gated")
+            nc.vector.tensor_tensor(by_token(gated), a_acc, by_token(gates[i]), ALU.mult)
+            if i > 0:
+                quantise_h(i - 1)
+            if ahead < TILES:
+                rest(ahead)
+            h = ring.tile([P, TOK * PACK], BF16, name="h", align_bytes=64)
+            nc.vector.tensor_tensor(h[:], gated[:], rests[i][:], ALU.subtract)
+            blended[i] = h
+        quantise_h(TILES - 1)

@@ -22,8 +22,11 @@ PASSES = K // (P * PACK)
 TOK = 128
 TILES = S // TOK
 HALF = S // 2
-VECTOR_SHARE = (32, 64, 64, 48)
-CHUNKS = (256, 256, 256, 128, 128)
+VECTOR_SHARE = (32, 72, 64, 40)
+SUMMED_TILES = 2
+LAG = 1
+POOL_TILES = ()
+CHUNKS = (256, 256, 128, 128, 128, 128)
 
 
 def tile_list_session_memory_blend_kernel(
@@ -125,35 +128,41 @@ def tile_list_session_memory_blend_kernel(
             dst = grouped[:].rearrange("p (t m j) -> p m t j", t=PACK, j=PACK)
             src = raw[n][:].rearrange("p j (m t) -> p m t j", t=PACK)
             cut = VECTOR_SHARE[n]
-            nc.scalar.copy(dst[:, cut:], src[:, cut:])
-            nc.vector.tensor_copy(dst[:, :cut], src[:, :cut])
+            if n < PASSES:
+                nc.scalar.copy(dst[:, cut:], src[:, cut:])
+                nc.vector.tensor_copy(dst[:, :cut], src[:, :cut])
+            else:
+                nc.scalar.activation(dst[:, cut:], src[:, cut:], ACT.Copy, scale=-1.0)
+                nc.vector.tensor_scalar_mul(dst[:, :cut], src[:, :cut], -1.0)
             codes = keep.tile([P, H], U32, name="w_codes%d" % n, align_bytes=64)
             scales = keep.tile([P, H], U8, name="w_scales%d" % n, align_bytes=64)
             nc.vector.quantize_mx(out=codes[:].bitcast(FP8X4), scales=scales[:], in_=grouped[:])
             w_codes.append(codes)
             w_scales.append(scales)
 
-        def first_product(kind, i, bank):
-            acc = psum.tile([P, PACK, TOK], F32, name="acc_%s%d" % (kind, i), tag="bank%d" % bank)
+        def stationary(kind, a, t):
+            if kind == "b":
+                cols = slice(a * H + t * P, a * H + (t + 1) * P)
+                return wb_codes[:, cols].bitcast(FP4X4), wb_sc[:, cols]
+            n = a if kind == "p" else PASSES + a
+            cols = slice(t * P, (t + 1) * P)
+            return w_codes[n][:, cols].bitcast(FP8X4), w_scales[n][:, cols]
+
+        def first_product(kinds, i, bank):
+            acc = psum.tile([P, PACK, TOK], F32, name="acc_%s%d" % (kinds, i), tag="bank%d" % bank)
             half, first = divmod(i * TOK, HALF)
-            for t in range(PACK):
-                for a in range(PASSES):
-                    if kind == "b":
-                        cols = slice(a * H + t * P, a * H + (t + 1) * P)
-                        lhs, lhs_scale = wb_codes[:, cols].bitcast(FP4X4), wb_sc[:, cols]
-                    else:
-                        n = a if kind == "p" else PASSES + a
-                        cols = slice(t * P, (t + 1) * P)
-                        lhs, lhs_scale = w_codes[n][:, cols].bitcast(FP8X4), w_scales[n][:, cols]
-                    nc.tensor.matmul_mx(
-                        out=acc[:, t, :],
-                        lhsT=lhs,
-                        lhsT_scale=lhs_scale,
-                        rhs=v_codes[half][:, a * HALF + first : a * HALF + first + TOK].bitcast(FP4X4),
-                        rhs_scale=v_scales[a][:, i * TOK : (i + 1) * TOK],
-                        start=(a == 0),
-                        stop=(a == PASSES - 1),
-                    )
+            steps = [(kind, a, t) for kind in kinds for a in range(PASSES) for t in range(PACK)]
+            for n, (kind, a, t) in enumerate(steps):
+                lhs, lhs_scale = stationary(kind, a, t)
+                nc.tensor.matmul_mx(
+                    out=acc[:, t, :],
+                    lhsT=lhs,
+                    lhsT_scale=lhs_scale,
+                    rhs=v_codes[half][:, a * HALF + first : a * HALF + first + TOK].bitcast(FP4X4),
+                    rhs_scale=v_scales[a][:, i * TOK : (i + 1) * TOK],
+                    start=(n == 0),
+                    stop=(n == len(steps) - 1),
+                )
             return acc[:].rearrange("p t s -> p s t")
 
         def by_token(tile):
@@ -210,15 +219,15 @@ def tile_list_session_memory_blend_kernel(
         for i in range(4):
             b_acc[i] = first_product("b", i, i)
         for i in range(4):
+            if i % 2 == 0:
+                quantise_weight(PASSES + i // 2)
             gate(i, 4 + i)
             rest(i)
-        quantise_weight(2)
-        quantise_weight(3)
 
         ends = {}
         done = 0
         for n, width in enumerate(CHUNKS):
-            ends[(done + width) // TOK - 1] = (done, width, (6, 4, 0)[n % 3])
+            ends[(done + width) // TOK - 1] = (done, width, (6, 6, 4, 6, 4, 6)[n])
             done = done + width
 
         blended = {}
@@ -231,17 +240,30 @@ def tile_list_session_memory_blend_kernel(
 
         for i in range(TILES):
             ahead = i + 4
-            a_acc = first_product("a", i, 2 + i % 2)
-            if ahead < TILES:
+            summed = i >= TILES - SUMMED_TILES
+            acc = first_product("ba" if summed else "a", i, 2 + i % 2)
+            if summed:
+                b_acc[i] = first_product("b", i, i % 2)
+            if ahead < TILES - SUMMED_TILES:
                 b_acc[ahead] = first_product("b", ahead, ahead % 2)
+            if ahead < TILES:
                 gate(ahead, 4 + ahead % 2)
             gated = ring.tile([P, TOK * PACK], F32, name="gated")
-            nc.vector.tensor_tensor(by_token(gated), a_acc, by_token(gates[i]), ALU.mult)
-            if i > 0:
-                quantise_h(i - 1)
-            if ahead < TILES:
+            if summed:
+                nc.vector.tensor_tensor(by_token(gated), acc, by_token(gates[i]), ALU.mult)
+            else:
+                nc.vector.scalar_tensor_tensor(by_token(gated), acc, -1.0, by_token(gates[i]), ALU.mult, ALU.mult)
+            if i >= LAG:
+                quantise_h(i - LAG)
+            if ahead < TILES - SUMMED_TILES:
                 rest(ahead)
             h = ring.tile([P, TOK * PACK], BF16, name="h", align_bytes=64)
-            nc.vector.tensor_tensor(h[:], gated[:], rests[i][:], ALU.subtract)
+            if summed:
+                nc.vector.tensor_tensor(by_token(h), b_acc[i], by_token(gated), ALU.subtract)
+            elif i in POOL_TILES:
+                nc.gpsimd.tensor_tensor(h[:], gated[:], rests[i][:], ALU.subtract)
+            else:
+                nc.vector.tensor_tensor(h[:], gated[:], rests[i][:], ALU.subtract)
             blended[i] = h
-        quantise_h(TILES - 1)
+        for i in range(TILES - LAG, TILES):
+            quantise_h(i)

@@ -19,14 +19,18 @@ ACT = mybir.ActivationFunctionType
 P = 128
 PACK = 4
 PASSES = K // (P * PACK)
+QUADS = 4
 TOK = 128
 TILES = S // TOK
+WIDE = TOK * PACK
 HALF = S // 2
-VECTOR_SHARE = (32, 72, 64, 40)
+PASS1_ROWS = 16
+VECTOR_SHARE = (0, 80, 64, 64)
+EARLY_TILES = 4
+FIRST_GATES = 2
+POOL_TILES = 2
 SUMMED_TILES = 2
-LAG = 1
-POOL_TILES = ()
-CHUNKS = (256, 256, 128, 128, 128, 128)
+CHUNKS = ((256, 6), (256, 6), (128, 6), (128, 0), (128, 6), (128, 0))
 
 
 def tile_list_session_memory_blend_kernel(
@@ -42,98 +46,96 @@ def tile_list_session_memory_blend_kernel(
         tab_words = keep.tile([P, T], I32, name="tab_words", align_bytes=64)
         tab_scales = keep.tile([P, T], U8, name="tab_scales", align_bytes=64)
         wb_raw = keep.tile([P, PASSES * H // 2], I32, name="wb_raw", align_bytes=64)
-        wb_scales_raw = keep.tile([P, PASSES * H], U8, name="wb_scales_raw", align_bytes=64)
+        wb_scales_raw = keep.tile([P, PASSES * H], U8, name="wb_scales_raw", tag="picked1", align_bytes=64)
         v_scales0 = keep.tile([P, S], U8, name="v_scales0", align_bytes=64)
         v_scales1 = keep.tile([P, S], U8, name="v_scales1", align_bytes=64)
         wo_codes = keep.tile([P, N], I32, name="wo_codes", align_bytes=64)
-        wo_sc = keep.tile([P, N], U8, name="wo_sc", align_bytes=64)
+        wo_scale_tile = keep.tile([P, N], U8, name="wo_scale_tile", align_bytes=64)
         warm = keep.tile([P, 2], F32, name="warm")
 
         nc.gpsimd.memset(tab_scales[:].bitcast(I32), 0)
         nc.gpsimd.memset(warm[:], 0.0)
         nc.gpsimd.memset(wb_scales_raw[:].bitcast(I32), 0)
         nc.gpsimd.memset(v_scales1[:].bitcast(I32), 0)
-        nc.gpsimd.memset(wo_sc[:].bitcast(I32), 0)
+        nc.gpsimd.memset(wo_scale_tile[:].bitcast(I32), 0)
         nc.scalar.activation(warm[:, 1:2], warm[:, 0:1], ACT.Sigmoid)
+
+        raw = []
+
+        def load_weight(w, a):
+            rows = keep.tile([P, PACK, H], F32, name="raw%d" % len(raw), tag="raw%d" % len(raw), align_bytes=64)
+            nc.sync.dma_start(rows[:], w[512 * a : 512 * (a + 1), :].rearrange("(p j) c -> p j c", j=PACK))
+            raw.append(rows)
 
         nc.sync.dma_start(offsets[:], offs)
         nc.sync.dma_start(
             wb_raw[:].rearrange("p (a w) -> p a w", a=PASSES),
             wb_words.bitcast(I32).rearrange("a p w -> p a w"),
         )
-        scale_rows = tab[0, 512 * T :].bitcast(I32).rearrange("(a quad r w) -> r quad a w", a=PASSES, quad=4, r=4)
+        scale_rows = tab[0, 512 * T :].bitcast(I32).rearrange("(a quad r w) -> r quad a w", a=PASSES, quad=QUADS, r=4)
         for r in range(4):
-            nc.sync.dma_start(tab_scales[r:P:16, :].bitcast(I32), scale_rows[r])
-        raw = []
-
-        def load_weight(w, a):
-            r = keep.tile([P, PACK, H], F32, name="raw%d" % len(raw), tag="raw%d" % len(raw))
-            nc.sync.dma_start(r[:], w[512 * a : 512 * (a + 1), :].rearrange("(p j) c -> p j c", j=PACK))
-            raw.append(r)
-
+            nc.sync.dma_start(tab_scales[r:P:PASS1_ROWS, :].bitcast(I32), scale_rows[r])
         nc.sync.dma_start(tab_words[:], tab[0, : 512 * T].rearrange("(p b) -> p b", p=P).bitcast(I32))
         wb_rows = wb_scales.bitcast(I32).rearrange("a q w -> q a w")
-        for quad in range(4):
+        for quad in range(QUADS):
             nc.sync.dma_start(
                 wb_scales_raw[32 * quad : 32 * quad + 4, :].bitcast(I32).rearrange("q (a w) -> q a w", a=PASSES),
                 wb_rows[4 * quad : 4 * quad + 4],
             )
         load_weight(wg, 0)
         load_weight(wg, 1)
-        load_weight(wa, 0)
-        load_weight(wa, 1)
-
-        nc.sync.dma_start(wo_codes[:], wo_words[0].rearrange("p c i -> p (c i)").bitcast(I32))
-        for quad in range(4):
-            nc.sync.dma_start(
-                wo_sc[32 * quad : 32 * quad + 4, :].bitcast(I32),
-                wo_scales[0, 4 * quad : 4 * quad + 4, :].bitcast(I32),
-            )
 
         wb_codes = keep.tile([P, PASSES * H], U16, name="wb_codes", align_bytes=64)
-        wb_sc = keep.tile([P, PASSES * H], U8, name="wb_sc", align_bytes=64)
+        wb_scale_tile = keep.tile([P, PASSES * H], U8, name="wb_scale_tile", align_bytes=64)
         nc.vector.tensor_copy(
             wb_codes[:].rearrange("p (a t m) -> p a t m", a=PASSES, t=PACK),
             wb_raw[:].bitcast(U16).rearrange("p (a m t) -> p a t m", a=PASSES, t=PACK),
         )
 
         nc.vector.tensor_copy(v_scales0[:], tab_scales[:].indirect(offsets[:]))
-        nc.scalar.dma_start(v_scales1[: P - 16, :].bitcast(I32), v_scales0[16:, :].bitcast(I32))
+        nc.sync.dma_start(v_scales1[: P - PASS1_ROWS, :].bitcast(I32), v_scales0[PASS1_ROWS:, :].bitcast(I32))
         v_scales = (v_scales0, v_scales1)
+
+        load_weight(wa, 0)
+        load_weight(wa, 1)
+        nc.sync.dma_start(wo_codes[:], wo_words[0].rearrange("p c i -> p (c i)").bitcast(I32))
+        for quad in range(QUADS):
+            nc.sync.dma_start(
+                wo_scale_tile[32 * quad : 32 * quad + 4, :].bitcast(I32),
+                wo_scales[0, 4 * quad : 4 * quad + 4, :].bitcast(I32),
+            )
+
         v_codes = []
 
-        def gather_words(half):
-            picked = keep.tile([P, HALF], U32, name="picked%d" % half, tag="picked", align_bytes=64)
+        def gather_words(half, parted_tag):
+            picked = keep.tile([P, HALF], U32, name="picked%d" % half, tag="picked%d" % half, align_bytes=64)
             cols = HALF // 16
             nc.vector.tensor_copy(
                 picked[:], tab_words[:].bitcast(U32).indirect(offsets[:, half * cols : (half + 1) * cols])
             )
-            parted = keep.tile([P, PASSES * HALF], U16, name="parted%d" % half, align_bytes=64)
+            parted = keep.tile([P, PASSES * HALF], U16, name="parted%d" % half, tag=parted_tag, align_bytes=64)
             nc.vector.tensor_copy(
                 parted[:].rearrange("p (a s) -> p a s", a=PASSES),
                 picked[:].bitcast(U16).rearrange("p (s a) -> p a s", a=PASSES),
             )
             v_codes.append(parted)
 
-        gather_words(0)
+        gather_words(0, "parted0")
         nc.vector.tensor_copy(
-            wb_sc[:].rearrange("p (a t m) -> p a t m", a=PASSES, t=PACK),
+            wb_scale_tile[:].rearrange("p (a t m) -> p a t m", a=PASSES, t=PACK),
             wb_scales_raw[:].rearrange("p (a m t) -> p a t m", a=PASSES, t=PACK),
         )
 
         w_codes, w_scales = [], []
 
-        def quantise_weight(n):
+        def quantise_weight(n, sign):
             grouped = keep.tile([P, H * PACK], BF16, name="grouped%d" % n, align_bytes=64)
             dst = grouped[:].rearrange("p (t m j) -> p m t j", t=PACK, j=PACK)
             src = raw[n][:].rearrange("p j (m t) -> p m t j", t=PACK)
             cut = VECTOR_SHARE[n]
-            if n < PASSES:
-                nc.scalar.copy(dst[:, cut:], src[:, cut:])
-                nc.vector.tensor_copy(dst[:, :cut], src[:, :cut])
-            else:
-                nc.scalar.activation(dst[:, cut:], src[:, cut:], ACT.Copy, scale=-1.0)
-                nc.vector.tensor_scalar_mul(dst[:, :cut], src[:, :cut], -1.0)
+            nc.scalar.activation(dst[:, cut:], src[:, cut:], ACT.Copy, scale=sign)
+            if cut:
+                nc.vector.tensor_scalar_mul(dst[:, :cut], src[:, :cut], sign)
             codes = keep.tile([P, H], U32, name="w_codes%d" % n, align_bytes=64)
             scales = keep.tile([P, H], U8, name="w_scales%d" % n, align_bytes=64)
             nc.vector.quantize_mx(out=codes[:].bitcast(FP8X4), scales=scales[:], in_=grouped[:])
@@ -143,7 +145,7 @@ def tile_list_session_memory_blend_kernel(
         def stationary(kind, a, t):
             if kind == "b":
                 cols = slice(a * H + t * P, a * H + (t + 1) * P)
-                return wb_codes[:, cols].bitcast(FP4X4), wb_sc[:, cols]
+                return wb_codes[:, cols].bitcast(FP4X4), wb_scale_tile[:, cols]
             n = a if kind == "p" else PASSES + a
             cols = slice(t * P, (t + 1) * P)
             return w_codes[n][:, cols].bitcast(FP8X4), w_scales[n][:, cols]
@@ -165,29 +167,50 @@ def tile_list_session_memory_blend_kernel(
                 )
             return acc[:].rearrange("p t s -> p s t")
 
-        def by_token(tile):
-            return tile[:].rearrange("p (s t) -> p s t", t=PACK)
+        def by_token(ap):
+            return ap.rearrange("p (s t) -> p s t", t=PACK)
 
-        gates, rests, b_acc = {}, {}, {}
+        gates, rests, b_acc, b_minus_a = {}, {}, {}, {}
 
-        def gate(i, bank):
-            acc = first_product("p", i, bank)
-            g = keep.tile([P, TOK * PACK], F32, name="gate%d" % i)
-            nc.scalar.activation(by_token(g), acc, ACT.Sigmoid)
-            gates[i] = g
+        def gate(i, bank, into):
+            nc.scalar.activation(by_token(into), first_product("p", i, bank), ACT.Sigmoid)
+            gates[i] = into
 
         def rest(i):
-            r = keep.tile([P, TOK * PACK], F32, name="rest%d" % i)
-            nc.vector.scalar_tensor_tensor(by_token(r), by_token(gates[i]), 1.0, b_acc[i], ALU.subtract, ALU.mult)
+            r = keep.tile([P, WIDE], F32, name="rest%d" % i)
+            nc.vector.scalar_tensor_tensor(by_token(r[:]), by_token(gates[i]), 1.0, b_acc[i], ALU.subtract, ALU.mult)
             rests[i] = r
 
+        quantise_weight(0, 1.0)
+        quantise_weight(1, 1.0)
+        bias = keep.tile([P, N // P], F32, name="bias", tag="raw0", align_bytes=64)
+        with nc.allow_non_contiguous_dma(reason="one bias value for each partition and block of 128 outputs"):
+            nc.sync.dma_start(bias[:], bo.rearrange("(c p) -> p c", p=P))
+        gather_words(1, "raw1")
+        for i in range(EARLY_TILES):
+            b_acc[i] = first_product("b", i, i)
+
+        quantise_weight(2, -1.0)
+        first_gates = keep.tile([P, FIRST_GATES * WIDE], F32, name="first_gates", tag="raw2", align_bytes=64)
+        for i in range(FIRST_GATES):
+            gate(i, 4 + i, first_gates[:, i * WIDE : (i + 1) * WIDE])
+            rest(i)
+        quantise_weight(3, -1.0)
+        later_gates = keep.tile([P, (TILES - FIRST_GATES) * WIDE], F32, name="later_gates", tag="raw3", align_bytes=64)
+
+        def later_gate(i, bank):
+            gate(i, bank, later_gates[:, (i - FIRST_GATES) * WIDE : (i - FIRST_GATES + 1) * WIDE])
+
+        for i in range(FIRST_GATES, EARLY_TILES):
+            later_gate(i, 4 + i)
+
+        h_pair = keep.tile([P, 2 * WIDE], BF16, name="h_pair", align_bytes=64)
         h_codes = keep.tile([P, S], U32, name="h_codes", align_bytes=64)
         h_scales = keep.tile([P, S], U8, name="h_scales", align_bytes=64)
         out_rows = out.rearrange("(c p) s -> p c s", p=P)
 
         def second_product(first, width, bank):
             cols = slice(first, first + width)
-            last = first + width == S
             for pair in range(2):
                 staged = ring.tile([P, 2, width], F32, name="staged", tag="staged%d" % pair)
                 acc = psum.tile([P, 2, width], F32, name="acc_y", tag="bank%d" % (bank + pair))
@@ -196,7 +219,7 @@ def tile_list_session_memory_blend_kernel(
                     nc.tensor.matmul_mx(
                         out=acc[:, e, :],
                         lhsT=wo_codes[:, c * P : (c + 1) * P].bitcast(FP8X4),
-                        lhsT_scale=wo_sc[:, c * P : (c + 1) * P],
+                        lhsT_scale=wo_scale_tile[:, c * P : (c + 1) * P],
                         rhs=h_codes[:, cols].bitcast(FP8X4),
                         rhs_scale=h_scales[:, cols],
                         start=True,
@@ -204,66 +227,59 @@ def tile_list_session_memory_blend_kernel(
                     )
                 for e in range(2):
                     c = 2 * pair + e
-                    if last and pair == 1:
+                    if first + width == S and pair == 1:
                         nc.vector.tensor_scalar_add(staged[:, e, :], acc[:, e, :], bias[:, c : c + 1])
                     else:
                         nc.scalar.activation(staged[:, e, :], acc[:, e, :], ACT.Identity, bias=bias[:, c : c + 1])
                 nc.sync.dma_start(out_rows[:, 2 * pair : 2 * pair + 2, cols], staged[:])
 
-        quantise_weight(0)
-        quantise_weight(1)
-        bias = keep.tile([P, N // P], F32, name="bias", tag="raw0")
-        with nc.allow_non_contiguous_dma(reason="one bias value for each partition and block of 128 outputs"):
-            nc.sync.dma_start(bias[:], bo.rearrange("(c p) -> p c", p=P))
-        gather_words(1)
-        for i in range(4):
-            b_acc[i] = first_product("b", i, i)
-        for i in range(4):
-            if i % 2 == 0:
-                quantise_weight(PASSES + i // 2)
-            gate(i, 4 + i)
-            rest(i)
+        chunk_ending_at = {}
+        first = 0
+        for width, bank in CHUNKS:
+            chunk_ending_at[(first + width) // TOK - 1] = (first, width, bank)
+            first = first + width
 
-        ends = {}
-        done = 0
-        for n, width in enumerate(CHUNKS):
-            ends[(done + width) // TOK - 1] = (done, width, (6, 6, 4, 6, 4, 6)[n])
-            done = done + width
+        def quantise_h(lo, hi):
+            cols = slice(lo * TOK, (hi + 1) * TOK)
+            nc.vector.quantize_mx(
+                out=h_codes[:, cols].bitcast(FP8X4),
+                scales=h_scales[:, cols],
+                in_=h_pair[:, lo % 2 * WIDE : (hi % 2 + 1) * WIDE],
+            )
+            if hi in chunk_ending_at:
+                second_product(*chunk_ending_at[hi])
 
-        blended = {}
-
-        def quantise_h(i):
-            cols = slice(i * TOK, (i + 1) * TOK)
-            nc.vector.quantize_mx(out=h_codes[:, cols].bitcast(FP8X4), scales=h_scales[:, cols], in_=blended[i][:])
-            if i in ends:
-                second_product(*ends[i])
-
+        plain_tiles = TILES - SUMMED_TILES
         for i in range(TILES):
-            ahead = i + 4
-            summed = i >= TILES - SUMMED_TILES
-            acc = first_product("ba" if summed else "a", i, 2 + i % 2)
-            if summed:
-                b_acc[i] = first_product("b", i, i % 2)
-            if ahead < TILES - SUMMED_TILES:
-                b_acc[ahead] = first_product("b", ahead, ahead % 2)
-            if ahead < TILES:
-                gate(ahead, 4 + ahead % 2)
-            gated = ring.tile([P, TOK * PACK], F32, name="gated")
-            if summed:
-                nc.vector.tensor_tensor(by_token(gated), acc, by_token(gates[i]), ALU.mult)
+            gated = ring.tile([P, WIDE], F32, name="gated")
+            h = h_pair[:, i % 2 * WIDE : (i % 2 + 1) * WIDE]
+            if i < plain_tiles:
+                minus_a = first_product("a", i, i % 2)
+            if plain_tiles <= i + 1 < TILES:
+                bank = 2 + 2 * (i + 1 - plain_tiles)
+                b_minus_a[i + 1] = first_product("ba", i + 1, bank)
+                b_acc[i + 1] = first_product("b", i + 1, bank + 1)
+            if i < plain_tiles:
+                nc.vector.scalar_tensor_tensor(
+                    by_token(gated[:]), minus_a, -1.0, by_token(gates[i]), ALU.mult, ALU.mult
+                )
             else:
-                nc.vector.scalar_tensor_tensor(by_token(gated), acc, -1.0, by_token(gates[i]), ALU.mult, ALU.mult)
-            if i >= LAG:
-                quantise_h(i - LAG)
-            if ahead < TILES - SUMMED_TILES:
-                rest(ahead)
-            h = ring.tile([P, TOK * PACK], BF16, name="h", align_bytes=64)
-            if summed:
-                nc.vector.tensor_tensor(by_token(h), b_acc[i], by_token(gated), ALU.subtract)
-            elif i in POOL_TILES:
-                nc.gpsimd.tensor_tensor(h[:], gated[:], rests[i][:], ALU.subtract)
+                nc.vector.tensor_tensor(by_token(gated[:]), b_minus_a[i], by_token(gates[i]), ALU.mult)
+            if i + FIRST_GATES < plain_tiles:
+                rest(i + FIRST_GATES)
+            if i == 2:
+                quantise_h(0, 1)
+            elif i > 2:
+                quantise_h(i - 1, i - 1)
+            if i < POOL_TILES:
+                nc.gpsimd.tensor_tensor(h, gated[:], rests[i][:], ALU.subtract)
+            elif i < plain_tiles:
+                nc.vector.tensor_tensor(h, gated[:], rests[i][:], ALU.subtract)
             else:
-                nc.vector.tensor_tensor(h[:], gated[:], rests[i][:], ALU.subtract)
-            blended[i] = h
-        for i in range(TILES - LAG, TILES):
-            quantise_h(i)
+                nc.vector.tensor_tensor(by_token(h), b_acc[i], by_token(gated[:]), ALU.subtract)
+            ahead = i + EARLY_TILES - 1
+            if EARLY_TILES <= ahead < TILES:
+                if ahead < plain_tiles:
+                    b_acc[ahead] = first_product("b", ahead, 2 + ahead % 2)
+                later_gate(ahead, 4 + ahead % 2)
+        quantise_h(TILES - 1, TILES - 1)

@@ -28,7 +28,7 @@ PASS1_ROWS = 16
 VECTOR_SHARE = (0, 80, 64, 64)
 EARLY_TILES = 4
 FIRST_GATES = 2
-POOL_TILES = 2
+POOL_TILES = 0
 SUMMED_TILES = 2
 CHUNKS = ((256, 6), (256, 6), (128, 6), (128, 0), (128, 6), (128, 0))
 
@@ -51,14 +51,11 @@ def tile_list_session_memory_blend_kernel(
         v_scales1 = keep.tile([P, S], U8, name="v_scales1", align_bytes=64)
         wo_codes = keep.tile([P, N], I32, name="wo_codes", align_bytes=64)
         wo_scale_tile = keep.tile([P, N], U8, name="wo_scale_tile", align_bytes=64)
-        warm = keep.tile([P, 2], F32, name="warm")
 
         nc.gpsimd.memset(tab_scales[:].bitcast(I32), 0)
-        nc.gpsimd.memset(warm[:], 0.0)
         nc.gpsimd.memset(wb_scales_raw[:].bitcast(I32), 0)
         nc.gpsimd.memset(v_scales1[:].bitcast(I32), 0)
         nc.gpsimd.memset(wo_scale_tile[:].bitcast(I32), 0)
-        nc.scalar.activation(warm[:, 1:2], warm[:, 0:1], ACT.Sigmoid)
 
         raw = []
 
@@ -133,7 +130,12 @@ def tile_list_session_memory_blend_kernel(
             dst = grouped[:].rearrange("p (t m j) -> p m t j", t=PACK, j=PACK)
             src = raw[n][:].rearrange("p j (m t) -> p m t j", t=PACK)
             cut = VECTOR_SHARE[n]
-            nc.scalar.activation(dst[:, cut:], src[:, cut:], ACT.Copy, scale=sign)
+            nc.scalar.activation(
+                dst[:, cut:].rearrange("p m t j -> p m j t"),
+                src[:, cut:].rearrange("p m t j -> p m j t"),
+                ACT.Copy,
+                scale=sign,
+            )
             if cut:
                 nc.vector.tensor_scalar_mul(dst[:, :cut], src[:, :cut], sign)
             codes = keep.tile([P, H], U32, name="w_codes%d" % n, align_bytes=64)
@@ -173,7 +175,7 @@ def tile_list_session_memory_blend_kernel(
         gates, rests, b_acc, b_minus_a = {}, {}, {}, {}
 
         def gate(i, bank, into):
-            nc.scalar.activation(by_token(into), first_product("p", i, bank), ACT.Sigmoid)
+            nc.scalar.activation(by_token(into), first_product("p", i, bank), ACT.Tanh, scale=0.5)
             gates[i] = into
 
         def rest(i):
@@ -228,9 +230,13 @@ def tile_list_session_memory_blend_kernel(
                 for e in range(2):
                     c = 2 * pair + e
                     if first + width == S and pair == 1:
-                        nc.vector.tensor_scalar_add(staged[:, e, :], acc[:, e, :], bias[:, c : c + 1])
+                        nc.vector.tensor_scalar(
+                            staged[:, e, :], acc[:, e, :], -0.5, bias[:, c : c + 1], ALU.mult, ALU.add
+                        )
                     else:
-                        nc.scalar.activation(staged[:, e, :], acc[:, e, :], ACT.Identity, bias=bias[:, c : c + 1])
+                        nc.scalar.activation(
+                            staged[:, e, :], acc[:, e, :], ACT.Identity, bias=bias[:, c : c + 1], scale=-0.5
+                        )
                 nc.sync.dma_start(out_rows[:, 2 * pair : 2 * pair + 2, cols], staged[:])
 
         chunk_ending_at = {}
@@ -261,10 +267,12 @@ def tile_list_session_memory_blend_kernel(
                 b_acc[i + 1] = first_product("b", i + 1, bank + 1)
             if i < plain_tiles:
                 nc.vector.scalar_tensor_tensor(
-                    by_token(gated[:]), minus_a, -1.0, by_token(gates[i]), ALU.mult, ALU.mult
+                    by_token(gated[:]), by_token(gates[i]), 1.0, minus_a, ALU.add, ALU.mult
                 )
             else:
-                nc.vector.tensor_tensor(by_token(gated[:]), b_minus_a[i], by_token(gates[i]), ALU.mult)
+                nc.vector.scalar_tensor_tensor(
+                    by_token(gated[:]), by_token(gates[i]), 1.0, b_minus_a[i], ALU.add, ALU.mult
+                )
             if i + FIRST_GATES < plain_tiles:
                 rest(i + FIRST_GATES)
             if i == 2:
@@ -272,11 +280,11 @@ def tile_list_session_memory_blend_kernel(
             elif i > 2:
                 quantise_h(i - 1, i - 1)
             if i < POOL_TILES:
-                nc.gpsimd.tensor_tensor(h, gated[:], rests[i][:], ALU.subtract)
+                nc.gpsimd.tensor_tensor(h, gated[:], rests[i][:], ALU.add)
             elif i < plain_tiles:
-                nc.vector.tensor_tensor(h, gated[:], rests[i][:], ALU.subtract)
+                nc.vector.tensor_tensor(h, gated[:], rests[i][:], ALU.add)
             else:
-                nc.vector.tensor_tensor(by_token(h), b_acc[i], by_token(gated[:]), ALU.subtract)
+                nc.vector.scalar_tensor_tensor(by_token(h), b_acc[i], -2.0, by_token(gated[:]), ALU.mult, ALU.add)
             ahead = i + EARLY_TILES - 1
             if EARLY_TILES <= ahead < TILES:
                 if ahead < plain_tiles:

@@ -20,17 +20,12 @@ P = 128
 PACK = 4
 PASSES = K // (P * PACK)
 QUADS = 4
-TOK = 128
-TILES = S // TOK
-WIDE = TOK * PACK
-HALF = S // 2
+BLOCK = 256
+BANK = 512
+BLOCKS = 3
+TAIL = 128
 PASS1_ROWS = 16
-VECTOR_SHARE = (0, 80, 64, 64)
-EARLY_TILES = 4
-FIRST_GATES = 2
-POOL_TILES = 0
-SUMMED_TILES = 2
-CHUNKS = ((256, 6), (256, 6), (128, 6), (128, 0), (128, 6), (128, 0))
+VECTOR_SHARE = (20, 58, 80, 58)
 
 
 def tile_list_session_memory_blend_kernel(
@@ -46,7 +41,7 @@ def tile_list_session_memory_blend_kernel(
         tab_words = keep.tile([P, T], I32, name="tab_words", align_bytes=64)
         tab_scales = keep.tile([P, T], U8, name="tab_scales", align_bytes=64)
         wb_raw = keep.tile([P, PASSES * H // 2], I32, name="wb_raw", align_bytes=64)
-        wb_scales_raw = keep.tile([P, PASSES * H], U8, name="wb_scales_raw", tag="picked1", align_bytes=64)
+        wb_scales_raw = keep.tile([P, PASSES * H], U8, name="wb_scales_raw", tag="picked23", align_bytes=64)
         v_scales0 = keep.tile([P, S], U8, name="v_scales0", align_bytes=64)
         v_scales1 = keep.tile([P, S], U8, name="v_scales1", align_bytes=64)
         wo_codes = keep.tile([P, N], I32, name="wo_codes", align_bytes=64)
@@ -80,19 +75,13 @@ def tile_list_session_memory_blend_kernel(
                 wb_rows[4 * quad : 4 * quad + 4],
             )
         load_weight(wg, 0)
-        load_weight(wg, 1)
-
-        wb_codes = keep.tile([P, PASSES * H], U16, name="wb_codes", align_bytes=64)
-        wb_scale_tile = keep.tile([P, PASSES * H], U8, name="wb_scale_tile", align_bytes=64)
-        nc.vector.tensor_copy(
-            wb_codes[:].rearrange("p (a t m) -> p a t m", a=PASSES, t=PACK),
-            wb_raw[:].bitcast(U16).rearrange("p (a m t) -> p a t m", a=PASSES, t=PACK),
-        )
 
         nc.vector.tensor_copy(v_scales0[:], tab_scales[:].indirect(offsets[:]))
-        nc.sync.dma_start(v_scales1[: P - PASS1_ROWS, :].bitcast(I32), v_scales0[PASS1_ROWS:, :].bitcast(I32))
+        for r in range(4):
+            nc.sync.dma_start(v_scales1[r:P:32, :].bitcast(I32), v_scales0[PASS1_ROWS + r : P : 32, :].bitcast(I32))
         v_scales = (v_scales0, v_scales1)
 
+        load_weight(wg, 1)
         load_weight(wa, 0)
         load_weight(wa, 1)
         nc.sync.dma_start(wo_codes[:], wo_words[0].rearrange("p c i -> p (c i)").bitcast(I32))
@@ -101,43 +90,48 @@ def tile_list_session_memory_blend_kernel(
                 wo_scale_tile[32 * quad : 32 * quad + 4, :].bitcast(I32),
                 wo_scales[0, 4 * quad : 4 * quad + 4, :].bitcast(I32),
             )
+        bias = keep.tile([P, N // P], F32, name="bias", align_bytes=64)
 
         v_codes = []
 
-        def gather_words(half, parted_tag):
-            picked = keep.tile([P, HALF], U32, name="picked%d" % half, tag="picked%d" % half, align_bytes=64)
-            cols = HALF // 16
-            nc.vector.tensor_copy(
-                picked[:], tab_words[:].bitcast(U32).indirect(offsets[:, half * cols : (half + 1) * cols])
-            )
-            parted = keep.tile([P, PASSES * HALF], U16, name="parted%d" % half, tag=parted_tag, align_bytes=64)
+        def gather_words(picked):
+            q = len(v_codes)
+            cols = BLOCK // 16
+            nc.vector.tensor_copy(picked, tab_words[:].bitcast(U32).indirect(offsets[:, q * cols : (q + 1) * cols]))
+            parted = keep.tile([P, PASSES * BLOCK], U16, name="parted%d" % q, align_bytes=64)
             nc.vector.tensor_copy(
                 parted[:].rearrange("p (a s) -> p a s", a=PASSES),
-                picked[:].bitcast(U16).rearrange("p (s a) -> p a s", a=PASSES),
+                picked.bitcast(U16).rearrange("p (s a) -> p a s", a=PASSES),
             )
             v_codes.append(parted)
 
-        gather_words(0, "parted0")
+        picked0 = keep.tile([P, BLOCK], U32, name="picked0", align_bytes=64)
+        gather_words(picked0[:])
+        wb_codes = keep.tile([P, PASSES * H], U16, name="wb_codes", align_bytes=64)
+        wb_scale_tile = keep.tile([P, PASSES * H], U8, name="wb_scale_tile", align_bytes=64)
+        nc.vector.tensor_copy(
+            wb_codes[:].rearrange("p (a t m) -> p a t m", a=PASSES, t=PACK),
+            wb_raw[:].bitcast(U16).rearrange("p (a m t) -> p a t m", a=PASSES, t=PACK),
+        )
         nc.vector.tensor_copy(
             wb_scale_tile[:].rearrange("p (a t m) -> p a t m", a=PASSES, t=PACK),
             wb_scales_raw[:].rearrange("p (a m t) -> p a t m", a=PASSES, t=PACK),
         )
+        picked1 = keep.tile([P, BLOCK], U32, name="picked1", align_bytes=64)
+        gather_words(picked1[:])
+        picked23 = keep.tile([P, 2 * BLOCK], U32, name="picked23", tag="picked23", align_bytes=64)
+        gather_words(picked23[:, :BLOCK])
+        gather_words(picked23[:, BLOCK:])
 
         w_codes, w_scales = [], []
 
         def quantise_weight(n, sign):
-            grouped = keep.tile([P, H * PACK], BF16, name="grouped%d" % n, align_bytes=64)
-            dst = grouped[:].rearrange("p (t m j) -> p m t j", t=PACK, j=PACK)
-            src = raw[n][:].rearrange("p j (m t) -> p m t j", t=PACK)
+            grouped = keep.tile([P, H * PACK], BF16, name="grouped%d" % n, tag="grouped%d" % n, align_bytes=64)
+            dst = grouped[:].rearrange("p (t m j) -> p m j t", t=PACK, j=PACK)
+            src = raw[n][:].rearrange("p j (m t) -> p m j t", t=PACK)
             cut = VECTOR_SHARE[n]
-            nc.scalar.activation(
-                dst[:, cut:].rearrange("p m t j -> p m j t"),
-                src[:, cut:].rearrange("p m t j -> p m j t"),
-                ACT.Copy,
-                scale=sign,
-            )
-            if cut:
-                nc.vector.tensor_scalar_mul(dst[:, :cut], src[:, :cut], sign)
+            nc.scalar.activation(dst[:, cut:], src[:, cut:], ACT.Copy, scale=sign)
+            nc.vector.tensor_scalar_mul(dst[:, :cut], src[:, :cut], sign)
             codes = keep.tile([P, H], U32, name="w_codes%d" % n, align_bytes=64)
             scales = keep.tile([P, H], U8, name="w_scales%d" % n, align_bytes=64)
             nc.vector.quantize_mx(out=codes[:].bitcast(FP8X4), scales=scales[:], in_=grouped[:])
@@ -152,70 +146,78 @@ def tile_list_session_memory_blend_kernel(
             cols = slice(t * P, (t + 1) * P)
             return w_codes[n][:, cols].bitcast(FP8X4), w_scales[n][:, cols]
 
+        def span(i):
+            if i < 2 * BLOCKS:
+                return (i // 2) * BLOCK, BLOCK, (2 * (i % 2), 2 * (i % 2) + 1)
+            return BLOCKS * BLOCK + (i - 2 * BLOCKS) * TAIL, TAIL, (0, 1, 2, 3)
+
         def first_product(kinds, i, bank):
-            acc = psum.tile([P, PACK, TOK], F32, name="acc_%s%d" % (kinds, i), tag="bank%d" % bank)
-            half, first = divmod(i * TOK, HALF)
-            steps = [(kind, a, t) for kind in kinds for a in range(PASSES) for t in range(PACK)]
-            for n, (kind, a, t) in enumerate(steps):
-                lhs, lhs_scale = stationary(kind, a, t)
+            first, width, slots = span(i)
+            acc = psum.tile([P, len(slots), width], F32, name="acc_%s%d" % (kinds, i), tag="bank%d" % bank)
+            q, lo = divmod(first, BLOCK)
+            steps = [(kind, a, e) for kind in kinds for a in range(PASSES) for e in range(len(slots))]
+            for n, (kind, a, e) in enumerate(steps):
+                lhs, lhs_scale = stationary(kind, a, slots[e])
                 nc.tensor.matmul_mx(
-                    out=acc[:, t, :],
+                    out=acc[:, e, :],
                     lhsT=lhs,
                     lhsT_scale=lhs_scale,
-                    rhs=v_codes[half][:, a * HALF + first : a * HALF + first + TOK].bitcast(FP4X4),
-                    rhs_scale=v_scales[a][:, i * TOK : (i + 1) * TOK],
+                    rhs=v_codes[q][:, a * BLOCK + lo : a * BLOCK + lo + width].bitcast(FP4X4),
+                    rhs_scale=v_scales[a][:, first : first + width],
                     start=(n == 0),
                     stop=(n == len(steps) - 1),
                 )
-            return acc[:].rearrange("p t s -> p s t")
+            return acc[:].rearrange("p e s -> p s e")
 
-        def by_token(ap):
-            return ap.rearrange("p (s t) -> p s t", t=PACK)
+        def by_token(ap, i):
+            return ap.rearrange("p (s e) -> p s e", e=len(span(i)[2]))
 
-        gates, rests, b_acc, b_minus_a = {}, {}, {}, {}
-
-        def gate(i, bank, into):
-            nc.scalar.activation(by_token(into), first_product("p", i, bank), ACT.Tanh, scale=0.5)
-            gates[i] = into
-
-        def rest(i):
-            r = keep.tile([P, WIDE], F32, name="rest%d" % i)
-            nc.vector.scalar_tensor_tensor(by_token(r[:]), by_token(gates[i]), 1.0, b_acc[i], ALU.subtract, ALU.mult)
-            rests[i] = r
-
-        quantise_weight(0, 1.0)
-        quantise_weight(1, 1.0)
-        bias = keep.tile([P, N // P], F32, name="bias", tag="raw0", align_bytes=64)
-        with nc.allow_non_contiguous_dma(reason="one bias value for each partition and block of 128 outputs"):
-            nc.sync.dma_start(bias[:], bo.rearrange("(c p) -> p c", p=P))
-        gather_words(1, "raw1")
-        for i in range(EARLY_TILES):
-            b_acc[i] = first_product("b", i, i)
-
-        quantise_weight(2, -1.0)
-        first_gates = keep.tile([P, FIRST_GATES * WIDE], F32, name="first_gates", tag="raw2", align_bytes=64)
-        for i in range(FIRST_GATES):
-            gate(i, 4 + i, first_gates[:, i * WIDE : (i + 1) * WIDE])
-            rest(i)
-        quantise_weight(3, -1.0)
-        later_gates = keep.tile([P, (TILES - FIRST_GATES) * WIDE], F32, name="later_gates", tag="raw3", align_bytes=64)
-
-        def later_gate(i, bank):
-            gate(i, bank, later_gates[:, (i - FIRST_GATES) * WIDE : (i - FIRST_GATES + 1) * WIDE])
-
-        for i in range(FIRST_GATES, EARLY_TILES):
-            later_gate(i, 4 + i)
-
-        h_pair = keep.tile([P, 2 * WIDE], BF16, name="h_pair", align_bytes=64)
+        gates = {}
+        rests = keep.tile([P, 2 * BLOCKS * BANK], F32, name="rests")
+        gated = keep.tile([P, 8 * BANK], F32, name="gated")
+        h_rounded = keep.tile([P, S * PACK], BF16, name="h_rounded", align_bytes=64)
         h_codes = keep.tile([P, S], U32, name="h_codes", align_bytes=64)
         h_scales = keep.tile([P, S], U8, name="h_scales", align_bytes=64)
         out_rows = out.rearrange("(c p) s -> p c s", p=P)
+        acc_p, acc_b, acc_a = {}, {}, {}
 
-        def second_product(first, width, bank):
+        def piece(tile, i):
+            return by_token(tile[:, i * BANK : (i + 1) * BANK], i)
+
+        def gate(i):
+            nc.scalar.activation(gates[i], acc_p[i], ACT.Tanh, scale=0.5)
+
+        def rest(i):
+            nc.vector.scalar_tensor_tensor(piece(rests, i), gates[i], 1.0, acc_b[i], ALU.subtract, ALU.mult)
+
+        def gate_a(i):
+            nc.vector.scalar_tensor_tensor(piece(gated, i), gates[i], 1.0, acc_a[i], ALU.add, ALU.mult)
+
+        def blend_block(k):
+            cols = slice(2 * k * BANK, 2 * (k + 1) * BANK)
+            nc.vector.tensor_tensor(
+                h_rounded[:, cols].rearrange("p (s u e) -> p s u e", u=2, e=2),
+                gated[:, cols].rearrange("p (u s e) -> p s u e", u=2, e=2),
+                rests[:, cols].rearrange("p (u s e) -> p s u e", u=2, e=2),
+                ALU.add,
+            )
+
+        def blend_tail(i):
+            nc.vector.scalar_tensor_tensor(piece(h_rounded, i), acc_b[i], -2.0, piece(gated, i), ALU.mult, ALU.add)
+
+        def quantise_h(first, width):
+            cols = slice(first, first + width)
+            nc.vector.quantize_mx(
+                out=h_codes[:, cols].bitcast(FP8X4),
+                scales=h_scales[:, cols],
+                in_=h_rounded[:, first * PACK : (first + width) * PACK],
+            )
+
+        def second_product(first, width, banks):
             cols = slice(first, first + width)
             for pair in range(2):
                 staged = ring.tile([P, 2, width], F32, name="staged", tag="staged%d" % pair)
-                acc = psum.tile([P, 2, width], F32, name="acc_y", tag="bank%d" % (bank + pair))
+                acc = psum.tile([P, 2, width], F32, name="acc_y", tag="bank%d" % banks[pair])
                 for e in range(2):
                     c = 2 * pair + e
                     nc.tensor.matmul_mx(
@@ -239,55 +241,70 @@ def tile_list_session_memory_blend_kernel(
                         )
                 nc.sync.dma_start(out_rows[:, 2 * pair : 2 * pair + 2, cols], staged[:])
 
-        chunk_ending_at = {}
-        first = 0
-        for width, bank in CHUNKS:
-            chunk_ending_at[(first + width) // TOK - 1] = (first, width, bank)
-            first = first + width
+        for i in range(4):
+            acc_b[i] = first_product("b", i, i)
+        quantise_weight(0, 1.0)
+        quantise_weight(1, 1.0)
+        with nc.allow_non_contiguous_dma(reason="one bias value for each partition and block of 128 outputs"):
+            nc.sync.dma_start(bias[:], bo.rearrange("(c p) -> p c", p=P))
+        for i in range(4):
+            acc_p[i] = first_product("p", i, 4 + i)
 
-        def quantise_h(lo, hi):
-            cols = slice(lo * TOK, (hi + 1) * TOK)
-            nc.vector.quantize_mx(
-                out=h_codes[:, cols].bitcast(FP8X4),
-                scales=h_scales[:, cols],
-                in_=h_pair[:, lo % 2 * WIDE : (hi % 2 + 1) * WIDE],
-            )
-            if hi in chunk_ending_at:
-                second_product(*chunk_ending_at[hi])
-
-        plain_tiles = TILES - SUMMED_TILES
-        for i in range(TILES):
-            gated = ring.tile([P, WIDE], F32, name="gated")
-            h = h_pair[:, i % 2 * WIDE : (i % 2 + 1) * WIDE]
-            if i < plain_tiles:
-                minus_a = first_product("a", i, i % 2)
-            if plain_tiles <= i + 1 < TILES:
-                bank = 2 + 2 * (i + 1 - plain_tiles)
-                b_minus_a[i + 1] = first_product("ba", i + 1, bank)
-                b_acc[i + 1] = first_product("b", i + 1, bank + 1)
-            if i < plain_tiles:
-                nc.vector.scalar_tensor_tensor(
-                    by_token(gated[:]), by_token(gates[i]), 1.0, minus_a, ALU.add, ALU.mult
-                )
-            else:
-                nc.vector.scalar_tensor_tensor(
-                    by_token(gated[:]), by_token(gates[i]), 1.0, b_minus_a[i], ALU.add, ALU.mult
-                )
-            if i + FIRST_GATES < plain_tiles:
-                rest(i + FIRST_GATES)
-            if i == 2:
-                quantise_h(0, 1)
-            elif i > 2:
-                quantise_h(i - 1, i - 1)
-            if i < POOL_TILES:
-                nc.gpsimd.tensor_tensor(h, gated[:], rests[i][:], ALU.add)
-            elif i < plain_tiles:
-                nc.vector.tensor_tensor(h, gated[:], rests[i][:], ALU.add)
-            else:
-                nc.vector.scalar_tensor_tensor(by_token(h), b_acc[i], -2.0, by_token(gated[:]), ALU.mult, ALU.add)
-            ahead = i + EARLY_TILES - 1
-            if EARLY_TILES <= ahead < TILES:
-                if ahead < plain_tiles:
-                    b_acc[ahead] = first_product("b", ahead, 2 + ahead % 2)
-                later_gate(ahead, 4 + ahead % 2)
-        quantise_h(TILES - 1, TILES - 1)
+        quantise_weight(2, -1.0)
+        first_gates = keep.tile([P, 2 * BANK], F32, name="first_gates", tag="raw2", align_bytes=64)
+        for i in range(2):
+            gates[i] = piece(first_gates, i)
+            gate(i)
+            rest(i)
+        for i in range(4, 6):
+            acc_p[i] = first_product("p", i, i)
+            acc_b[i] = first_product("b", i, i - 4)
+        quantise_weight(3, -1.0)
+        later_gates = keep.tile([P, 6 * BANK], F32, name="later_gates", tag="raw3", align_bytes=64)
+        for i in range(2, 8):
+            gates[i] = by_token(later_gates[:, (i - 2) * BANK : (i - 1) * BANK], i)
+        gate(2)
+        gate(3)
+        acc_a[0] = first_product("a", 0, 6)
+        acc_a[1] = first_product("a", 1, 7)
+        rest(2)
+        rest(3)
+        gate(4)
+        gate(5)
+        gate_a(0)
+        gate_a(1)
+        acc_a[2] = first_product("a", 2, 4)
+        acc_a[3] = first_product("a", 3, 2)
+        acc_p[6] = first_product("p", 6, 5)
+        acc_p[7] = first_product("p", 7, 3)
+        rest(4)
+        blend_block(0)
+        gate(6)
+        gate(7)
+        acc_a[4] = first_product("a", 4, 6)
+        acc_a[5] = first_product("a", 5, 7)
+        gate_a(2)
+        quantise_h(0, BLOCK)
+        second_product(0, BLOCK, (5, 3))
+        gate_a(3)
+        rest(5)
+        blend_block(1)
+        acc_a[6] = first_product("ba", 6, 0)
+        acc_b[6] = first_product("b", 6, 4)
+        gate_a(4)
+        quantise_h(BLOCK, BLOCK)
+        gate_a(5)
+        acc_a[7] = first_product("ba", 7, 2)
+        acc_b[7] = first_product("b", 7, 1)
+        second_product(BLOCK, BLOCK, (5, 3))
+        gate_a(6)
+        blend_block(2)
+        blend_tail(6)
+        quantise_h(2 * BLOCK, BLOCK)
+        second_product(2 * BLOCK, BLOCK, (6, 7))
+        gate_a(7)
+        quantise_h(3 * BLOCK, TAIL)
+        second_product(3 * BLOCK, TAIL, (0, 4))
+        blend_tail(7)
+        quantise_h(3 * BLOCK + TAIL, TAIL)
+        second_product(3 * BLOCK + TAIL, TAIL, (5, 3))

@@ -34,7 +34,7 @@ def tile_list_session_memory_blend_kernel(
     nc = tc.nc
     with ExitStack() as ctx:
         keep = ctx.enter_context(tc.tile_pool(name="keep", bufs=1))
-        ring = ctx.enter_context(tc.tile_pool(name="ring", bufs=3))
+        ring = ctx.enter_context(tc.tile_pool(name="ring", bufs=5))
         psum = ctx.enter_context(tc.psum_pool(name="psum", bufs=1))
 
         offsets = keep.tile([P, S // 16], U16, name="offsets")
@@ -130,8 +130,14 @@ def tile_list_session_memory_blend_kernel(
             dst = grouped[:].rearrange("p (t m j) -> p m j t", t=PACK, j=PACK)
             src = raw[n][:].rearrange("p j (m t) -> p m j t", t=PACK)
             cut = VECTOR_SHARE[n]
-            nc.scalar.activation(dst[:, cut:], src[:, cut:], ACT.Copy, scale=sign)
-            nc.vector.tensor_scalar_mul(dst[:, :cut], src[:, :cut], sign)
+            if sign < 0:
+                nc.scalar.activation(dst[:, cut:], src[:, cut:], ACT.Copy, scale=sign)
+                nc.vector.tensor_scalar_mul(dst[:, :cut], src[:, :cut], sign)
+            else:
+                dst = grouped[:].rearrange("p (t m y z) -> p m y t z", t=PACK, y=2, z=2)
+                src = raw[n][:].rearrange("p (y z) (m t) -> p m y t z", y=2, t=PACK)
+                nc.scalar.copy(dst[:, cut:], src[:, cut:])
+                nc.vector.tensor_copy(dst[:, :cut], src[:, :cut])
             codes = keep.tile([P, H], U32, name="w_codes%d" % n, align_bytes=64)
             scales = keep.tile([P, H], U8, name="w_scales%d" % n, align_bytes=64)
             nc.vector.quantize_mx(out=codes[:].bitcast(FP8X4), scales=scales[:], in_=grouped[:])
@@ -173,7 +179,7 @@ def tile_list_session_memory_blend_kernel(
             return ap.rearrange("p (s e) -> p s e", e=len(span(i)[2]))
 
         gates = {}
-        rests = keep.tile([P, 2 * BLOCKS * BANK], F32, name="rests")
+        rests = keep.tile([P, 6 * BANK], F32, name="rests")
         gated = keep.tile([P, 8 * BANK], F32, name="gated")
         h_rounded = keep.tile([P, S * PACK], BF16, name="h_rounded", align_bytes=64)
         h_codes = keep.tile([P, S], U32, name="h_codes", align_bytes=64)
@@ -193,12 +199,12 @@ def tile_list_session_memory_blend_kernel(
         def gate_a(i):
             nc.vector.scalar_tensor_tensor(piece(gated, i), gates[i], 1.0, acc_a[i], ALU.add, ALU.mult)
 
-        def blend_block(k):
+        def blend_block(k, engine, lo=0, hi=BLOCK):
             cols = slice(2 * k * BANK, 2 * (k + 1) * BANK)
-            nc.vector.tensor_tensor(
-                h_rounded[:, cols].rearrange("p (s u e) -> p s u e", u=2, e=2),
-                gated[:, cols].rearrange("p (u s e) -> p s u e", u=2, e=2),
-                rests[:, cols].rearrange("p (u s e) -> p s u e", u=2, e=2),
+            engine.tensor_tensor(
+                h_rounded[:, cols].rearrange("p (s u e) -> p s u e", u=2, e=2)[:, lo:hi],
+                gated[:, cols].rearrange("p (u s e) -> p s u e", u=2, e=2)[:, lo:hi],
+                rests[:, cols].rearrange("p (u s e) -> p s u e", u=2, e=2)[:, lo:hi],
                 ALU.add,
             )
 
@@ -213,7 +219,7 @@ def tile_list_session_memory_blend_kernel(
                 in_=h_rounded[:, first * PACK : (first + width) * PACK],
             )
 
-        def second_product(first, width, banks):
+        def second_product(first, width, banks, shared=False):
             cols = slice(first, first + width)
             for pair in range(2):
                 staged = ring.tile([P, 2, width], F32, name="staged", tag="staged%d" % pair)
@@ -229,13 +235,12 @@ def tile_list_session_memory_blend_kernel(
                         start=True,
                         stop=True,
                     )
-                for e in range(2):
-                    c = 2 * pair + e
-                    if first + width == S and pair == 1:
-                        nc.vector.tensor_scalar(
-                            staged[:, e, :], acc[:, e, :], -0.5, bias[:, c : c + 1], ALU.mult, ALU.add
-                        )
-                    else:
+                if shared and pair == 1:
+                    spread = bias[:, 2:].unsqueeze(2).to_broadcast([P, 2, width])
+                    nc.vector.scalar_tensor_tensor(staged[:], acc[:], -0.5, spread, ALU.mult, ALU.add)
+                else:
+                    for e in range(2):
+                        c = 2 * pair + e
                         nc.scalar.activation(
                             staged[:, e, :], acc[:, e, :], ACT.Identity, bias=bias[:, c : c + 1], scale=-0.5
                         )
@@ -268,43 +273,43 @@ def tile_list_session_memory_blend_kernel(
         acc_a[0] = first_product("a", 0, 6)
         acc_a[1] = first_product("a", 1, 7)
         rest(2)
-        rest(3)
         gate(4)
         gate(5)
         gate_a(0)
         gate_a(1)
+        blend_block(0, nc.gpsimd)
         acc_a[2] = first_product("a", 2, 4)
         acc_a[3] = first_product("a", 3, 2)
         acc_p[6] = first_product("p", 6, 5)
-        acc_p[7] = first_product("p", 7, 3)
-        rest(4)
-        blend_block(0)
+        rest(3)
         gate(6)
-        gate(7)
         acc_a[4] = first_product("a", 4, 6)
         acc_a[5] = first_product("a", 5, 7)
+        acc_a[6] = first_product("ba", 6, 3)
         gate_a(2)
-        quantise_h(0, BLOCK)
-        second_product(0, BLOCK, (5, 3))
         gate_a(3)
+        acc_p[7] = first_product("p", 7, 5)
+        gate(7)
+        rest(4)
         rest(5)
-        blend_block(1)
-        acc_a[6] = first_product("ba", 6, 0)
-        acc_b[6] = first_product("b", 6, 4)
         gate_a(4)
-        quantise_h(BLOCK, BLOCK)
+        quantise_h(0, BLOCK)
+        second_product(0, BLOCK, (2, 4))
+        acc_b[6] = first_product("b", 6, 0)
+        blend_block(1, nc.vector)
         gate_a(5)
-        acc_a[7] = first_product("ba", 7, 2)
-        acc_b[7] = first_product("b", 7, 1)
-        second_product(BLOCK, BLOCK, (5, 3))
+        quantise_h(BLOCK, BLOCK)
+        second_product(BLOCK, BLOCK, (5, 6))
+        acc_a[7] = first_product("ba", 7, 1)
+        acc_b[7] = first_product("b", 7, 7)
+        blend_block(2, nc.vector)
         gate_a(6)
-        blend_block(2)
-        blend_tail(6)
         quantise_h(2 * BLOCK, BLOCK)
-        second_product(2 * BLOCK, BLOCK, (6, 7))
+        second_product(2 * BLOCK, BLOCK, (2, 4))
+        blend_tail(6)
         gate_a(7)
         quantise_h(3 * BLOCK, TAIL)
-        second_product(3 * BLOCK, TAIL, (0, 4))
+        second_product(3 * BLOCK, TAIL, (3, 0))
         blend_tail(7)
         quantise_h(3 * BLOCK + TAIL, TAIL)
-        second_product(3 * BLOCK + TAIL, TAIL, (5, 3))
+        second_product(3 * BLOCK + TAIL, TAIL, (5, 6), True)

@@ -25,6 +25,7 @@ BANK = 512
 BLOCKS = 3
 TAIL = 128
 PASS1_ROWS = 16
+POOL_EXTRA = 80
 VECTOR_SHARE = (20, 58, 80, 58)
 
 
@@ -153,6 +154,8 @@ def tile_list_session_memory_blend_kernel(
             return w_codes[n][:, cols].bitcast(FP8X4), w_scales[n][:, cols]
 
         def span(i):
+            if i < 2:
+                return i * TAIL, TAIL, (0, 1, 2, 3)
             if i < 2 * BLOCKS:
                 return (i // 2) * BLOCK, BLOCK, (2 * (i % 2), 2 * (i % 2) + 1)
             return BLOCKS * BLOCK + (i - 2 * BLOCKS) * TAIL, TAIL, (0, 1, 2, 3)
@@ -208,6 +211,10 @@ def tile_list_session_memory_blend_kernel(
                 ALU.add,
             )
 
+        def blend_tile(i):
+            cols = slice(i * BANK, (i + 1) * BANK)
+            nc.gpsimd.tensor_tensor(h_rounded[:, cols], gated[:, cols], rests[:, cols], ALU.add)
+
         def blend_tail(i):
             nc.vector.scalar_tensor_tensor(piece(h_rounded, i), acc_b[i], -2.0, piece(gated, i), ALU.mult, ALU.add)
 
@@ -244,6 +251,10 @@ def tile_list_session_memory_blend_kernel(
                         nc.scalar.activation(
                             staged[:, e, :], acc[:, e, :], ACT.Identity, bias=bias[:, c : c + 1], scale=-0.5
                         )
+                        if width == BLOCK:
+                            nc.sync.dma_start(out_rows[:, c, cols], staged[:, e, :])
+                if width == BLOCK:
+                    continue
                 nc.sync.dma_start(out_rows[:, 2 * pair : 2 * pair + 2, cols], staged[:])
 
         for i in range(4):
@@ -276,8 +287,9 @@ def tile_list_session_memory_blend_kernel(
         gate(4)
         gate(5)
         gate_a(0)
+        blend_tile(0)
         gate_a(1)
-        blend_block(0, nc.gpsimd)
+        blend_tile(1)
         acc_a[2] = first_product("a", 2, 4)
         acc_a[3] = first_product("a", 3, 2)
         acc_p[6] = first_product("p", 6, 5)
@@ -288,6 +300,7 @@ def tile_list_session_memory_blend_kernel(
         acc_a[6] = first_product("ba", 6, 3)
         gate_a(2)
         gate_a(3)
+        blend_block(1, nc.gpsimd, 0, POOL_EXTRA)
         acc_p[7] = first_product("p", 7, 5)
         gate(7)
         rest(4)
@@ -296,12 +309,12 @@ def tile_list_session_memory_blend_kernel(
         quantise_h(0, BLOCK)
         second_product(0, BLOCK, (2, 4))
         acc_b[6] = first_product("b", 6, 0)
-        blend_block(1, nc.vector)
+        acc_a[7] = first_product("ba", 7, 1)
+        acc_b[7] = first_product("b", 7, 6)
+        blend_block(1, nc.vector, POOL_EXTRA, BLOCK)
         gate_a(5)
         quantise_h(BLOCK, BLOCK)
-        second_product(BLOCK, BLOCK, (5, 6))
-        acc_a[7] = first_product("ba", 7, 1)
-        acc_b[7] = first_product("b", 7, 7)
+        second_product(BLOCK, BLOCK, (5, 7))
         blend_block(2, nc.vector)
         gate_a(6)
         quantise_h(2 * BLOCK, BLOCK)
@@ -312,4 +325,4 @@ def tile_list_session_memory_blend_kernel(
         second_product(3 * BLOCK, TAIL, (3, 0))
         blend_tail(7)
         quantise_h(3 * BLOCK + TAIL, TAIL)
-        second_product(3 * BLOCK + TAIL, TAIL, (5, 6), True)
+        second_product(3 * BLOCK + TAIL, TAIL, (5, 7), True)

@@ -182,7 +182,7 @@ def tile_list_session_memory_blend_kernel(
             return ap.rearrange("p (s e) -> p s e", e=len(span(i)[2]))
 
         gates = {}
-        rests = keep.tile([P, 6 * BANK], F32, name="rests")
+        rests = keep.tile([P, 8 * BANK], F32, name="rests")
         gated = keep.tile([P, 8 * BANK], F32, name="gated")
         h_rounded = keep.tile([P, S * PACK], BF16, name="h_rounded", align_bytes=64)
         h_codes = keep.tile([P, S], U32, name="h_codes", align_bytes=64)
@@ -211,9 +211,9 @@ def tile_list_session_memory_blend_kernel(
                 ALU.add,
             )
 
-        def blend_tile(i):
+        def blend_tile(i, engine=nc.gpsimd):
             cols = slice(i * BANK, (i + 1) * BANK)
-            nc.gpsimd.tensor_tensor(h_rounded[:, cols], gated[:, cols], rests[:, cols], ALU.add)
+            engine.tensor_tensor(h_rounded[:, cols], gated[:, cols], rests[:, cols], ALU.add)
 
         def blend_tail(i):
             nc.vector.scalar_tensor_tensor(piece(h_rounded, i), acc_b[i], -2.0, piece(gated, i), ALU.mult, ALU.add)
@@ -309,20 +309,21 @@ def tile_list_session_memory_blend_kernel(
         quantise_h(0, BLOCK)
         second_product(0, BLOCK, (2, 4))
         acc_b[6] = first_product("b", 6, 0)
-        acc_a[7] = first_product("ba", 7, 1)
         acc_b[7] = first_product("b", 7, 6)
         blend_block(1, nc.vector, POOL_EXTRA, BLOCK)
         gate_a(5)
         quantise_h(BLOCK, BLOCK)
-        second_product(BLOCK, BLOCK, (5, 7))
+        second_product(BLOCK, BLOCK, (5, 1))
+        acc_a[7] = first_product("a", 7, 7)
         blend_block(2, nc.vector)
         gate_a(6)
         quantise_h(2 * BLOCK, BLOCK)
         second_product(2 * BLOCK, BLOCK, (2, 4))
+        rest(7)
         blend_tail(6)
         gate_a(7)
         quantise_h(3 * BLOCK, TAIL)
         second_product(3 * BLOCK, TAIL, (3, 0))
-        blend_tail(7)
+        blend_tile(7, nc.vector)
         quantise_h(3 * BLOCK + TAIL, TAIL)
-        second_product(3 * BLOCK + TAIL, TAIL, (5, 7), True)
+        second_product(3 * BLOCK + TAIL, TAIL, (5, 1), True)

@@ -26,7 +26,7 @@ BLOCKS = 3
 TAIL = 128
 PASS1_ROWS = 16
 POOL_EXTRA = 80
-VECTOR_SHARE = (20, 58, 80, 58)
+VECTOR_SHARE = (20, 58, 80, 72)
 
 
 def tile_list_session_memory_blend_kernel(
@@ -267,8 +267,8 @@ def tile_list_session_memory_blend_kernel(
             acc_p[i] = first_product("p", i, 4 + i)
 
         quantise_weight(2, -1.0)
-        first_gates = keep.tile([P, 2 * BANK], F32, name="first_gates", tag="raw2", align_bytes=64)
-        for i in range(2):
+        first_gates = keep.tile([P, 3 * BANK], F32, name="first_gates", tag="raw2", align_bytes=64)
+        for i in range(3):
             gates[i] = piece(first_gates, i)
             gate(i)
             rest(i)
@@ -276,54 +276,52 @@ def tile_list_session_memory_blend_kernel(
             acc_p[i] = first_product("p", i, i)
             acc_b[i] = first_product("b", i, i - 4)
         quantise_weight(3, -1.0)
-        later_gates = keep.tile([P, 6 * BANK], F32, name="later_gates", tag="raw3", align_bytes=64)
-        for i in range(2, 8):
-            gates[i] = by_token(later_gates[:, (i - 2) * BANK : (i - 1) * BANK], i)
-        gate(2)
-        gate(3)
+        later_gates = keep.tile([P, 5 * BANK], F32, name="later_gates", tag="raw3", align_bytes=64)
+        for i in range(3, 8):
+            gates[i] = by_token(later_gates[:, (i - 3) * BANK : (i - 2) * BANK], i)
         acc_a[0] = first_product("a", 0, 6)
-        acc_a[1] = first_product("a", 1, 7)
-        rest(2)
+        acc_a[1] = first_product("a", 1, 2)
+        gate(3)
         gate(4)
         gate(5)
+        rest(3)
+        rest(4)
         gate_a(0)
         blend_tile(0)
         gate_a(1)
         blend_tile(1)
-        acc_a[2] = first_product("a", 2, 4)
-        acc_a[3] = first_product("a", 3, 2)
+        acc_a[2] = first_product("a", 2, 7)
+        acc_a[3] = first_product("a", 3, 4)
         acc_p[6] = first_product("p", 6, 5)
-        rest(3)
         gate(6)
         acc_a[4] = first_product("a", 4, 6)
-        acc_a[5] = first_product("a", 5, 7)
+        acc_a[5] = first_product("a", 5, 2)
         acc_a[6] = first_product("ba", 6, 3)
         gate_a(2)
         gate_a(3)
         blend_block(1, nc.gpsimd, 0, POOL_EXTRA)
         acc_p[7] = first_product("p", 7, 5)
         gate(7)
-        rest(4)
         rest(5)
         gate_a(4)
-        quantise_h(0, BLOCK)
-        second_product(0, BLOCK, (2, 4))
-        acc_b[6] = first_product("b", 6, 0)
-        acc_b[7] = first_product("b", 7, 6)
-        blend_block(1, nc.vector, POOL_EXTRA, BLOCK)
         gate_a(5)
-        quantise_h(BLOCK, BLOCK)
-        second_product(BLOCK, BLOCK, (5, 1))
-        acc_a[7] = first_product("a", 7, 7)
-        blend_block(2, nc.vector)
+        quantise_h(0, BLOCK)
+        second_product(0, BLOCK, (7, 4))
+        acc_b[6] = first_product("b", 6, 6)
+        blend_block(1, nc.vector, POOL_EXTRA, BLOCK)
         gate_a(6)
-        quantise_h(2 * BLOCK, BLOCK)
-        second_product(2 * BLOCK, BLOCK, (2, 4))
-        rest(7)
+        quantise_h(BLOCK, BLOCK)
+        second_product(BLOCK, BLOCK, (5, 0))
+        acc_b[7] = first_product("b", 7, 3)
+        acc_a[7] = first_product("a", 7, 2)
+        blend_block(2, nc.vector)
         blend_tail(6)
+        quantise_h(2 * BLOCK, BLOCK)
+        second_product(2 * BLOCK, BLOCK, (7, 4))
+        rest(7)
         gate_a(7)
         quantise_h(3 * BLOCK, TAIL)
-        second_product(3 * BLOCK, TAIL, (3, 0))
+        second_product(3 * BLOCK, TAIL, (1, 6))
         blend_tile(7, nc.vector)
         quantise_h(3 * BLOCK + TAIL, TAIL)
-        second_product(3 * BLOCK + TAIL, TAIL, (5, 1), True)
+        second_product(3 * BLOCK + TAIL, TAIL, (5, 0), True)

@@ -25,8 +25,8 @@ BANK = 512
 BLOCKS = 3
 TAIL = 128
 PASS1_ROWS = 16
-POOL_EXTRA = 80
-VECTOR_SHARE = (20, 58, 80, 72)
+POOL = 80
+VECTOR_SHARE = (28, 68, 84, 60)
 
 
 def tile_list_session_memory_blend_kernel(
@@ -36,53 +36,71 @@ def tile_list_session_memory_blend_kernel(
     with ExitStack() as ctx:
         keep = ctx.enter_context(tc.tile_pool(name="keep", bufs=1))
         ring = ctx.enter_context(tc.tile_pool(name="ring", bufs=5))
+        shared = ctx.enter_context(tc.tile_pool(name="shared", bufs=1))
         psum = ctx.enter_context(tc.psum_pool(name="psum", bufs=1))
 
         offsets = keep.tile([P, S // 16], U16, name="offsets")
         tab_words = keep.tile([P, T], I32, name="tab_words", align_bytes=64)
         tab_scales = keep.tile([P, T], U8, name="tab_scales", align_bytes=64)
         wb_raw = keep.tile([P, PASSES * H // 2], I32, name="wb_raw", align_bytes=64)
-        wb_scales_raw = keep.tile([P, PASSES * H], U8, name="wb_scales_raw", tag="picked23", align_bytes=64)
+        wb_scales_raw = shared.tile([P, PASSES * H], U8, name="wb_scales_raw", offset=H, align_bytes=64)
+        picked_scales = keep.tile([P, S], U8, name="picked_scales", align_bytes=64)
         v_scales0 = keep.tile([P, S], U8, name="v_scales0", align_bytes=64)
         v_scales1 = keep.tile([P, S], U8, name="v_scales1", align_bytes=64)
         wo_codes = keep.tile([P, N], I32, name="wo_codes", align_bytes=64)
         wo_scale_tile = keep.tile([P, N], U8, name="wo_scale_tile", align_bytes=64)
 
-        nc.gpsimd.memset(tab_scales[:].bitcast(I32), 0)
         nc.gpsimd.memset(wb_scales_raw[:].bitcast(I32), 0)
-        nc.gpsimd.memset(v_scales1[:].bitcast(I32), 0)
-        nc.gpsimd.memset(wo_scale_tile[:].bitcast(I32), 0)
+        nc.gpsimd.memset(tab_scales[32:64, :].bitcast(I32), 0)
+        nc.vector.memset(tab_scales[64:, :].bitcast(I32), 0)
+        nc.vector.memset(v_scales0[:].bitcast(I32), 0)
+        nc.vector.memset(v_scales1[:].bitcast(I32), 0)
+        nc.vector.memset(wo_scale_tile[:].bitcast(I32), 0)
 
         raw = []
 
-        def load_weight(w, a):
-            rows = keep.tile([P, PACK, H], F32, name="raw%d" % len(raw), tag="raw%d" % len(raw), align_bytes=64)
-            nc.sync.dma_start(rows[:], w[512 * a : 512 * (a + 1), :].rearrange("(p j) c -> p j c", j=PACK))
-            raw.append(rows)
+        def load_weight(w, a, half=None):
+            src = w[512 * a : 512 * (a + 1), :].rearrange("(p j) c -> p j c", j=PACK)
+            if half != 1:
+                raw.append(keep.tile([P, PACK, H], F32, name="raw%d" % len(raw), tag="raw%d" % len(raw), align_bytes=64))
+            rows = slice(0, PACK) if half is None else slice(2 * half, 2 * half + 2)
+            nc.sync.dma_start(raw[-1][:, rows, :], src[:, rows, :])
 
         nc.sync.dma_start(offsets[:], offs)
+        scale_rows = tab[0, 512 * T :].bitcast(I32).rearrange("(q w) -> q w", q=32)
+        nc.sync.dma_start(tab_scales[:32, :].bitcast(I32), scale_rows)
+        nc.sync.dma_start(tab_words[:], tab[0, : 512 * T].rearrange("(p b) -> p b", p=P).bitcast(I32))
         nc.sync.dma_start(
             wb_raw[:].rearrange("p (a w) -> p a w", a=PASSES),
             wb_words.bitcast(I32).rearrange("a p w -> p a w"),
         )
-        scale_rows = tab[0, 512 * T :].bitcast(I32).rearrange("(a quad r w) -> r quad a w", a=PASSES, quad=QUADS, r=4)
-        for r in range(4):
-            nc.sync.dma_start(tab_scales[r:P:PASS1_ROWS, :].bitcast(I32), scale_rows[r])
-        nc.sync.dma_start(tab_words[:], tab[0, : 512 * T].rearrange("(p b) -> p b", p=P).bitcast(I32))
         wb_rows = wb_scales.bitcast(I32).rearrange("a q w -> q a w")
         for quad in range(QUADS):
             nc.sync.dma_start(
                 wb_scales_raw[32 * quad : 32 * quad + 4, :].bitcast(I32).rearrange("q (a w) -> q a w", a=PASSES),
                 wb_rows[4 * quad : 4 * quad + 4],
             )
-        load_weight(wg, 0)
+        load_weight(wg, 1)
 
-        nc.vector.tensor_copy(v_scales0[:], tab_scales[:].indirect(offsets[:]))
-        for r in range(4):
-            nc.sync.dma_start(v_scales1[r:P:32, :].bitcast(I32), v_scales0[PASS1_ROWS + r : P : 32, :].bitcast(I32))
+        wb_codes = keep.tile([P, PASSES * H], U16, name="wb_codes", align_bytes=64)
+        wb_scale_tile = keep.tile([P, PASSES * H], U8, name="wb_scale_tile", align_bytes=64)
+        nc.scalar.copy(
+            wb_codes[:].rearrange("p (a t m) -> p a t m", a=PASSES, t=PACK),
+            wb_raw[:].bitcast(U16).rearrange("p (a m t) -> p a t m", a=PASSES, t=PACK),
+        )
+        nc.vector.tensor_copy(picked_scales[:], tab_scales[:].indirect(offsets[:]))
         v_scales = (v_scales0, v_scales1)
 
-        load_weight(wg, 1)
+        def place_scales(a):
+            for quad in range(QUADS):
+                row = 16 * a + 4 * quad
+                nc.sync.dma_start(
+                    v_scales[a][32 * quad : 32 * quad + 4, :].bitcast(I32), picked_scales[row : row + 4, :].bitcast(I32)
+                )
+
+        place_scales(0)
+        load_weight(wg, 0)
+        place_scales(1)
         load_weight(wa, 0)
         load_weight(wa, 1)
         nc.sync.dma_start(wo_codes[:], wo_words[0].rearrange("p c i -> p (c i)").bitcast(I32))
@@ -93,55 +111,64 @@ def tile_list_session_memory_blend_kernel(
             )
         bias = keep.tile([P, N // P], F32, name="bias", align_bytes=64)
 
-        v_codes = []
+        v_codes = {}
 
-        def gather_words(picked):
-            q = len(v_codes)
+        def gather_words(picked, q):
             cols = BLOCK // 16
             nc.vector.tensor_copy(picked, tab_words[:].bitcast(U32).indirect(offsets[:, q * cols : (q + 1) * cols]))
-            parted = keep.tile([P, PASSES * BLOCK], U16, name="parted%d" % q, align_bytes=64)
+
+        def part_words(picked, first, width):
+            if first == 0:
+                parted = shared.tile([P, PASSES * width], U16, name="parted0", offset=0, align_bytes=64)
+            else:
+                parted = keep.tile([P, PASSES * width], U16, name="parted%d" % first, align_bytes=64)
             nc.vector.tensor_copy(
                 parted[:].rearrange("p (a s) -> p a s", a=PASSES),
                 picked.bitcast(U16).rearrange("p (s a) -> p a s", a=PASSES),
             )
-            v_codes.append(parted)
+            v_codes[first] = parted
 
         picked0 = keep.tile([P, BLOCK], U32, name="picked0", align_bytes=64)
-        gather_words(picked0[:])
-        wb_codes = keep.tile([P, PASSES * H], U16, name="wb_codes", align_bytes=64)
-        wb_scale_tile = keep.tile([P, PASSES * H], U8, name="wb_scale_tile", align_bytes=64)
-        nc.vector.tensor_copy(
-            wb_codes[:].rearrange("p (a t m) -> p a t m", a=PASSES, t=PACK),
-            wb_raw[:].bitcast(U16).rearrange("p (a m t) -> p a t m", a=PASSES, t=PACK),
-        )
+        gather_words(picked0[:], 0)
         nc.vector.tensor_copy(
             wb_scale_tile[:].rearrange("p (a t m) -> p a t m", a=PASSES, t=PACK),
             wb_scales_raw[:].rearrange("p (a m t) -> p a t m", a=PASSES, t=PACK),
         )
-        picked1 = keep.tile([P, BLOCK], U32, name="picked1", align_bytes=64)
-        gather_words(picked1[:])
-        picked23 = keep.tile([P, 2 * BLOCK], U32, name="picked23", tag="picked23", align_bytes=64)
-        gather_words(picked23[:, :BLOCK])
-        gather_words(picked23[:, BLOCK:])
+        part_words(picked0[:], 0, BLOCK)
+        picked = shared.tile([P, 3 * BLOCK], U32, name="picked", offset=2 * H, align_bytes=64)
+        gather_words(picked[:, :BLOCK], 1)
+        gather_words(picked[:, BLOCK : 2 * BLOCK], 2)
+        part_words(picked[:, :BLOCK], BLOCK, BLOCK)
+        gather_words(picked[:, 2 * BLOCK :], 3)
+        for first, width in ((2 * BLOCK, BLOCK), (3 * BLOCK, BLOCK)):
+            part_words(picked[:, first - BLOCK : first - BLOCK + width], first, width)
 
         w_codes, w_scales = [], []
 
-        def quantise_weight(n, sign):
+        def quantise_weight(n):
             grouped = keep.tile([P, H * PACK], BF16, name="grouped%d" % n, tag="grouped%d" % n, align_bytes=64)
-            dst = grouped[:].rearrange("p (t m j) -> p m j t", t=PACK, j=PACK)
-            src = raw[n][:].rearrange("p j (m t) -> p m j t", t=PACK)
             cut = VECTOR_SHARE[n]
-            if sign < 0:
-                nc.scalar.activation(dst[:, cut:], src[:, cut:], ACT.Copy, scale=sign)
-                nc.vector.tensor_scalar_mul(dst[:, :cut], src[:, :cut], sign)
+            if n >= PASSES:
+                dst = grouped[:].rearrange("p (t m j) -> p m j t", t=PACK, j=PACK)
+                src = raw[n][:].rearrange("p j (m t) -> p m j t", t=PACK)
+                if cut < P:
+                    nc.scalar.activation(dst[:, cut:], src[:, cut:], ACT.Copy, scale=-1.0)
+                nc.vector.tensor_scalar_mul(dst[:, :cut], src[:, :cut], -1.0)
             else:
                 dst = grouped[:].rearrange("p (t m y z) -> p m y t z", t=PACK, y=2, z=2)
                 src = raw[n][:].rearrange("p (y z) (m t) -> p m y t z", y=2, t=PACK)
                 nc.scalar.copy(dst[:, cut:], src[:, cut:])
-                nc.vector.tensor_copy(dst[:, :cut], src[:, :cut])
+                if cut:
+                    nc.vector.tensor_copy(dst[:, :cut], src[:, :cut])
             codes = keep.tile([P, H], U32, name="w_codes%d" % n, align_bytes=64)
             scales = keep.tile([P, H], U8, name="w_scales%d" % n, align_bytes=64)
-            nc.vector.quantize_mx(out=codes[:].bitcast(FP8X4), scales=scales[:], in_=grouped[:])
+            for u in range(2):
+                cols = slice(u * H // 2, (u + 1) * H // 2)
+                nc.vector.quantize_mx(
+                    out=codes[:, cols].bitcast(FP8X4),
+                    scales=scales[:, cols],
+                    in_=grouped[:, u * H * PACK // 2 : (u + 1) * H * PACK // 2],
+                )
             w_codes.append(codes)
             w_scales.append(scales)
 
@@ -149,46 +176,59 @@ def tile_list_session_memory_blend_kernel(
             if kind == "b":
                 cols = slice(a * H + t * P, a * H + (t + 1) * P)
                 return wb_codes[:, cols].bitcast(FP4X4), wb_scale_tile[:, cols]
-            n = a if kind == "p" else PASSES + a
+            n = 1 - a if kind == "p" else PASSES + a
             cols = slice(t * P, (t + 1) * P)
             return w_codes[n][:, cols].bitcast(FP8X4), w_scales[n][:, cols]
 
         def span(i):
-            if i < 2:
-                return i * TAIL, TAIL, (0, 1, 2, 3)
-            if i < 2 * BLOCKS:
+            if 2 <= i < 2 * BLOCKS:
                 return (i // 2) * BLOCK, BLOCK, (2 * (i % 2), 2 * (i % 2) + 1)
-            return BLOCKS * BLOCK + (i - 2 * BLOCKS) * TAIL, TAIL, (0, 1, 2, 3)
+            return i * TAIL, TAIL, (0, 1, 2, 3)
 
-        def first_product(kinds, i, bank):
+        banks, todo = {}, {}
+
+        def open_product(kinds, i, bank):
             first, width, slots = span(i)
             acc = psum.tile([P, len(slots), width], F32, name="acc_%s%d" % (kinds, i), tag="bank%d" % bank)
+            banks[kinds, i] = acc
+            todo[kinds, i] = [(kind, a) for kind in kinds for a in ((1, 0) if kind == "p" and i < 4 else (0, 1))]
+            return acc[:].rearrange("p e s -> p s e")
+
+        def run_pass(kinds, i):
+            first, width, slots = span(i)
             q, lo = divmod(first, BLOCK)
-            steps = [(kind, a, e) for kind in kinds for a in range(PASSES) for e in range(len(slots))]
-            for n, (kind, a, e) in enumerate(steps):
-                lhs, lhs_scale = stationary(kind, a, slots[e])
+            opening = len(todo[kinds, i]) == PASSES * len(kinds)
+            kind, a = todo[kinds, i].pop(0)
+            for e, t in enumerate(slots):
+                lhs, lhs_scale = stationary(kind, a, t)
                 nc.tensor.matmul_mx(
-                    out=acc[:, e, :],
+                    out=banks[kinds, i][:, e, :],
                     lhsT=lhs,
                     lhsT_scale=lhs_scale,
-                    rhs=v_codes[q][:, a * BLOCK + lo : a * BLOCK + lo + width].bitcast(FP4X4),
+                    rhs=v_codes[q * BLOCK][:, a * BLOCK + lo : a * BLOCK + lo + width].bitcast(FP4X4),
                     rhs_scale=v_scales[a][:, first : first + width],
-                    start=(n == 0),
-                    stop=(n == len(steps) - 1),
+                    start=(opening and e == 0),
+                    stop=(not todo[kinds, i] and e == len(slots) - 1),
                 )
-            return acc[:].rearrange("p e s -> p s e")
+
+        def first_product(kinds, i, bank):
+            acc = open_product(kinds, i, bank)
+            while todo[kinds, i]:
+                run_pass(kinds, i)
+            return acc
 
         def by_token(ap, i):
             return ap.rearrange("p (s e) -> p s e", e=len(span(i)[2]))
 
         gates = {}
-        rests = keep.tile([P, 8 * BANK], F32, name="rests")
+        rests = {}
         gated = keep.tile([P, 8 * BANK], F32, name="gated")
         h_rounded = keep.tile([P, S * PACK], BF16, name="h_rounded", align_bytes=64)
+        h_rows = {}
         h_codes = keep.tile([P, S], U32, name="h_codes", align_bytes=64)
         h_scales = keep.tile([P, S], U8, name="h_scales", align_bytes=64)
         out_rows = out.rearrange("(c p) s -> p c s", p=P)
-        acc_p, acc_b, acc_a = {}, {}, {}
+        acc_p, acc_b, acc_a, rest_pairs = {}, {}, {}, {}
 
         def piece(tile, i):
             return by_token(tile[:, i * BANK : (i + 1) * BANK], i)
@@ -197,34 +237,35 @@ def tile_list_session_memory_blend_kernel(
             nc.scalar.activation(gates[i], acc_p[i], ACT.Tanh, scale=0.5)
 
         def rest(i):
-            nc.vector.scalar_tensor_tensor(piece(rests, i), gates[i], 1.0, acc_b[i], ALU.subtract, ALU.mult)
+            nc.vector.scalar_tensor_tensor(by_token(rests[i], i), gates[i], 1.0, acc_b[i], ALU.subtract, ALU.mult)
 
         def gate_a(i):
             nc.vector.scalar_tensor_tensor(piece(gated, i), gates[i], 1.0, acc_a[i], ALU.add, ALU.mult)
 
-        def blend_block(k, engine, lo=0, hi=BLOCK):
+        def rows(first, count):
+            return h_rounded[:, first * PACK : (first + count) * PACK]
+
+        def blend_block(k, engine, lo, hi, place):
             cols = slice(2 * k * BANK, 2 * (k + 1) * BANK)
             engine.tensor_tensor(
-                h_rounded[:, cols].rearrange("p (s u e) -> p s u e", u=2, e=2)[:, lo:hi],
+                rows(place, hi - lo).rearrange("p (s u e) -> p s u e", u=2, e=2),
                 gated[:, cols].rearrange("p (u s e) -> p s u e", u=2, e=2)[:, lo:hi],
-                rests[:, cols].rearrange("p (u s e) -> p s u e", u=2, e=2)[:, lo:hi],
+                rest_pairs[k].rearrange("p (u s e) -> p s u e", u=2, e=2)[:, lo:hi],
                 ALU.add,
             )
 
-        def blend_tile(i, engine=nc.gpsimd):
-            cols = slice(i * BANK, (i + 1) * BANK)
-            engine.tensor_tensor(h_rounded[:, cols], gated[:, cols], rests[:, cols], ALU.add)
-
-        def blend_tail(i):
-            nc.vector.scalar_tensor_tensor(piece(h_rounded, i), acc_b[i], -2.0, piece(gated, i), ALU.mult, ALU.add)
-
-        def quantise_h(first, width):
-            cols = slice(first, first + width)
-            nc.vector.quantize_mx(
-                out=h_codes[:, cols].bitcast(FP8X4),
-                scales=h_scales[:, cols],
-                in_=h_rounded[:, first * PACK : (first + width) * PACK],
+        def blend_tile(i, engine, lo=0, hi=TAIL):
+            cols = slice(lo * PACK, hi * PACK)
+            engine.tensor_tensor(
+                h_rows[i][:, cols], gated[:, i * BANK : (i + 1) * BANK][:, cols], rests[i][:, cols], ALU.add
             )
+
+        def blend_summed(i):
+            nc.vector.scalar_tensor_tensor(by_token(h_rows[i], i), acc_b[i], -2.0, piece(gated, i), ALU.mult, ALU.add)
+
+        def quantise_h(first, width, rows):
+            cols = slice(first, first + width)
+            nc.vector.quantize_mx(out=h_codes[:, cols].bitcast(FP8X4), scales=h_scales[:, cols], in_=rows)
 
         def second_product(first, width, banks, shared=False):
             cols = slice(first, first + width)
@@ -257,39 +298,51 @@ def tile_list_session_memory_blend_kernel(
                     continue
                 nc.sync.dma_start(out_rows[:, 2 * pair : 2 * pair + 2, cols], staged[:])
 
+        for i in (0, 1, 6, 7):
+            h_rows[i] = rows(i * TAIL, TAIL)
         for i in range(4):
-            acc_b[i] = first_product("b", i, i)
-        quantise_weight(0, 1.0)
-        quantise_weight(1, 1.0)
+            acc_b[i] = open_product("b", i, i)
+            run_pass("b", i)
+        for i in range(4):
+            run_pass("b", i)
+        quantise_weight(0)
+        for i in range(4):
+            acc_p[i] = open_product("p", i, 4 + i)
+            run_pass("p", i)
+        quantise_weight(1)
         with nc.allow_non_contiguous_dma(reason="one bias value for each partition and block of 128 outputs"):
             nc.sync.dma_start(bias[:], bo.rearrange("(c p) -> p c", p=P))
         for i in range(4):
-            acc_p[i] = first_product("p", i, 4 + i)
-
-        quantise_weight(2, -1.0)
-        first_gates = keep.tile([P, 3 * BANK], F32, name="first_gates", tag="raw2", align_bytes=64)
+            run_pass("p", i)
+        quantise_weight(2)
+        early = keep.tile([P, 3 * BANK], F32, name="early", tag="raw2", align_bytes=64)
+        all_rests = keep.tile([P, 8 * BANK], F32, name="all_rests", align_bytes=64)
+        for i in range(8):
+            rests[i] = all_rests[:, i * BANK : (i + 1) * BANK]
+        for k in (1, 2):
+            rest_pairs[k] = all_rests[:, 2 * k * BANK : 2 * (k + 1) * BANK]
         for i in range(3):
-            gates[i] = piece(first_gates, i)
+            gates[i] = piece(early, i)
             gate(i)
             rest(i)
         for i in range(4, 6):
             acc_p[i] = first_product("p", i, i)
             acc_b[i] = first_product("b", i, i - 4)
-        quantise_weight(3, -1.0)
-        later_gates = keep.tile([P, 5 * BANK], F32, name="later_gates", tag="raw3", align_bytes=64)
+        quantise_weight(3)
+        late = keep.tile([P, 5 * BANK], F32, name="late", tag="raw3", align_bytes=64)
         for i in range(3, 8):
-            gates[i] = by_token(later_gates[:, (i - 3) * BANK : (i - 2) * BANK], i)
+            gates[i] = by_token(late[:, (i - 3) * BANK : (i - 2) * BANK], i)
         acc_a[0] = first_product("a", 0, 6)
         acc_a[1] = first_product("a", 1, 2)
         gate(3)
         gate(4)
         gate(5)
         rest(3)
-        rest(4)
         gate_a(0)
-        blend_tile(0)
+        blend_tile(0, nc.gpsimd)
         gate_a(1)
-        blend_tile(1)
+        blend_tile(1, nc.gpsimd)
+        rest(4)
         acc_a[2] = first_product("a", 2, 7)
         acc_a[3] = first_product("a", 3, 4)
         acc_p[6] = first_product("p", 6, 5)
@@ -299,29 +352,29 @@ def tile_list_session_memory_blend_kernel(
         acc_a[6] = first_product("ba", 6, 3)
         gate_a(2)
         gate_a(3)
-        blend_block(1, nc.gpsimd, 0, POOL_EXTRA)
+        blend_block(1, nc.gpsimd, 0, POOL, BLOCK)
         acc_p[7] = first_product("p", 7, 5)
         gate(7)
         rest(5)
         gate_a(4)
         gate_a(5)
-        quantise_h(0, BLOCK)
+        quantise_h(0, BLOCK, rows(0, BLOCK))
         second_product(0, BLOCK, (7, 4))
         acc_b[6] = first_product("b", 6, 6)
-        blend_block(1, nc.vector, POOL_EXTRA, BLOCK)
+        blend_block(1, nc.vector, POOL, BLOCK, BLOCK + POOL)
         gate_a(6)
-        quantise_h(BLOCK, BLOCK)
+        quantise_h(BLOCK, BLOCK, rows(BLOCK, BLOCK))
         second_product(BLOCK, BLOCK, (5, 0))
         acc_b[7] = first_product("b", 7, 3)
         acc_a[7] = first_product("a", 7, 2)
-        blend_block(2, nc.vector)
-        blend_tail(6)
-        quantise_h(2 * BLOCK, BLOCK)
+        blend_block(2, nc.vector, 0, BLOCK, 2 * BLOCK)
+        blend_summed(6)
+        quantise_h(2 * BLOCK, BLOCK, rows(2 * BLOCK, BLOCK))
         second_product(2 * BLOCK, BLOCK, (7, 4))
         rest(7)
         gate_a(7)
-        quantise_h(3 * BLOCK, TAIL)
+        quantise_h(3 * BLOCK, TAIL, h_rows[6])
         second_product(3 * BLOCK, TAIL, (1, 6))
         blend_tile(7, nc.vector)
-        quantise_h(3 * BLOCK + TAIL, TAIL)
+        quantise_h(3 * BLOCK + TAIL, TAIL, h_rows[7])
         second_product(3 * BLOCK + TAIL, TAIL, (5, 0), True)

@@ -40,15 +40,15 @@ def tile_list_session_memory_blend_kernel(
         psum = ctx.enter_context(tc.psum_pool(name="psum", bufs=1))
 
         offsets = keep.tile([P, S // 16], U16, name="offsets")
-        tab_words = keep.tile([P, T], I32, name="tab_words", align_bytes=64)
-        tab_scales = keep.tile([P, T], U8, name="tab_scales", align_bytes=64)
-        wb_raw = keep.tile([P, PASSES * H // 2], I32, name="wb_raw", align_bytes=64)
-        wb_scales_raw = shared.tile([P, PASSES * H], U8, name="wb_scales_raw", offset=H, align_bytes=64)
-        picked_scales = keep.tile([P, S], U8, name="picked_scales", align_bytes=64)
-        v_scales0 = keep.tile([P, S], U8, name="v_scales0", align_bytes=64)
-        v_scales1 = keep.tile([P, S], U8, name="v_scales1", align_bytes=64)
-        wo_codes = keep.tile([P, N], I32, name="wo_codes", align_bytes=64)
-        wo_scale_tile = keep.tile([P, N], U8, name="wo_scale_tile", align_bytes=64)
+        tab_words = keep.tile([P, T], I32, name="tab_words", align_bytes=256)
+        tab_scales = keep.tile([P, T], U8, name="tab_scales", align_bytes=256)
+        wb_raw = keep.tile([P, PASSES * H // 2], I32, name="wb_raw", align_bytes=256)
+        wb_scales_raw = shared.tile([P, PASSES * H], U8, name="wb_scales_raw", offset=H, align_bytes=256)
+        picked_scales = keep.tile([P, S], U8, name="picked_scales", align_bytes=256)
+        v_scales0 = keep.tile([P, S], U8, name="v_scales0", align_bytes=256)
+        v_scales1 = keep.tile([P, S], U8, name="v_scales1", align_bytes=256)
+        wo_codes = keep.tile([P, N], I32, name="wo_codes", align_bytes=256)
+        wo_scale_tile = keep.tile([P, N], U8, name="wo_scale_tile", align_bytes=256)
 
         nc.gpsimd.memset(wb_scales_raw[:].bitcast(I32), 0)
         nc.gpsimd.memset(tab_scales[32:64, :].bitcast(I32), 0)
@@ -62,7 +62,7 @@ def tile_list_session_memory_blend_kernel(
         def load_weight(w, a, half=None):
             src = w[512 * a : 512 * (a + 1), :].rearrange("(p j) c -> p j c", j=PACK)
             if half != 1:
-                raw.append(keep.tile([P, PACK, H], F32, name="raw%d" % len(raw), tag="raw%d" % len(raw), align_bytes=64))
+                raw.append(keep.tile([P, PACK, H], F32, name="raw%d" % len(raw), tag="raw%d" % len(raw), align_bytes=256))
             rows = slice(0, PACK) if half is None else slice(2 * half, 2 * half + 2)
             nc.sync.dma_start(raw[-1][:, rows, :], src[:, rows, :])
 
@@ -82,8 +82,8 @@ def tile_list_session_memory_blend_kernel(
             )
         load_weight(wg, 1)
 
-        wb_codes = keep.tile([P, PASSES * H], U16, name="wb_codes", align_bytes=64)
-        wb_scale_tile = keep.tile([P, PASSES * H], U8, name="wb_scale_tile", align_bytes=64)
+        wb_codes = keep.tile([P, PASSES * H], U16, name="wb_codes", align_bytes=256)
+        wb_scale_tile = keep.tile([P, PASSES * H], U8, name="wb_scale_tile", align_bytes=256)
         nc.scalar.copy(
             wb_codes[:].rearrange("p (a t m) -> p a t m", a=PASSES, t=PACK),
             wb_raw[:].bitcast(U16).rearrange("p (a m t) -> p a t m", a=PASSES, t=PACK),
@@ -109,7 +109,7 @@ def tile_list_session_memory_blend_kernel(
                 wo_scale_tile[32 * quad : 32 * quad + 4, :].bitcast(I32),
                 wo_scales[0, 4 * quad : 4 * quad + 4, :].bitcast(I32),
             )
-        bias = keep.tile([P, N // P], F32, name="bias", align_bytes=64)
+        bias = keep.tile([P, N // P], F32, name="bias", align_bytes=256)
 
         v_codes = {}
 
@@ -119,23 +119,23 @@ def tile_list_session_memory_blend_kernel(
 
         def part_words(picked, first, width):
             if first == 0:
-                parted = shared.tile([P, PASSES * width], U16, name="parted0", offset=0, align_bytes=64)
+                parted = shared.tile([P, PASSES * width], U16, name="parted0", offset=0, align_bytes=256)
             else:
-                parted = keep.tile([P, PASSES * width], U16, name="parted%d" % first, align_bytes=64)
+                parted = keep.tile([P, PASSES * width], U16, name="parted%d" % first, align_bytes=256)
             nc.vector.tensor_copy(
                 parted[:].rearrange("p (a s) -> p a s", a=PASSES),
                 picked.bitcast(U16).rearrange("p (s a) -> p a s", a=PASSES),
             )
             v_codes[first] = parted
 
-        picked0 = keep.tile([P, BLOCK], U32, name="picked0", align_bytes=64)
+        picked0 = keep.tile([P, BLOCK], U32, name="picked0", align_bytes=256)
         gather_words(picked0[:], 0)
         nc.vector.tensor_copy(
             wb_scale_tile[:].rearrange("p (a t m) -> p a t m", a=PASSES, t=PACK),
             wb_scales_raw[:].rearrange("p (a m t) -> p a t m", a=PASSES, t=PACK),
         )
         part_words(picked0[:], 0, BLOCK)
-        picked = shared.tile([P, 3 * BLOCK], U32, name="picked", offset=2 * H, align_bytes=64)
+        picked = shared.tile([P, 3 * BLOCK], U32, name="picked", offset=2 * H, align_bytes=256)
         gather_words(picked[:, :BLOCK], 1)
         gather_words(picked[:, BLOCK : 2 * BLOCK], 2)
         part_words(picked[:, :BLOCK], BLOCK, BLOCK)
@@ -146,7 +146,7 @@ def tile_list_session_memory_blend_kernel(
         w_codes, w_scales = [], []
 
         def quantise_weight(n):
-            grouped = keep.tile([P, H * PACK], BF16, name="grouped%d" % n, tag="grouped%d" % n, align_bytes=64)
+            grouped = keep.tile([P, H * PACK], BF16, name="grouped%d" % n, tag="grouped%d" % n, align_bytes=256)
             cut = VECTOR_SHARE[n]
             if n >= PASSES:
                 dst = grouped[:].rearrange("p (t m j) -> p m j t", t=PACK, j=PACK)
@@ -160,8 +160,8 @@ def tile_list_session_memory_blend_kernel(
                 nc.scalar.copy(dst[:, cut:], src[:, cut:])
                 if cut:
                     nc.vector.tensor_copy(dst[:, :cut], src[:, :cut])
-            codes = keep.tile([P, H], U32, name="w_codes%d" % n, align_bytes=64)
-            scales = keep.tile([P, H], U8, name="w_scales%d" % n, align_bytes=64)
+            codes = keep.tile([P, H], U32, name="w_codes%d" % n, align_bytes=256)
+            scales = keep.tile([P, H], U8, name="w_scales%d" % n, align_bytes=256)
             for u in range(2):
                 cols = slice(u * H // 2, (u + 1) * H // 2)
                 nc.vector.quantize_mx(
@@ -222,11 +222,11 @@ def tile_list_session_memory_blend_kernel(
 
         gates = {}
         rests = {}
-        gated = keep.tile([P, 8 * BANK], F32, name="gated")
-        h_rounded = keep.tile([P, S * PACK], BF16, name="h_rounded", align_bytes=64)
+        gated = keep.tile([P, 8 * BANK], F32, name="gated", align_bytes=256)
+        h_rounded = keep.tile([P, S * PACK], BF16, name="h_rounded", align_bytes=256)
         h_rows = {}
-        h_codes = keep.tile([P, S], U32, name="h_codes", align_bytes=64)
-        h_scales = keep.tile([P, S], U8, name="h_scales", align_bytes=64)
+        h_codes = keep.tile([P, S], U32, name="h_codes", align_bytes=256)
+        h_scales = keep.tile([P, S], U8, name="h_scales", align_bytes=256)
         out_rows = out.rearrange("(c p) s -> p c s", p=P)
         acc_p, acc_b, acc_a, rest_pairs = {}, {}, {}, {}
 
@@ -270,7 +270,7 @@ def tile_list_session_memory_blend_kernel(
         def second_product(first, width, banks, shared=False):
             cols = slice(first, first + width)
             for pair in range(2):
-                staged = ring.tile([P, 2, width], F32, name="staged", tag="staged%d" % pair)
+                staged = ring.tile([P, 2, width], F32, name="staged", tag="staged%d" % pair, align_bytes=256)
                 acc = psum.tile([P, 2, width], F32, name="acc_y", tag="bank%d" % banks[pair])
                 for e in range(2):
                     c = 2 * pair + e
@@ -315,8 +315,8 @@ def tile_list_session_memory_blend_kernel(
         for i in range(4):
             run_pass("p", i)
         quantise_weight(2)
-        early = keep.tile([P, 3 * BANK], F32, name="early", tag="raw2", align_bytes=64)
-        all_rests = keep.tile([P, 8 * BANK], F32, name="all_rests", align_bytes=64)
+        early = keep.tile([P, 3 * BANK], F32, name="early", tag="raw2", align_bytes=256)
+        all_rests = keep.tile([P, 8 * BANK], F32, name="all_rests", align_bytes=256)
         for i in range(8):
             rests[i] = all_rests[:, i * BANK : (i + 1) * BANK]
         for k in (1, 2):
@@ -329,7 +329,7 @@ def tile_list_session_memory_blend_kernel(
             acc_p[i] = first_product("p", i, i)
             acc_b[i] = first_product("b", i, i - 4)
         quantise_weight(3)
-        late = keep.tile([P, 5 * BANK], F32, name="late", tag="raw3", align_bytes=64)
+        late = keep.tile([P, 5 * BANK], F32, name="late", tag="raw3", align_bytes=256)
         for i in range(3, 8):
             gates[i] = by_token(late[:, (i - 3) * BANK : (i - 2) * BANK], i)
         acc_a[0] = first_product("a", 0, 6)

@@ -24,9 +24,12 @@ BLOCK = 256
 BANK = 512
 BLOCKS = 3
 TAIL = 128
-PASS1_ROWS = 16
-POOL = 80
-VECTOR_SHARE = (28, 68, 84, 60)
+ALIGN = 256
+FIRST_POOL = 56
+POOL = 136
+VECTOR_SHARE = (48, 76, 64)
+GPSIMD_SHARE = 60
+FIRST_PIECE = 16
 
 
 def tile_list_session_memory_blend_kernel(
@@ -39,32 +42,32 @@ def tile_list_session_memory_blend_kernel(
         shared = ctx.enter_context(tc.tile_pool(name="shared", bufs=1))
         psum = ctx.enter_context(tc.psum_pool(name="psum", bufs=1))
 
+        def kept(name, width, dtype):
+            return keep.tile([P, width], dtype, name=name, align_bytes=ALIGN)
+
         offsets = keep.tile([P, S // 16], U16, name="offsets")
-        tab_words = keep.tile([P, T], I32, name="tab_words", align_bytes=256)
-        tab_scales = keep.tile([P, T], U8, name="tab_scales", align_bytes=256)
-        wb_raw = keep.tile([P, PASSES * H // 2], I32, name="wb_raw", align_bytes=256)
-        wb_scales_raw = shared.tile([P, PASSES * H], U8, name="wb_scales_raw", offset=H, align_bytes=256)
-        picked_scales = keep.tile([P, S], U8, name="picked_scales", align_bytes=256)
-        v_scales0 = keep.tile([P, S], U8, name="v_scales0", align_bytes=256)
-        v_scales1 = keep.tile([P, S], U8, name="v_scales1", align_bytes=256)
-        wo_codes = keep.tile([P, N], I32, name="wo_codes", align_bytes=256)
-        wo_scale_tile = keep.tile([P, N], U8, name="wo_scale_tile", align_bytes=256)
+        tab_words = kept("tab_words", T, I32)
+        tab_scales = kept("tab_scales", T, U8)
+        wb_raw = kept("wb_raw", PASSES * H // 2, I32)
+        wb_scales_raw = shared.tile([P, PASSES * H], U8, name="wb_scales_raw", offset=0, align_bytes=ALIGN)
+        picked_scales = kept("picked_scales", S, U8)
+        v_scales = [kept("v_scales%d" % a, S, U8) for a in range(PASSES)]
+        wo_codes = kept("wo_codes", N, I32)
+        wo_scale_tile = kept("wo_scale_tile", N, U8)
 
         nc.gpsimd.memset(wb_scales_raw[:].bitcast(I32), 0)
         nc.gpsimd.memset(tab_scales[32:64, :].bitcast(I32), 0)
         nc.vector.memset(tab_scales[64:, :].bitcast(I32), 0)
-        nc.vector.memset(v_scales0[:].bitcast(I32), 0)
-        nc.vector.memset(v_scales1[:].bitcast(I32), 0)
+        nc.vector.memset(v_scales[0][:].bitcast(I32), 0)
+        nc.vector.memset(v_scales[1][:].bitcast(I32), 0)
         nc.vector.memset(wo_scale_tile[:].bitcast(I32), 0)
 
-        raw = []
+        rows_width = PACK * H
+        raw_tiles = [kept("raw%d" % n, rows_width + (BANK if n == 3 else 0), F32) for n in range(4)]
+        raw = [t[:, :rows_width].rearrange("p (j c) -> p j c", j=PACK) for t in raw_tiles]
 
-        def load_weight(w, a, half=None):
-            src = w[512 * a : 512 * (a + 1), :].rearrange("(p j) c -> p j c", j=PACK)
-            if half != 1:
-                raw.append(keep.tile([P, PACK, H], F32, name="raw%d" % len(raw), tag="raw%d" % len(raw), align_bytes=256))
-            rows = slice(0, PACK) if half is None else slice(2 * half, 2 * half + 2)
-            nc.sync.dma_start(raw[-1][:, rows, :], src[:, rows, :])
+        def load_weight(w, a, n):
+            nc.sync.dma_start(raw[n], w[512 * a : 512 * (a + 1), :].rearrange("(p j) c -> p j c", j=PACK))
 
         nc.sync.dma_start(offsets[:], offs)
         scale_rows = tab[0, 512 * T :].bitcast(I32).rearrange("(q w) -> q w", q=32)
@@ -80,16 +83,15 @@ def tile_list_session_memory_blend_kernel(
                 wb_scales_raw[32 * quad : 32 * quad + 4, :].bitcast(I32).rearrange("q (a w) -> q a w", a=PASSES),
                 wb_rows[4 * quad : 4 * quad + 4],
             )
-        load_weight(wg, 1)
+        load_weight(wg, 0, 0)
 
-        wb_codes = keep.tile([P, PASSES * H], U16, name="wb_codes", align_bytes=256)
-        wb_scale_tile = keep.tile([P, PASSES * H], U8, name="wb_scale_tile", align_bytes=256)
+        wb_codes = kept("wb_codes", PASSES * H, U16)
+        wb_scale_tile = kept("wb_scale_tile", PASSES * H, U8)
         nc.scalar.copy(
             wb_codes[:].rearrange("p (a t m) -> p a t m", a=PASSES, t=PACK),
             wb_raw[:].bitcast(U16).rearrange("p (a m t) -> p a t m", a=PASSES, t=PACK),
         )
         nc.vector.tensor_copy(picked_scales[:], tab_scales[:].indirect(offsets[:]))
-        v_scales = (v_scales0, v_scales1)
 
         def place_scales(a):
             for quad in range(QUADS):
@@ -99,17 +101,17 @@ def tile_list_session_memory_blend_kernel(
                 )
 
         place_scales(0)
-        load_weight(wg, 0)
+        load_weight(wg, 1, 1)
         place_scales(1)
-        load_weight(wa, 0)
-        load_weight(wa, 1)
+        load_weight(wa, 0, 2)
+        load_weight(wa, 1, 3)
         nc.sync.dma_start(wo_codes[:], wo_words[0].rearrange("p c i -> p (c i)").bitcast(I32))
         for quad in range(QUADS):
             nc.sync.dma_start(
                 wo_scale_tile[32 * quad : 32 * quad + 4, :].bitcast(I32),
                 wo_scales[0, 4 * quad : 4 * quad + 4, :].bitcast(I32),
             )
-        bias = keep.tile([P, N // P], F32, name="bias", align_bytes=256)
+        bias = kept("bias", N // P, F32)
 
         v_codes = {}
 
@@ -117,51 +119,58 @@ def tile_list_session_memory_blend_kernel(
             cols = BLOCK // 16
             nc.vector.tensor_copy(picked, tab_words[:].bitcast(U32).indirect(offsets[:, q * cols : (q + 1) * cols]))
 
-        def part_words(picked, first, width):
-            if first == 0:
-                parted = shared.tile([P, PASSES * width], U16, name="parted0", offset=0, align_bytes=256)
-            else:
-                parted = keep.tile([P, PASSES * width], U16, name="parted%d" % first, align_bytes=256)
+        def part_words(picked, q):
+            parted = kept("parted%d" % q, PASSES * BLOCK, U16)
             nc.vector.tensor_copy(
                 parted[:].rearrange("p (a s) -> p a s", a=PASSES),
                 picked.bitcast(U16).rearrange("p (s a) -> p a s", a=PASSES),
             )
-            v_codes[first] = parted
+            v_codes[q] = parted
 
-        picked0 = keep.tile([P, BLOCK], U32, name="picked0", align_bytes=256)
-        gather_words(picked0[:], 0)
+        early = kept("early", 2 * BLOCK, U32)
+        gather_words(early[:, :BLOCK], 0)
+        gather_words(early[:, BLOCK:], 1)
+        part_words(early[:, :BLOCK], 0)
         nc.vector.tensor_copy(
             wb_scale_tile[:].rearrange("p (a t m) -> p a t m", a=PASSES, t=PACK),
             wb_scales_raw[:].rearrange("p (a m t) -> p a t m", a=PASSES, t=PACK),
         )
-        part_words(picked0[:], 0, BLOCK)
-        picked = shared.tile([P, 3 * BLOCK], U32, name="picked", offset=2 * H, align_bytes=256)
-        gather_words(picked[:, :BLOCK], 1)
-        gather_words(picked[:, BLOCK : 2 * BLOCK], 2)
-        part_words(picked[:, :BLOCK], BLOCK, BLOCK)
-        gather_words(picked[:, 2 * BLOCK :], 3)
-        for first, width in ((2 * BLOCK, BLOCK), (3 * BLOCK, BLOCK)):
-            part_words(picked[:, first - BLOCK : first - BLOCK + width], first, width)
+        part_words(early[:, BLOCK:], 1)
+        late = shared.tile([P, 2 * BLOCK], U32, name="late", offset=0, align_bytes=ALIGN)
+        gather_words(late[:, :BLOCK], 2)
+        gather_words(late[:, BLOCK:], 3)
 
+        grouped_tiles = [kept("grouped%d" % n, 2 * BANK, F32) for n in range(3)]
+        grouped_tiles.insert(2, grouped_tiles[1])
         w_codes, w_scales = [], []
 
-        def quantise_weight(n):
-            grouped = keep.tile([P, H * PACK], BF16, name="grouped%d" % n, tag="grouped%d" % n, align_bytes=256)
-            cut = VECTOR_SHARE[n]
-            if n >= PASSES:
-                dst = grouped[:].rearrange("p (t m j) -> p m j t", t=PACK, j=PACK)
-                src = raw[n][:].rearrange("p j (m t) -> p m j t", t=PACK)
-                if cut < P:
-                    nc.scalar.activation(dst[:, cut:], src[:, cut:], ACT.Copy, scale=-1.0)
-                nc.vector.tensor_scalar_mul(dst[:, :cut], src[:, :cut], -1.0)
-            else:
-                dst = grouped[:].rearrange("p (t m y z) -> p m y t z", t=PACK, y=2, z=2)
-                src = raw[n][:].rearrange("p (y z) (m t) -> p m y t z", y=2, t=PACK)
+        def cast_weight(n):
+            grouped = grouped_tiles[n][:].bitcast(BF16)
+            if n < PASSES:
+                cut = VECTOR_SHARE[n]
+                dst = grouped.rearrange("p (t m y z) -> p m y t z", t=PACK, y=2, z=2)
+                src = raw[n].rearrange("p (y z) (m t) -> p m y t z", y=2, t=PACK)
                 nc.scalar.copy(dst[:, cut:], src[:, cut:])
-                if cut:
-                    nc.vector.tensor_copy(dst[:, :cut], src[:, :cut])
-            codes = keep.tile([P, H], U32, name="w_codes%d" % n, align_bytes=256)
-            scales = keep.tile([P, H], U8, name="w_scales%d" % n, align_bytes=256)
+                nc.vector.tensor_copy(dst[:, :cut], src[:, :cut])
+                return
+            dst = grouped.rearrange("p (t m j) -> p m j t", t=PACK, j=PACK)
+            src = raw[n].rearrange("p j (m t) -> p m j t", t=PACK)
+            if n == PASSES:
+                cut = VECTOR_SHARE[n]
+                nc.vector.tensor_scalar_mul(dst[:, :cut], src[:, :cut], -1.0)
+                pieces = ((cut, cut + FIRST_PIECE), (cut + FIRST_PIECE, P))
+            else:
+                nc.scalar.activation(dst[:, GPSIMD_SHARE:], src[:, GPSIMD_SHARE:], ACT.Copy, scale=-1.0)
+                pieces = ((0, GPSIMD_SHARE),)
+            dst = grouped.rearrange("p (t m j) -> p m t j", t=PACK, j=PACK)
+            src = raw[n].rearrange("p j (m t) -> p m t j", t=PACK)
+            for lo, hi in pieces:
+                nc.gpsimd.tensor_scalar(dst[:, lo:hi], src[:, lo:hi], -1.0, 0.0, ALU.mult, ALU.add)
+
+        def quantise_weight(n):
+            grouped = grouped_tiles[n][:].bitcast(BF16)
+            codes = kept("w_codes%d" % n, H, U32)
+            scales = kept("w_scales%d" % n, H, U8)
             for u in range(2):
                 cols = slice(u * H // 2, (u + 1) * H // 2)
                 nc.vector.quantize_mx(
@@ -176,23 +185,16 @@ def tile_list_session_memory_blend_kernel(
             if kind == "b":
                 cols = slice(a * H + t * P, a * H + (t + 1) * P)
                 return wb_codes[:, cols].bitcast(FP4X4), wb_scale_tile[:, cols]
-            n = 1 - a if kind == "p" else PASSES + a
+            n = a if kind == "p" else PASSES + a
             cols = slice(t * P, (t + 1) * P)
             return w_codes[n][:, cols].bitcast(FP8X4), w_scales[n][:, cols]
 
         def span(i):
-            if 2 <= i < 2 * BLOCKS:
+            if i < 2 * BLOCKS:
                 return (i // 2) * BLOCK, BLOCK, (2 * (i % 2), 2 * (i % 2) + 1)
             return i * TAIL, TAIL, (0, 1, 2, 3)
 
-        banks, todo = {}, {}
-
-        def open_product(kinds, i, bank):
-            first, width, slots = span(i)
-            acc = psum.tile([P, len(slots), width], F32, name="acc_%s%d" % (kinds, i), tag="bank%d" % bank)
-            banks[kinds, i] = acc
-            todo[kinds, i] = [(kind, a) for kind in kinds for a in ((1, 0) if kind == "p" and i < 4 else (0, 1))]
-            return acc[:].rearrange("p e s -> p s e")
+        banks, todo, acc = {}, {}, {}
 
         def run_pass(kinds, i):
             first, width, slots = span(i)
@@ -205,77 +207,84 @@ def tile_list_session_memory_blend_kernel(
                     out=banks[kinds, i][:, e, :],
                     lhsT=lhs,
                     lhsT_scale=lhs_scale,
-                    rhs=v_codes[q * BLOCK][:, a * BLOCK + lo : a * BLOCK + lo + width].bitcast(FP4X4),
+                    rhs=v_codes[q][:, a * BLOCK + lo : a * BLOCK + lo + width].bitcast(FP4X4),
                     rhs_scale=v_scales[a][:, first : first + width],
                     start=(opening and e == 0),
                     stop=(not todo[kinds, i] and e == len(slots) - 1),
                 )
 
-        def first_product(kinds, i, bank):
-            acc = open_product(kinds, i, bank)
-            while todo[kinds, i]:
+        def open_product(kinds, i, bank, left=0):
+            first, width, slots = span(i)
+            tile = psum.tile([P, len(slots), width], F32, name="acc_%s%d" % (kinds, i), tag="bank%d" % bank)
+            banks[kinds, i] = tile
+            acc[kinds, i] = tile[:].rearrange("p e s -> p s e")
+            todo[kinds, i] = [(kind, a) for kind in kinds for a in range(PASSES)]
+            while len(todo[kinds, i]) > left:
                 run_pass(kinds, i)
-            return acc
 
         def by_token(ap, i):
             return ap.rearrange("p (s e) -> p s e", e=len(span(i)[2]))
 
-        gates = {}
-        rests = {}
-        gated = keep.tile([P, 8 * BANK], F32, name="gated", align_bytes=256)
-        h_rounded = keep.tile([P, S * PACK], BF16, name="h_rounded", align_bytes=256)
-        h_rows = {}
-        h_codes = keep.tile([P, S], U32, name="h_codes", align_bytes=256)
-        h_scales = keep.tile([P, S], U8, name="h_scales", align_bytes=256)
+        gated = kept("gated", 8 * BANK, F32)
+        gate_tile = kept("gate_tile", 7 * BANK, F32)
+        h_rounded = kept("h_rounded", S * PACK, BF16)
+        h_codes = kept("h_codes", S, U32)
+        h_scales = kept("h_scales", S, U8)
         out_rows = out.rearrange("(c p) s -> p c s", p=P)
-        acc_p, acc_b, acc_a, rest_pairs = {}, {}, {}, {}
 
-        def piece(tile, i):
-            return by_token(tile[:, i * BANK : (i + 1) * BANK], i)
+        gates = {i: by_token(gate_tile[:, k * BANK : (k + 1) * BANK], i) for k, i in enumerate((0, 1, 2, 3, 4, 6, 7))}
+        gates[5] = by_token(raw_tiles[3][:, rows_width - TAIL : rows_width - TAIL + BANK], 5)
+        all_rests = kept("all_rests", 8 * BANK, F32)
+        rest_pairs = [all_rests[:, 2 * k * BANK : 2 * (k + 1) * BANK] for k in range(BLOCKS + 1)]
+
+        def rest_rows(i):
+            return rest_pairs[i // 2][:, (i % 2) * BANK : (i % 2 + 1) * BANK]
+
+        def gated_rows(i):
+            return gated[:, i * BANK : (i + 1) * BANK]
 
         def gate(i):
-            nc.scalar.activation(gates[i], acc_p[i], ACT.Tanh, scale=0.5)
+            nc.scalar.activation(gates[i], acc["p", i], ACT.Tanh, scale=0.5)
 
         def rest(i):
-            nc.vector.scalar_tensor_tensor(by_token(rests[i], i), gates[i], 1.0, acc_b[i], ALU.subtract, ALU.mult)
+            nc.vector.scalar_tensor_tensor(by_token(rest_rows(i), i), gates[i], 1.0, acc["b", i], ALU.subtract, ALU.mult)
 
-        def gate_a(i):
-            nc.vector.scalar_tensor_tensor(piece(gated, i), gates[i], 1.0, acc_a[i], ALU.add, ALU.mult)
+        def gate_a(i, kinds="a"):
+            nc.vector.scalar_tensor_tensor(by_token(gated_rows(i), i), gates[i], 1.0, acc[kinds, i], ALU.add, ALU.mult)
 
         def rows(first, count):
-            return h_rounded[:, first * PACK : (first + count) * PACK]
+            place = first
+            return h_rounded[:, place * PACK : (place + count) * PACK]
 
-        def blend_block(k, engine, lo, hi, place):
-            cols = slice(2 * k * BANK, 2 * (k + 1) * BANK)
+        def blend_block(k, engine, lo=0, hi=BLOCK):
             engine.tensor_tensor(
-                rows(place, hi - lo).rearrange("p (s u e) -> p s u e", u=2, e=2),
-                gated[:, cols].rearrange("p (u s e) -> p s u e", u=2, e=2)[:, lo:hi],
+                rows(k * BLOCK + lo, hi - lo).rearrange("p (s u e) -> p s u e", u=2, e=2),
+                gated[:, 2 * k * BANK : 2 * (k + 1) * BANK].rearrange("p (u s e) -> p s u e", u=2, e=2)[:, lo:hi],
                 rest_pairs[k].rearrange("p (u s e) -> p s u e", u=2, e=2)[:, lo:hi],
                 ALU.add,
             )
 
-        def blend_tile(i, engine, lo=0, hi=TAIL):
-            cols = slice(lo * PACK, hi * PACK)
-            engine.tensor_tensor(
-                h_rows[i][:, cols], gated[:, i * BANK : (i + 1) * BANK][:, cols], rests[i][:, cols], ALU.add
-            )
+        def blend_tile(i, engine):
+            engine.tensor_tensor(rows(i * TAIL, TAIL), gated_rows(i), rest_rows(i), ALU.add)
 
         def blend_summed(i):
-            nc.vector.scalar_tensor_tensor(by_token(h_rows[i], i), acc_b[i], -2.0, piece(gated, i), ALU.mult, ALU.add)
+            nc.vector.scalar_tensor_tensor(
+                by_token(rows(i * TAIL, TAIL), i), acc["b", i], -2.0, by_token(gated_rows(i), i), ALU.mult, ALU.add
+            )
 
-        def quantise_h(first, width, rows):
+        def quantise_h(first, width):
             cols = slice(first, first + width)
-            nc.vector.quantize_mx(out=h_codes[:, cols].bitcast(FP8X4), scales=h_scales[:, cols], in_=rows)
+            nc.vector.quantize_mx(out=h_codes[:, cols].bitcast(FP8X4), scales=h_scales[:, cols], in_=rows(first, width))
 
-        def second_product(first, width, banks, shared=False):
+        def second_product(first, width, pair_banks, shared_end=False):
             cols = slice(first, first + width)
             for pair in range(2):
-                staged = ring.tile([P, 2, width], F32, name="staged", tag="staged%d" % pair, align_bytes=256)
-                acc = psum.tile([P, 2, width], F32, name="acc_y", tag="bank%d" % banks[pair])
+                staged = ring.tile([P, 2, width], F32, name="staged", tag="staged%d" % pair, align_bytes=ALIGN)
+                acc_y = psum.tile([P, 2, width], F32, name="acc_y", tag="bank%d" % pair_banks[pair])
                 for e in range(2):
                     c = 2 * pair + e
                     nc.tensor.matmul_mx(
-                        out=acc[:, e, :],
+                        out=acc_y[:, e, :],
                         lhsT=wo_codes[:, c * P : (c + 1) * P].bitcast(FP8X4),
                         lhsT_scale=wo_scale_tile[:, c * P : (c + 1) * P],
                         rhs=h_codes[:, cols].bitcast(FP8X4),
@@ -283,98 +292,100 @@ def tile_list_session_memory_blend_kernel(
                         start=True,
                         stop=True,
                     )
-                if shared and pair == 1:
-                    spread = bias[:, 2:].unsqueeze(2).to_broadcast([P, 2, width])
-                    nc.vector.scalar_tensor_tensor(staged[:], acc[:], -0.5, spread, ALU.mult, ALU.add)
-                else:
-                    for e in range(2):
-                        c = 2 * pair + e
-                        nc.scalar.activation(
-                            staged[:, e, :], acc[:, e, :], ACT.Identity, bias=bias[:, c : c + 1], scale=-0.5
+                for e in range(2):
+                    c = 2 * pair + e
+                    if shared_end and pair == 1:
+                        nc.vector.tensor_scalar(
+                            staged[:, e, :], acc_y[:, e, :], -0.5, bias[:, c : c + 1], ALU.mult, ALU.add
                         )
-                        if width == BLOCK:
-                            nc.sync.dma_start(out_rows[:, c, cols], staged[:, e, :])
-                if width == BLOCK:
-                    continue
-                nc.sync.dma_start(out_rows[:, 2 * pair : 2 * pair + 2, cols], staged[:])
+                    else:
+                        nc.scalar.activation(
+                            staged[:, e, :], acc_y[:, e, :], ACT.Identity, bias=bias[:, c : c + 1], scale=-0.5
+                        )
+                    if width == BLOCK:
+                        nc.sync.dma_start(out_rows[:, c, cols], staged[:, e, :])
+                if width < BLOCK:
+                    nc.sync.dma_start(out_rows[:, 2 * pair : 2 * pair + 2, cols], staged[:])
 
-        for i in (0, 1, 6, 7):
-            h_rows[i] = rows(i * TAIL, TAIL)
         for i in range(4):
-            acc_b[i] = open_product("b", i, i)
-            run_pass("b", i)
-        for i in range(4):
-            run_pass("b", i)
+            open_product("b", i, i, left=1)
+        cast_weight(0)
+        part_words(late[:, :BLOCK], 2)
+        part_words(late[:, BLOCK:], 3)
         quantise_weight(0)
-        for i in range(4):
-            acc_p[i] = open_product("p", i, 4 + i)
-            run_pass("p", i)
+        for i in (0, 2, 1, 3):
+            open_product("p", i, 4 + i, left=1)
+        run_pass("b", 0)
+        run_pass("b", 2)
+        cast_weight(1)
         quantise_weight(1)
         with nc.allow_non_contiguous_dma(reason="one bias value for each partition and block of 128 outputs"):
             nc.sync.dma_start(bias[:], bo.rearrange("(c p) -> p c", p=P))
-        for i in range(4):
+        run_pass("p", 0)
+        run_pass("p", 2)
+        for i in (1, 3):
             run_pass("p", i)
-        quantise_weight(2)
-        early = keep.tile([P, 3 * BANK], F32, name="early", tag="raw2", align_bytes=256)
-        all_rests = keep.tile([P, 8 * BANK], F32, name="all_rests", align_bytes=256)
-        for i in range(8):
-            rests[i] = all_rests[:, i * BANK : (i + 1) * BANK]
-        for k in (1, 2):
-            rest_pairs[k] = all_rests[:, 2 * k * BANK : 2 * (k + 1) * BANK]
-        for i in range(3):
-            gates[i] = piece(early, i)
-            gate(i)
-            rest(i)
-        for i in range(4, 6):
-            acc_p[i] = first_product("p", i, i)
-            acc_b[i] = first_product("b", i, i - 4)
-        quantise_weight(3)
-        late = keep.tile([P, 5 * BANK], F32, name="late", tag="raw3", align_bytes=256)
-        for i in range(3, 8):
-            gates[i] = by_token(late[:, (i - 3) * BANK : (i - 2) * BANK], i)
-        acc_a[0] = first_product("a", 0, 6)
-        acc_a[1] = first_product("a", 1, 2)
+            run_pass("b", i)
+        cast_weight(2)
+        gate(0)
+        open_product("p", 4, 4)
+        gate(2)
+        open_product("b", 4, 6)
+        rest(0)
+        gate(1)
+        open_product("p", 5, 0)
+        open_product("b", 5, 5)
+        rest(2)
         gate(3)
+        open_product("p", 6, 2)
         gate(4)
-        gate(5)
+        rest(1)
+        open_product("ba", 6, 7, left=2)
+        cast_weight(3)
         rest(3)
-        gate_a(0)
-        blend_tile(0, nc.gpsimd)
-        gate_a(1)
-        blend_tile(1, nc.gpsimd)
         rest(4)
-        acc_a[2] = first_product("a", 2, 7)
-        acc_a[3] = first_product("a", 3, 4)
-        acc_p[6] = first_product("p", 6, 5)
+        quantise_weight(2)
+        open_product("a", 0, 4, left=1)
+        open_product("a", 1, 1, left=1)
+        gate(5)
+        quantise_weight(3)
+        run_pass("a", 0)
+        run_pass("a", 1)
         gate(6)
-        acc_a[4] = first_product("a", 4, 6)
-        acc_a[5] = first_product("a", 5, 2)
-        acc_a[6] = first_product("ba", 6, 3)
-        gate_a(2)
-        gate_a(3)
-        blend_block(1, nc.gpsimd, 0, POOL, BLOCK)
-        acc_p[7] = first_product("p", 7, 5)
-        gate(7)
+        open_product("a", 2, 3)
+        open_product("a", 4, 6)
         rest(5)
+        open_product("a", 3, 0)
+        run_pass("ba", 6)
+        run_pass("ba", 6)
+        open_product("a", 5, 5)
+        gate_a(1)
+        open_product("b", 6, 2)
+        gate_a(0)
+        blend_block(0, nc.gpsimd, 0, TAIL)
+        blend_block(0, nc.gpsimd, TAIL, BLOCK)
+        open_product("p", 7, 1)
+        open_product("ba", 7, 4)
+        gate(7)
+        gate_a(2)
         gate_a(4)
+        gate_a(3)
+        blend_block(1, nc.gpsimd, 0, FIRST_POOL)
+        gate_a(6, "ba")
         gate_a(5)
-        quantise_h(0, BLOCK, rows(0, BLOCK))
-        second_product(0, BLOCK, (7, 4))
-        acc_b[6] = first_product("b", 6, 6)
-        blend_block(1, nc.vector, POOL, BLOCK, BLOCK + POOL)
-        gate_a(6)
-        quantise_h(BLOCK, BLOCK, rows(BLOCK, BLOCK))
-        second_product(BLOCK, BLOCK, (5, 0))
-        acc_b[7] = first_product("b", 7, 3)
-        acc_a[7] = first_product("a", 7, 2)
-        blend_block(2, nc.vector, 0, BLOCK, 2 * BLOCK)
         blend_summed(6)
-        quantise_h(2 * BLOCK, BLOCK, rows(2 * BLOCK, BLOCK))
-        second_product(2 * BLOCK, BLOCK, (7, 4))
-        rest(7)
-        gate_a(7)
-        quantise_h(3 * BLOCK, TAIL, h_rows[6])
-        second_product(3 * BLOCK, TAIL, (1, 6))
-        blend_tile(7, nc.vector)
-        quantise_h(3 * BLOCK + TAIL, TAIL, h_rows[7])
-        second_product(3 * BLOCK + TAIL, TAIL, (5, 0), True)
+        quantise_h(0, BLOCK)
+        second_product(0, BLOCK, (6, 0))
+        open_product("b", 7, 3)
+        blend_block(1, nc.vector, FIRST_POOL, BLOCK)
+        quantise_h(3 * BLOCK, TAIL)
+        second_product(3 * BLOCK, TAIL, (7, 5))
+        quantise_h(BLOCK, BLOCK)
+        second_product(BLOCK, BLOCK, (2, 1))
+        blend_block(2, nc.vector)
+        gate_a(7, "ba")
+        quantise_h(2 * BLOCK, BLOCK)
+        second_product(2 * BLOCK, BLOCK, (6, 0))
+        blend_summed(7)
+        quantise_h(3 * BLOCK + TAIL, TAIL)
+        second_product(3 * BLOCK + TAIL, TAIL, (4, 7), True)

@@ -25,11 +25,10 @@ BANK = 512
 BLOCKS = 3
 TAIL = 128
 ALIGN = 256
-FIRST_POOL = 56
-POOL = 136
-VECTOR_SHARE = (48, 76, 64)
-GPSIMD_SHARE = 60
-FIRST_PIECE = 16
+POOL = 128
+FIRST_GATES = (2, 0, 1, 3)
+FIRST_PART = 96
+VECTOR_SHARE = (32, 84, 128, 44)
 
 
 def tile_list_session_memory_blend_kernel(
@@ -49,7 +48,7 @@ def tile_list_session_memory_blend_kernel(
         tab_words = kept("tab_words", T, I32)
         tab_scales = kept("tab_scales", T, U8)
         wb_raw = kept("wb_raw", PASSES * H // 2, I32)
-        wb_scales_raw = shared.tile([P, PASSES * H], U8, name="wb_scales_raw", offset=0, align_bytes=ALIGN)
+        wb_scales_raw = shared.tile([P, PASSES * H], U8, name="wb_scales_raw", offset=H, align_bytes=ALIGN)
         picked_scales = kept("picked_scales", S, U8)
         v_scales = [kept("v_scales%d" % a, S, U8) for a in range(PASSES)]
         wo_codes = kept("wo_codes", N, I32)
@@ -63,8 +62,8 @@ def tile_list_session_memory_blend_kernel(
         nc.vector.memset(wo_scale_tile[:].bitcast(I32), 0)
 
         rows_width = PACK * H
-        raw_tiles = [kept("raw%d" % n, rows_width + (BANK if n == 3 else 0), F32) for n in range(4)]
-        raw = [t[:, :rows_width].rearrange("p (j c) -> p j c", j=PACK) for t in raw_tiles]
+        raw_tiles = [kept("raw%d" % n, rows_width + (TAIL if n == 2 else 0), F32) for n in range(4)]
+        raw = [t[:, t.shape[1] - rows_width :].rearrange("p (j c) -> p j c", j=PACK) for t in raw_tiles]
 
         def load_weight(w, a, n):
             nc.sync.dma_start(raw[n], w[512 * a : 512 * (a + 1), :].rearrange("(p j) c -> p j c", j=PACK))
@@ -140,8 +139,7 @@ def tile_list_session_memory_blend_kernel(
         gather_words(late[:, :BLOCK], 2)
         gather_words(late[:, BLOCK:], 3)
 
-        grouped_tiles = [kept("grouped%d" % n, 2 * BANK, F32) for n in range(3)]
-        grouped_tiles.insert(2, grouped_tiles[1])
+        grouped_tiles = [kept("grouped%d" % n, 2 * BANK, F32) for n in range(4)]
         w_codes, w_scales = [], []
 
         def cast_weight(n):
@@ -155,17 +153,11 @@ def tile_list_session_memory_blend_kernel(
                 return
             dst = grouped.rearrange("p (t m j) -> p m j t", t=PACK, j=PACK)
             src = raw[n].rearrange("p j (m t) -> p m j t", t=PACK)
-            if n == PASSES:
-                cut = VECTOR_SHARE[n]
-                nc.vector.tensor_scalar_mul(dst[:, :cut], src[:, :cut], -1.0)
-                pieces = ((cut, cut + FIRST_PIECE), (cut + FIRST_PIECE, P))
-            else:
-                nc.scalar.activation(dst[:, GPSIMD_SHARE:], src[:, GPSIMD_SHARE:], ACT.Copy, scale=-1.0)
-                pieces = ((0, GPSIMD_SHARE),)
-            dst = grouped.rearrange("p (t m j) -> p m t j", t=PACK, j=PACK)
-            src = raw[n].rearrange("p j (m t) -> p m t j", t=PACK)
-            for lo, hi in pieces:
-                nc.gpsimd.tensor_scalar(dst[:, lo:hi], src[:, lo:hi], -1.0, 0.0, ALU.mult, ALU.add)
+            cut = VECTOR_SHARE[n]
+            if cut < P:
+                nc.scalar.activation(dst[:, cut:], src[:, cut:], ACT.Copy, scale=-1.0)
+            for lo, hi in ((0, FIRST_PART), (FIRST_PART, P)) if cut == P else ((0, cut),):
+                nc.vector.tensor_scalar_mul(dst[:, lo:hi], src[:, lo:hi], -1.0)
 
         def quantise_weight(n):
             grouped = grouped_tiles[n][:].bitcast(BF16)
@@ -190,7 +182,7 @@ def tile_list_session_memory_blend_kernel(
             return w_codes[n][:, cols].bitcast(FP8X4), w_scales[n][:, cols]
 
         def span(i):
-            if i < 2 * BLOCKS:
+            if 2 <= i < 2 * BLOCKS:
                 return (i // 2) * BLOCK, BLOCK, (2 * (i % 2), 2 * (i % 2) + 1)
             return i * TAIL, TAIL, (0, 1, 2, 3)
 
@@ -226,16 +218,16 @@ def tile_list_session_memory_blend_kernel(
             return ap.rearrange("p (s e) -> p s e", e=len(span(i)[2]))
 
         gated = kept("gated", 8 * BANK, F32)
-        gate_tile = kept("gate_tile", 7 * BANK, F32)
+        gate_tile = kept("gate_tile", 4 * BANK, F32)
         h_rounded = kept("h_rounded", S * PACK, BF16)
         h_codes = kept("h_codes", S, U32)
         h_scales = kept("h_scales", S, U8)
         out_rows = out.rearrange("(c p) s -> p c s", p=P)
 
-        gates = {i: by_token(gate_tile[:, k * BANK : (k + 1) * BANK], i) for k, i in enumerate((0, 1, 2, 3, 4, 6, 7))}
-        gates[5] = by_token(raw_tiles[3][:, rows_width - TAIL : rows_width - TAIL + BANK], 5)
-        all_rests = kept("all_rests", 8 * BANK, F32)
-        rest_pairs = [all_rests[:, 2 * k * BANK : 2 * (k + 1) * BANK] for k in range(BLOCKS + 1)]
+        gate_rows = [gate_tile[:, i * BANK : (i + 1) * BANK] for i in range(4)]
+        gate_rows += [raw_tiles[3][:, i * BANK : (i + 1) * BANK] for i in range(4)]
+        gates = [by_token(gate_rows[i], i) for i in range(8)]
+        rest_pairs = [raw_tiles[2][:, 2 * BANK : 4 * BANK], raw_tiles[2][:, : 2 * BANK], grouped_tiles[3][:]]
 
         def rest_rows(i):
             return rest_pairs[i // 2][:, (i % 2) * BANK : (i % 2 + 1) * BANK]
@@ -307,85 +299,81 @@ def tile_list_session_memory_blend_kernel(
                 if width < BLOCK:
                     nc.sync.dma_start(out_rows[:, 2 * pair : 2 * pair + 2, cols], staged[:])
 
-        for i in range(4):
-            open_product("b", i, i, left=1)
-        cast_weight(0)
+        for bank, i in enumerate(FIRST_GATES):
+            open_product("b", i, bank, left=1)
         part_words(late[:, :BLOCK], 2)
         part_words(late[:, BLOCK:], 3)
+        cast_weight(0)
         quantise_weight(0)
-        for i in (0, 2, 1, 3):
-            open_product("p", i, 4 + i, left=1)
-        run_pass("b", 0)
-        run_pass("b", 2)
+        for bank, i in enumerate(FIRST_GATES):
+            open_product("p", i, 4 + bank, left=1)
+        for i in FIRST_GATES:
+            run_pass("b", i)
         cast_weight(1)
         quantise_weight(1)
         with nc.allow_non_contiguous_dma(reason="one bias value for each partition and block of 128 outputs"):
             nc.sync.dma_start(bias[:], bo.rearrange("(c p) -> p c", p=P))
-        run_pass("p", 0)
-        run_pass("p", 2)
-        for i in (1, 3):
+        for i in FIRST_GATES:
             run_pass("p", i)
-            run_pass("b", i)
         cast_weight(2)
-        gate(0)
-        open_product("p", 4, 4)
         gate(2)
-        open_product("b", 4, 6)
-        rest(0)
+        open_product("p", 4, 4)
+        gate(0)
+        open_product("b", 4, 5)
         gate(1)
-        open_product("p", 5, 0)
-        open_product("b", 5, 5)
-        rest(2)
+        open_product("p", 5, 6)
         gate(3)
-        open_product("p", 6, 2)
-        gate(4)
+        open_product("b", 5, 7)
+        rest(2)
+        quantise_weight(2)
+        open_product("a", 0, 0, left=1)
+        rest(0)
+        open_product("a", 1, 1, left=1)
         rest(1)
-        open_product("ba", 6, 7, left=2)
+        open_product("ba", 6, 2, left=1)
         cast_weight(3)
         rest(3)
-        rest(4)
-        quantise_weight(2)
-        open_product("a", 0, 4, left=1)
-        open_product("a", 1, 1, left=1)
-        gate(5)
+        gate(4)
         quantise_weight(3)
         run_pass("a", 0)
         run_pass("a", 1)
-        gate(6)
         open_product("a", 2, 3)
-        open_product("a", 4, 6)
-        rest(5)
-        open_product("a", 3, 0)
+        gate(5)
+        open_product("a", 3, 4)
+        rest(4)
+        open_product("p", 6, 6)
+        open_product("a", 4, 5)
         run_pass("ba", 6)
-        run_pass("ba", 6)
-        open_product("a", 5, 5)
-        gate_a(1)
-        open_product("b", 6, 2)
         gate_a(0)
-        blend_block(0, nc.gpsimd, 0, TAIL)
-        blend_block(0, nc.gpsimd, TAIL, BLOCK)
-        open_product("p", 7, 1)
-        open_product("ba", 7, 4)
-        gate(7)
+        blend_tile(0, nc.gpsimd)
+        open_product("a", 5, 0)
+        gate_a(1)
+        blend_tile(1, nc.gpsimd)
+        gate(6)
+        open_product("b", 6, 1)
+        rest(5)
+        open_product("p", 7, 7)
         gate_a(2)
-        gate_a(4)
         gate_a(3)
-        blend_block(1, nc.gpsimd, 0, FIRST_POOL)
+        blend_block(1, nc.gpsimd, 0, POOL)
+        gate(7)
+        gate_a(4)
         gate_a(6, "ba")
         gate_a(5)
-        blend_summed(6)
         quantise_h(0, BLOCK)
-        second_product(0, BLOCK, (6, 0))
-        open_product("b", 7, 3)
-        blend_block(1, nc.vector, FIRST_POOL, BLOCK)
-        quantise_h(3 * BLOCK, TAIL)
-        second_product(3 * BLOCK, TAIL, (7, 5))
+        second_product(0, BLOCK, (3, 4))
+        open_product("ba", 7, 6)
+        blend_block(1, nc.vector, POOL, BLOCK)
+        blend_summed(6)
         quantise_h(BLOCK, BLOCK)
-        second_product(BLOCK, BLOCK, (2, 1))
+        second_product(BLOCK, BLOCK, (5, 2))
+        open_product("b", 7, 7)
         blend_block(2, nc.vector)
+        quantise_h(3 * BLOCK, TAIL)
+        second_product(3 * BLOCK, TAIL, (0, 1))
         gate_a(7, "ba")
         quantise_h(2 * BLOCK, BLOCK)
-        second_product(2 * BLOCK, BLOCK, (6, 0))
+        second_product(2 * BLOCK, BLOCK, (3, 4))
         blend_summed(7)
         quantise_h(3 * BLOCK + TAIL, TAIL)
-        second_product(3 * BLOCK + TAIL, TAIL, (4, 7), True)
+        second_product(3 * BLOCK + TAIL, TAIL, (6, 5), True)

@@ -25,10 +25,10 @@ BANK = 512
 BLOCKS = 3
 TAIL = 128
 ALIGN = 256
-POOL = 128
+POOL = 80
 FIRST_GATES = (2, 0, 1, 3)
 FIRST_PART = 96
-VECTOR_SHARE = (32, 84, 128, 44)
+VECTOR_SHARE = (16, 72, 128, 44)
 
 
 def tile_list_session_memory_blend_kernel(
@@ -47,8 +47,8 @@ def tile_list_session_memory_blend_kernel(
         offsets = keep.tile([P, S // 16], U16, name="offsets")
         tab_words = kept("tab_words", T, I32)
         tab_scales = kept("tab_scales", T, U8)
-        wb_raw = kept("wb_raw", PASSES * H // 2, I32)
-        wb_scales_raw = shared.tile([P, PASSES * H], U8, name="wb_scales_raw", offset=H, align_bytes=ALIGN)
+        wb_raw = shared.tile([P, PASSES * H // 2], I32, name="wb_raw", offset=0, align_bytes=ALIGN)
+        wb_scales_raw = kept("wb_scales_raw", PASSES * H, U8)
         picked_scales = kept("picked_scales", S, U8)
         v_scales = [kept("v_scales%d" % a, S, U8) for a in range(PASSES)]
         wo_codes = kept("wo_codes", N, I32)
@@ -65,8 +65,9 @@ def tile_list_session_memory_blend_kernel(
         raw_tiles = [kept("raw%d" % n, rows_width + (TAIL if n == 2 else 0), F32) for n in range(4)]
         raw = [t[:, t.shape[1] - rows_width :].rearrange("p (j c) -> p j c", j=PACK) for t in raw_tiles]
 
-        def load_weight(w, a, n):
-            nc.sync.dma_start(raw[n], w[512 * a : 512 * (a + 1), :].rearrange("(p j) c -> p j c", j=PACK))
+        def load_weight(w, a, n, rows=slice(0, PACK)):
+            src = w[512 * a : 512 * (a + 1), :].rearrange("(p j) c -> p j c", j=PACK)
+            nc.sync.dma_start(raw[n][:, rows, :], src[:, rows, :])
 
         nc.sync.dma_start(offsets[:], offs)
         scale_rows = tab[0, 512 * T :].bitcast(I32).rearrange("(q w) -> q w", q=32)
@@ -82,7 +83,7 @@ def tile_list_session_memory_blend_kernel(
                 wb_scales_raw[32 * quad : 32 * quad + 4, :].bitcast(I32).rearrange("q (a w) -> q a w", a=PASSES),
                 wb_rows[4 * quad : 4 * quad + 4],
             )
-        load_weight(wg, 0, 0)
+        load_weight(wg, 1, 0)
 
         wb_codes = kept("wb_codes", PASSES * H, U16)
         wb_scale_tile = kept("wb_scale_tile", PASSES * H, U8)
@@ -100,7 +101,7 @@ def tile_list_session_memory_blend_kernel(
                 )
 
         place_scales(0)
-        load_weight(wg, 1, 1)
+        load_weight(wg, 0, 1)
         place_scales(1)
         load_weight(wa, 0, 2)
         load_weight(wa, 1, 3)
@@ -177,12 +178,12 @@ def tile_list_session_memory_blend_kernel(
             if kind == "b":
                 cols = slice(a * H + t * P, a * H + (t + 1) * P)
                 return wb_codes[:, cols].bitcast(FP4X4), wb_scale_tile[:, cols]
-            n = a if kind == "p" else PASSES + a
+            n = 1 - a if kind == "p" else PASSES + a
             cols = slice(t * P, (t + 1) * P)
             return w_codes[n][:, cols].bitcast(FP8X4), w_scales[n][:, cols]
 
         def span(i):
-            if 2 <= i < 2 * BLOCKS:
+            if i < 2 * BLOCKS:
                 return (i // 2) * BLOCK, BLOCK, (2 * (i % 2), 2 * (i % 2) + 1)
             return i * TAIL, TAIL, (0, 1, 2, 3)
 
@@ -205,12 +206,12 @@ def tile_list_session_memory_blend_kernel(
                     stop=(not todo[kinds, i] and e == len(slots) - 1),
                 )
 
-        def open_product(kinds, i, bank, left=0):
+        def open_product(kinds, i, bank, left=0, order=(0, 1)):
             first, width, slots = span(i)
             tile = psum.tile([P, len(slots), width], F32, name="acc_%s%d" % (kinds, i), tag="bank%d" % bank)
             banks[kinds, i] = tile
             acc[kinds, i] = tile[:].rearrange("p e s -> p s e")
-            todo[kinds, i] = [(kind, a) for kind in kinds for a in range(PASSES)]
+            todo[kinds, i] = [(kind, a) for kind in kinds for a in (order if kind == kinds[-1] else (0, 1))]
             while len(todo[kinds, i]) > left:
                 run_pass(kinds, i)
 
@@ -299,16 +300,16 @@ def tile_list_session_memory_blend_kernel(
                 if width < BLOCK:
                     nc.sync.dma_start(out_rows[:, 2 * pair : 2 * pair + 2, cols], staged[:])
 
-        for bank, i in enumerate(FIRST_GATES):
-            open_product("b", i, bank, left=1)
         part_words(late[:, :BLOCK], 2)
         part_words(late[:, BLOCK:], 3)
+        for bank, i in enumerate(FIRST_GATES[:3]):
+            open_product("b", i, bank, left=1)
         cast_weight(0)
         quantise_weight(0)
-        for bank, i in enumerate(FIRST_GATES):
-            open_product("p", i, 4 + bank, left=1)
-        for i in FIRST_GATES:
+        for i in FIRST_GATES[:3]:
             run_pass("b", i)
+        for bank, i in enumerate(FIRST_GATES):
+            open_product("p", i, 4 + bank, left=1, order=(1, 0))
         cast_weight(1)
         quantise_weight(1)
         with nc.allow_non_contiguous_dma(reason="one bias value for each partition and block of 128 outputs"):
@@ -317,63 +318,65 @@ def tile_list_session_memory_blend_kernel(
             run_pass("p", i)
         cast_weight(2)
         gate(2)
-        open_product("p", 4, 4)
+        open_product("b", 3, 4)
         gate(0)
-        open_product("b", 4, 5)
+        open_product("p", 4, 5)
         gate(1)
-        open_product("p", 5, 6)
+        open_product("b", 4, 6)
         gate(3)
-        open_product("b", 5, 7)
+        open_product("p", 5, 7)
         rest(2)
         quantise_weight(2)
-        open_product("a", 0, 0, left=1)
+        open_product("b", 5, 0)
+        open_product("a", 0, 3, left=1)
         rest(0)
         open_product("a", 1, 1, left=1)
         rest(1)
-        open_product("ba", 6, 2, left=1)
+        open_product("ba", 6, 2, left=2, order=(1, 0))
         cast_weight(3)
         rest(3)
         gate(4)
         quantise_weight(3)
         run_pass("a", 0)
         run_pass("a", 1)
-        open_product("a", 2, 3)
+        open_product("a", 2, 4, order=(1, 0))
         gate(5)
-        open_product("a", 3, 4)
+        open_product("a", 3, 5)
         rest(4)
-        open_product("p", 6, 6)
-        open_product("a", 4, 5)
+        open_product("p", 6, 7)
+        open_product("a", 4, 6)
         run_pass("ba", 6)
-        gate_a(0)
-        blend_tile(0, nc.gpsimd)
-        open_product("a", 5, 0)
+        run_pass("ba", 6)
         gate_a(1)
-        blend_tile(1, nc.gpsimd)
+        open_product("a", 5, 1)
+        gate_a(0)
+        blend_block(0, nc.gpsimd, 0, TAIL)
+        blend_block(0, nc.gpsimd, TAIL, BLOCK)
         gate(6)
-        open_product("b", 6, 1)
+        open_product("b", 6, 3)
         rest(5)
-        open_product("p", 7, 7)
-        gate_a(2)
+        open_product("p", 7, 0)
         gate_a(3)
+        gate_a(2)
         blend_block(1, nc.gpsimd, 0, POOL)
         gate(7)
         gate_a(4)
         gate_a(6, "ba")
         gate_a(5)
         quantise_h(0, BLOCK)
-        second_product(0, BLOCK, (3, 4))
-        open_product("ba", 7, 6)
+        second_product(0, BLOCK, (5, 4))
+        open_product("ba", 7, 7)
         blend_block(1, nc.vector, POOL, BLOCK)
         blend_summed(6)
         quantise_h(BLOCK, BLOCK)
-        second_product(BLOCK, BLOCK, (5, 2))
-        open_product("b", 7, 7)
+        second_product(BLOCK, BLOCK, (6, 2))
+        open_product("b", 7, 4)
         blend_block(2, nc.vector)
         quantise_h(3 * BLOCK, TAIL)
-        second_product(3 * BLOCK, TAIL, (0, 1))
+        second_product(3 * BLOCK, TAIL, (1, 3))
         gate_a(7, "ba")
         quantise_h(2 * BLOCK, BLOCK)
-        second_product(2 * BLOCK, BLOCK, (3, 4))
+        second_product(2 * BLOCK, BLOCK, (5, 0))
         blend_summed(7)
         quantise_h(3 * BLOCK + TAIL, TAIL)
-        second_product(3 * BLOCK + TAIL, TAIL, (6, 5), True)
+        second_product(3 * BLOCK + TAIL, TAIL, (7, 6), True)

@@ -25,7 +25,7 @@ BANK = 512
 BLOCKS = 3
 TAIL = 128
 ALIGN = 256
-POOL = 80
+POOL = 112
 FIRST_GATES = (2, 0, 1, 3)
 FIRST_PART = 96
 VECTOR_SHARE = (16, 72, 128, 44)
@@ -220,7 +220,8 @@ def tile_list_session_memory_blend_kernel(
 
         gated = kept("gated", 8 * BANK, F32)
         gate_tile = kept("gate_tile", 4 * BANK, F32)
-        h_rounded = kept("h_rounded", S * PACK, BF16)
+        h_tiles = [kept("h_rounded%d" % k, BLOCK * PACK, BF16) for k in range(S // BLOCK)]
+        h_halves = kept("h_halves", 4 * BANK, BF16)
         h_codes = kept("h_codes", S, U32)
         h_scales = kept("h_scales", S, U8)
         out_rows = out.rearrange("(c p) s -> p c s", p=P)
@@ -246,8 +247,8 @@ def tile_list_session_memory_blend_kernel(
             nc.vector.scalar_tensor_tensor(by_token(gated_rows(i), i), gates[i], 1.0, acc[kinds, i], ALU.add, ALU.mult)
 
         def rows(first, count):
-            place = first
-            return h_rounded[:, place * PACK : (place + count) * PACK]
+            k, lo = divmod(first, BLOCK)
+            return h_tiles[k][:, lo * PACK : (lo + count) * PACK]
 
         def blend_block(k, engine, lo=0, hi=BLOCK):
             engine.tensor_tensor(
@@ -257,8 +258,18 @@ def tile_list_session_memory_blend_kernel(
                 ALU.add,
             )
 
-        def blend_tile(i, engine):
-            engine.tensor_tensor(rows(i * TAIL, TAIL), gated_rows(i), rest_rows(i), ALU.add)
+        def blend_apart(pieces, count):
+            def runs(ap):
+                return ap.rearrange("p (u c) -> p u c", c=BANK)[:, :, : 2 * count]
+
+            cols = slice(pieces[0] * BANK, (pieces[-1] + 1) * BANK)
+            lo = (pieces[0] % 2) * BANK
+            rest_part = rest_pairs[pieces[0] // 2][:, lo : lo + len(pieces) * BANK]
+            nc.gpsimd.tensor_tensor(runs(h_halves[:, cols]), runs(gated[:, cols]), runs(rest_part), ALU.add)
+
+        def weave(k, count):
+            halves = h_halves[:, 2 * k * BANK : 2 * (k + 1) * BANK].bitcast(U32).rearrange("p (u s) -> p s u", u=2)
+            nc.scalar.copy(rows(k * BLOCK, count).bitcast(U32).rearrange("p (s u) -> p s u", u=2), halves[:, :count])
 
         def blend_summed(i):
             nc.vector.scalar_tensor_tensor(
@@ -347,19 +358,21 @@ def tile_list_session_memory_blend_kernel(
         open_product("a", 4, 6)
         run_pass("ba", 6)
         run_pass("ba", 6)
-        gate_a(1)
-        open_product("a", 5, 1)
         gate_a(0)
-        blend_block(0, nc.gpsimd, 0, TAIL)
-        blend_block(0, nc.gpsimd, TAIL, BLOCK)
+        blend_apart((0,), BLOCK)
+        open_product("a", 5, 3)
+        gate_a(1)
+        blend_apart((1,), BLOCK)
         gate(6)
-        open_product("b", 6, 3)
         rest(5)
-        open_product("p", 7, 0)
+        open_product("p", 7, 1)
+        open_product("b", 6, 0)
         gate_a(3)
         gate_a(2)
-        blend_block(1, nc.gpsimd, 0, POOL)
+        blend_apart((2, 3), POOL)
+        weave(0, BLOCK)
         gate(7)
+        weave(1, POOL)
         gate_a(4)
         gate_a(6, "ba")
         gate_a(5)

@@ -28,7 +28,7 @@ ALIGN = 256
 POOL = 112
 FIRST_GATES = (2, 0, 1, 3)
 FIRST_PART = 96
-VECTOR_SHARE = (16, 72, 128, 44)
+VECTOR_SHARE = (20, 56, 128, 44)
 
 
 def tile_list_session_memory_blend_kernel(
@@ -150,7 +150,8 @@ def tile_list_session_memory_blend_kernel(
                 dst = grouped.rearrange("p (t m y z) -> p m y t z", t=PACK, y=2, z=2)
                 src = raw[n].rearrange("p (y z) (m t) -> p m y t z", y=2, t=PACK)
                 nc.scalar.copy(dst[:, cut:], src[:, cut:])
-                nc.vector.tensor_copy(dst[:, :cut], src[:, :cut])
+                if cut:
+                    nc.vector.tensor_copy(dst[:, :cut], src[:, :cut])
                 return
             dst = grouped.rearrange("p (t m j) -> p m j t", t=PACK, j=PACK)
             src = raw[n].rearrange("p j (m t) -> p m j t", t=PACK)
@@ -296,29 +297,26 @@ def tile_list_session_memory_blend_kernel(
                         start=True,
                         stop=True,
                     )
-                for e in range(2):
-                    c = 2 * pair + e
-                    if shared_end and pair == 1:
-                        nc.vector.tensor_scalar(
-                            staged[:, e, :], acc_y[:, e, :], -0.5, bias[:, c : c + 1], ALU.mult, ALU.add
-                        )
-                    else:
+                if shared_end and pair == 1:
+                    spread = bias[:, 2:].unsqueeze(2).to_broadcast([P, 2, width])
+                    nc.vector.scalar_tensor_tensor(staged[:], acc_y[:], -0.5, spread, ALU.mult, ALU.add)
+                else:
+                    for e in range(2):
+                        c = 2 * pair + e
                         nc.scalar.activation(
                             staged[:, e, :], acc_y[:, e, :], ACT.Identity, bias=bias[:, c : c + 1], scale=-0.5
                         )
-                    if width == BLOCK:
-                        nc.sync.dma_start(out_rows[:, c, cols], staged[:, e, :])
+                        if width == BLOCK:
+                            nc.sync.dma_start(out_rows[:, c, cols], staged[:, e, :])
                 if width < BLOCK:
                     nc.sync.dma_start(out_rows[:, 2 * pair : 2 * pair + 2, cols], staged[:])
 
         part_words(late[:, :BLOCK], 2)
         part_words(late[:, BLOCK:], 3)
-        for bank, i in enumerate(FIRST_GATES[:3]):
+        for bank, i in enumerate(FIRST_GATES):
             open_product("b", i, bank, left=1)
         cast_weight(0)
         quantise_weight(0)
-        for i in FIRST_GATES[:3]:
-            run_pass("b", i)
         for bank, i in enumerate(FIRST_GATES):
             open_product("p", i, 4 + bank, left=1, order=(1, 0))
         cast_weight(1)
@@ -327,46 +325,46 @@ def tile_list_session_memory_blend_kernel(
             nc.sync.dma_start(bias[:], bo.rearrange("(c p) -> p c", p=P))
         for i in FIRST_GATES:
             run_pass("p", i)
+        for i in FIRST_GATES:
+            run_pass("b", i)
         cast_weight(2)
         gate(2)
-        open_product("b", 3, 4)
+        open_product("p", 4, 4)
         gate(0)
-        open_product("p", 4, 5)
+        open_product("b", 4, 5)
         gate(1)
-        open_product("b", 4, 6)
+        open_product("p", 5, 6)
         gate(3)
-        open_product("p", 5, 7)
+        open_product("b", 5, 7)
         rest(2)
         quantise_weight(2)
-        open_product("b", 5, 0)
-        open_product("a", 0, 3, left=1)
+        open_product("a", 0, 0, left=1)
         rest(0)
         open_product("a", 1, 1, left=1)
         rest(1)
-        open_product("ba", 6, 2, left=2, order=(1, 0))
+        open_product("ba", 6, 2, left=1)
         cast_weight(3)
         rest(3)
         gate(4)
         quantise_weight(3)
         run_pass("a", 0)
         run_pass("a", 1)
-        open_product("a", 2, 4, order=(1, 0))
+        open_product("a", 2, 3, order=(1, 0))
         gate(5)
-        open_product("a", 3, 5)
+        open_product("a", 3, 4)
         rest(4)
-        open_product("p", 6, 7)
-        open_product("a", 4, 6)
-        run_pass("ba", 6)
+        open_product("p", 6, 6)
+        open_product("a", 4, 5)
         run_pass("ba", 6)
         gate_a(0)
         blend_apart((0,), BLOCK)
-        open_product("a", 5, 3)
+        open_product("a", 5, 0)
         gate_a(1)
         blend_apart((1,), BLOCK)
         gate(6)
         rest(5)
         open_product("p", 7, 1)
-        open_product("b", 6, 0)
+        open_product("b", 6, 7)
         gate_a(3)
         gate_a(2)
         blend_apart((2, 3), POOL)
@@ -377,19 +375,19 @@ def tile_list_session_memory_blend_kernel(
         gate_a(6, "ba")
         gate_a(5)
         quantise_h(0, BLOCK)
-        second_product(0, BLOCK, (5, 4))
-        open_product("ba", 7, 7)
+        second_product(0, BLOCK, (4, 3))
+        open_product("ba", 7, 6)
         blend_block(1, nc.vector, POOL, BLOCK)
         blend_summed(6)
         quantise_h(BLOCK, BLOCK)
-        second_product(BLOCK, BLOCK, (6, 2))
-        open_product("b", 7, 4)
+        second_product(BLOCK, BLOCK, (5, 2))
+        open_product("b", 7, 3)
         blend_block(2, nc.vector)
         quantise_h(3 * BLOCK, TAIL)
-        second_product(3 * BLOCK, TAIL, (1, 3))
+        second_product(3 * BLOCK, TAIL, (1, 0))
         gate_a(7, "ba")
         quantise_h(2 * BLOCK, BLOCK)
-        second_product(2 * BLOCK, BLOCK, (5, 0))
+        second_product(2 * BLOCK, BLOCK, (4, 7))
         blend_summed(7)
         quantise_h(3 * BLOCK + TAIL, TAIL)
-        second_product(3 * BLOCK + TAIL, TAIL, (7, 6), True)
+        second_product(3 * BLOCK + TAIL, TAIL, (6, 5), True)

@@ -28,7 +28,7 @@ ALIGN = 256
 POOL = 112
 FIRST_GATES = (2, 0, 1, 3)
 FIRST_PART = 96
-VECTOR_SHARE = (20, 56, 128, 44)
+VECTOR_SHARE = (20, 56, 128, 36)
 
 
 def tile_list_session_memory_blend_kernel(
@@ -339,10 +339,10 @@ def tile_list_session_memory_blend_kernel(
         rest(2)
         quantise_weight(2)
         open_product("a", 0, 0, left=1)
+        rest(1)
+        open_product("ba", 6, 2, left=2, order=(1, 0))
         rest(0)
         open_product("a", 1, 1, left=1)
-        rest(1)
-        open_product("ba", 6, 2, left=1)
         cast_weight(3)
         rest(3)
         gate(4)
@@ -355,6 +355,7 @@ def tile_list_session_memory_blend_kernel(
         rest(4)
         open_product("p", 6, 6)
         open_product("a", 4, 5)
+        run_pass("ba", 6)
         run_pass("ba", 6)
         gate_a(0)
         blend_apart((0,), BLOCK)

@@ -25,10 +25,10 @@ BANK = 512
 BLOCKS = 3
 TAIL = 128
 ALIGN = 256
-POOL = 112
+POOL = 88
 FIRST_GATES = (2, 0, 1, 3)
 FIRST_PART = 96
-VECTOR_SHARE = (20, 56, 128, 36)
+VECTOR_SHARE = (20, 56, 128, 30)
 
 
 def tile_list_session_memory_blend_kernel(

@@ -25,10 +25,10 @@ BANK = 512
 BLOCKS = 3
 TAIL = 128
 ALIGN = 256
-POOL = 88
+POOL = 104
 FIRST_GATES = (2, 0, 1, 3)
 FIRST_PART = 96
-VECTOR_SHARE = (20, 56, 128, 30)
+VECTOR_SHARE = (20, 56, 128, 34)
 
 
 def tile_list_session_memory_blend_kernel(
@@ -311,6 +311,23 @@ def tile_list_session_memory_blend_kernel(
                 if width < BLOCK:
                     nc.sync.dma_start(out_rows[:, 2 * pair : 2 * pair + 2, cols], staged[:])
 
+        def second_product_by_rows(first, four_banks):
+            cols = slice(first, first + BLOCK)
+            for c in range(N // P):
+                staged = ring.tile([P, BLOCK], F32, name="row_staged", tag="row_staged", align_bytes=ALIGN)
+                acc_y = psum.tile([P, BLOCK], F32, name="acc_row", tag="bank%d" % four_banks[c])
+                nc.tensor.matmul_mx(
+                    out=acc_y[:],
+                    lhsT=wo_codes[:, c * P : (c + 1) * P].bitcast(FP8X4),
+                    lhsT_scale=wo_scale_tile[:, c * P : (c + 1) * P],
+                    rhs=h_codes[:, cols].bitcast(FP8X4),
+                    rhs_scale=h_scales[:, cols],
+                    start=True,
+                    stop=True,
+                )
+                nc.scalar.activation(staged[:], acc_y[:], ACT.Identity, bias=bias[:, c : c + 1], scale=-0.5)
+                nc.sync.dma_start(out_rows[:, c, cols], staged[:])
+
         part_words(late[:, :BLOCK], 2)
         part_words(late[:, BLOCK:], 3)
         for bank, i in enumerate(FIRST_GATES):
@@ -388,7 +405,7 @@ def tile_list_session_memory_blend_kernel(
         second_product(3 * BLOCK, TAIL, (1, 0))
         gate_a(7, "ba")
         quantise_h(2 * BLOCK, BLOCK)
-        second_product(2 * BLOCK, BLOCK, (4, 7))
+        second_product_by_rows(2 * BLOCK, (4, 7, 5, 2))
         blend_summed(7)
         quantise_h(3 * BLOCK + TAIL, TAIL)
-        second_product(3 * BLOCK + TAIL, TAIL, (6, 5), True)
+        second_product(3 * BLOCK + TAIL, TAIL, (6, 3), True)

from contextlib import ExitStack

import concourse.mybir as mybir

K, T, S, H, N = 1024, 2048, 1024, 512, 512
FLOPS = 2 * K * H * S * 3 + 2 * H * N * S

F32 = mybir.dt.float32
BF16 = mybir.dt.bfloat16
I32 = mybir.dt.int32
U32 = mybir.dt.uint32
U16 = mybir.dt.uint16
U8 = mybir.dt.uint8
FP8X4 = mybir.dt.float8_e4m3fn_x4
FP4X4 = mybir.dt.float4_e2m1fn_x4
ALU = mybir.AluOpType
ACT = mybir.ActivationFunctionType

P = 128
PACK = 4
PASSES = K // (P * PACK)
QUADS = 4
BLOCK = 256
BANK = 512
BLOCKS = 3
TAIL = 128
ALIGN = 256
POOL = 104
FIRST_GATES = (2, 0, 1, 3)
FIRST_PART = 96
VECTOR_SHARE = (20, 56, 128, 34)


def tile_list_session_memory_blend_kernel(
    tc, tab, offs, wg, wa, wb_words, wb_scales, wo_words, wo_scales, bo, out
):
    nc = tc.nc
    with ExitStack() as ctx:
        keep = ctx.enter_context(tc.tile_pool(name="keep", bufs=1))
        ring = ctx.enter_context(tc.tile_pool(name="ring", bufs=5))
        shared = ctx.enter_context(tc.tile_pool(name="shared", bufs=1))
        psum = ctx.enter_context(tc.psum_pool(name="psum", bufs=1))

        def kept(name, width, dtype):
            return keep.tile([P, width], dtype, name=name, align_bytes=ALIGN)

        offsets = keep.tile([P, S // 16], U16, name="offsets")
        tab_words = kept("tab_words", T, I32)
        tab_scales = kept("tab_scales", T, U8)
        wb_raw = shared.tile([P, PASSES * H // 2], I32, name="wb_raw", offset=0, align_bytes=ALIGN)
        wb_scales_raw = kept("wb_scales_raw", PASSES * H, U8)
        picked_scales = kept("picked_scales", S, U8)
        v_scales = [kept("v_scales%d" % a, S, U8) for a in range(PASSES)]
        wo_codes = kept("wo_codes", N, I32)
        wo_scale_tile = kept("wo_scale_tile", N, U8)

        nc.gpsimd.memset(wb_scales_raw[:].bitcast(I32), 0)
        nc.gpsimd.memset(tab_scales[32:64, :].bitcast(I32), 0)
        nc.vector.memset(tab_scales[64:, :].bitcast(I32), 0)
        nc.vector.memset(v_scales[0][:].bitcast(I32), 0)
        nc.vector.memset(v_scales[1][:].bitcast(I32), 0)
        nc.vector.memset(wo_scale_tile[:].bitcast(I32), 0)

        rows_width = PACK * H
        raw_tiles = [kept("raw%d" % n, rows_width + (TAIL if n == 2 else 0), F32) for n in range(4)]
        raw = [t[:, t.shape[1] - rows_width :].rearrange("p (j c) -> p j c", j=PACK) for t in raw_tiles]

        def load_weight(w, a, n, rows=slice(0, PACK)):
            src = w[512 * a : 512 * (a + 1), :].rearrange("(p j) c -> p j c", j=PACK)
            nc.sync.dma_start(raw[n][:, rows, :], src[:, rows, :])

        nc.sync.dma_start(offsets[:], offs)
        scale_rows = tab[0, 512 * T :].bitcast(I32).rearrange("(q w) -> q w", q=32)
        nc.sync.dma_start(tab_scales[:32, :].bitcast(I32), scale_rows)
        nc.sync.dma_start(tab_words[:], tab[0, : 512 * T].rearrange("(p b) -> p b", p=P).bitcast(I32))
        nc.sync.dma_start(
            wb_raw[:].rearrange("p (a w) -> p a w", a=PASSES),
            wb_words.bitcast(I32).rearrange("a p w -> p a w"),
        )
        wb_rows = wb_scales.bitcast(I32).rearrange("a q w -> q a w")
        for quad in range(QUADS):
            nc.sync.dma_start(
                wb_scales_raw[32 * quad : 32 * quad + 4, :].bitcast(I32).rearrange("q (a w) -> q a w", a=PASSES),
                wb_rows[4 * quad : 4 * quad + 4],
            )
        load_weight(wg, 1, 0)

        wb_codes = kept("wb_codes", PASSES * H, U16)
        wb_scale_tile = kept("wb_scale_tile", PASSES * H, U8)
        nc.scalar.copy(
            wb_codes[:].rearrange("p (a t m) -> p a t m", a=PASSES, t=PACK),
            wb_raw[:].bitcast(U16).rearrange("p (a m t) -> p a t m", a=PASSES, t=PACK),
        )
        nc.vector.tensor_copy(picked_scales[:], tab_scales[:].indirect(offsets[:]))

        def place_scales(a):
            for quad in range(QUADS):
                row = 16 * a + 4 * quad
                nc.sync.dma_start(
                    v_scales[a][32 * quad : 32 * quad + 4, :].bitcast(I32), picked_scales[row : row + 4, :].bitcast(I32)
                )

        place_scales(0)
        load_weight(wg, 0, 1)
        place_scales(1)
        load_weight(wa, 0, 2)
        load_weight(wa, 1, 3)
        nc.sync.dma_start(wo_codes[:], wo_words[0].rearrange("p c i -> p (c i)").bitcast(I32))
        for quad in range(QUADS):
            nc.sync.dma_start(
                wo_scale_tile[32 * quad : 32 * quad + 4, :].bitcast(I32),
                wo_scales[0, 4 * quad : 4 * quad + 4, :].bitcast(I32),
            )
        bias = kept("bias", N // P, F32)

        v_codes = {}

        def gather_words(picked, q):
            cols = BLOCK // 16
            nc.vector.tensor_copy(picked, tab_words[:].bitcast(U32).indirect(offsets[:, q * cols : (q + 1) * cols]))

        def part_words(picked, q):
            parted = kept("parted%d" % q, PASSES * BLOCK, U16)
            nc.vector.tensor_copy(
                parted[:].rearrange("p (a s) -> p a s", a=PASSES),
                picked.bitcast(U16).rearrange("p (s a) -> p a s", a=PASSES),
            )
            v_codes[q] = parted

        early = kept("early", 2 * BLOCK, U32)
        gather_words(early[:, :BLOCK], 0)
        gather_words(early[:, BLOCK:], 1)
        part_words(early[:, :BLOCK], 0)
        nc.vector.tensor_copy(
            wb_scale_tile[:].rearrange("p (a t m) -> p a t m", a=PASSES, t=PACK),
            wb_scales_raw[:].rearrange("p (a m t) -> p a t m", a=PASSES, t=PACK),
        )
        part_words(early[:, BLOCK:], 1)
        late = shared.tile([P, 2 * BLOCK], U32, name="late", offset=0, align_bytes=ALIGN)
        gather_words(late[:, :BLOCK], 2)
        gather_words(late[:, BLOCK:], 3)

        grouped_tiles = [kept("grouped%d" % n, 2 * BANK, F32) for n in range(4)]
        w_codes, w_scales = [], []

        def cast_weight(n):
            grouped = grouped_tiles[n][:].bitcast(BF16)
            if n < PASSES:
                cut = VECTOR_SHARE[n]
                dst = grouped.rearrange("p (t m y z) -> p m y t z", t=PACK, y=2, z=2)
                src = raw[n].rearrange("p (y z) (m t) -> p m y t z", y=2, t=PACK)
                nc.scalar.copy(dst[:, cut:], src[:, cut:])
                if cut:
                    nc.vector.tensor_copy(dst[:, :cut], src[:, :cut])
                return
            dst = grouped.rearrange("p (t m j) -> p m j t", t=PACK, j=PACK)
            src = raw[n].rearrange("p j (m t) -> p m j t", t=PACK)
            cut = VECTOR_SHARE[n]
            if cut < P:
                nc.scalar.activation(dst[:, cut:], src[:, cut:], ACT.Copy, scale=-1.0)
            for lo, hi in ((0, FIRST_PART), (FIRST_PART, P)) if cut == P else ((0, cut),):
                nc.vector.tensor_scalar_mul(dst[:, lo:hi], src[:, lo:hi], -1.0)

        def quantise_weight(n):
            grouped = grouped_tiles[n][:].bitcast(BF16)
            codes = kept("w_codes%d" % n, H, U32)
            scales = kept("w_scales%d" % n, H, U8)
            for u in range(2):
                cols = slice(u * H // 2, (u + 1) * H // 2)
                nc.vector.quantize_mx(
                    out=codes[:, cols].bitcast(FP8X4),
                    scales=scales[:, cols],
                    in_=grouped[:, u * H * PACK // 2 : (u + 1) * H * PACK // 2],
                )
            w_codes.append(codes)
            w_scales.append(scales)

        def stationary(kind, a, t):
            if kind == "b":
                cols = slice(a * H + t * P, a * H + (t + 1) * P)
                return wb_codes[:, cols].bitcast(FP4X4), wb_scale_tile[:, cols]
            n = 1 - a if kind == "p" else PASSES + a
            cols = slice(t * P, (t + 1) * P)
            return w_codes[n][:, cols].bitcast(FP8X4), w_scales[n][:, cols]

        def span(i):
            if i < 2 * BLOCKS:
                return (i // 2) * BLOCK, BLOCK, (2 * (i % 2), 2 * (i % 2) + 1)
            return i * TAIL, TAIL, (0, 1, 2, 3)

        banks, todo, acc = {}, {}, {}

        def run_pass(kinds, i):
            first, width, slots = span(i)
            q, lo = divmod(first, BLOCK)
            opening = len(todo[kinds, i]) == PASSES * len(kinds)
            kind, a = todo[kinds, i].pop(0)
            for e, t in enumerate(slots):
                lhs, lhs_scale = stationary(kind, a, t)
                nc.tensor.matmul_mx(
                    out=banks[kinds, i][:, e, :],
                    lhsT=lhs,
                    lhsT_scale=lhs_scale,
                    rhs=v_codes[q][:, a * BLOCK + lo : a * BLOCK + lo + width].bitcast(FP4X4),
                    rhs_scale=v_scales[a][:, first : first + width],
                    start=(opening and e == 0),
                    stop=(not todo[kinds, i] and e == len(slots) - 1),
                )

        def open_product(kinds, i, bank, left=0, order=(0, 1)):
            first, width, slots = span(i)
            tile = psum.tile([P, len(slots), width], F32, name="acc_%s%d" % (kinds, i), tag="bank%d" % bank)
            banks[kinds, i] = tile
            acc[kinds, i] = tile[:].rearrange("p e s -> p s e")
            todo[kinds, i] = [(kind, a) for kind in kinds for a in (order if kind == kinds[-1] else (0, 1))]
            while len(todo[kinds, i]) > left:
                run_pass(kinds, i)

        def by_token(ap, i):
            return ap.rearrange("p (s e) -> p s e", e=len(span(i)[2]))

        gated = kept("gated", 8 * BANK, F32)
        gate_tile = kept("gate_tile", 4 * BANK, F32)
        h_tiles = [kept("h_rounded%d" % k, BLOCK * PACK, BF16) for k in range(S // BLOCK)]
        h_halves = kept("h_halves", 4 * BANK, BF16)
        h_codes = kept("h_codes", S, U32)
        h_scales = kept("h_scales", S, U8)
        out_rows = out.rearrange("(c p) s -> p c s", p=P)

        gate_rows = [gate_tile[:, i * BANK : (i + 1) * BANK] for i in range(4)]
        gate_rows += [raw_tiles[3][:, i * BANK : (i + 1) * BANK] for i in range(4)]
        gates = [by_token(gate_rows[i], i) for i in range(8)]
        rest_pairs = [raw_tiles[2][:, 2 * BANK : 4 * BANK], raw_tiles[2][:, : 2 * BANK], grouped_tiles[3][:]]

        def rest_rows(i):
            return rest_pairs[i // 2][:, (i % 2) * BANK : (i % 2 + 1) * BANK]

        def gated_rows(i):
            return gated[:, i * BANK : (i + 1) * BANK]

        def gate(i):
            nc.scalar.activation(gates[i], acc["p", i], ACT.Tanh, scale=0.5)

        def rest(i):
            nc.vector.scalar_tensor_tensor(by_token(rest_rows(i), i), gates[i], 1.0, acc["b", i], ALU.subtract, ALU.mult)

        def gate_a(i, kinds="a"):
            nc.vector.scalar_tensor_tensor(by_token(gated_rows(i), i), gates[i], 1.0, acc[kinds, i], ALU.add, ALU.mult)

        def rows(first, count):
            k, lo = divmod(first, BLOCK)
            return h_tiles[k][:, lo * PACK : (lo + count) * PACK]

        def blend_block(k, engine, lo=0, hi=BLOCK):
            engine.tensor_tensor(
                rows(k * BLOCK + lo, hi - lo).rearrange("p (s u e) -> p s u e", u=2, e=2),
                gated[:, 2 * k * BANK : 2 * (k + 1) * BANK].rearrange("p (u s e) -> p s u e", u=2, e=2)[:, lo:hi],
                rest_pairs[k].rearrange("p (u s e) -> p s u e", u=2, e=2)[:, lo:hi],
                ALU.add,
            )

        def blend_apart(pieces, count):
            def runs(ap):
                return ap.rearrange("p (u c) -> p u c", c=BANK)[:, :, : 2 * count]

            cols = slice(pieces[0] * BANK, (pieces[-1] + 1) * BANK)
            lo = (pieces[0] % 2) * BANK
            rest_part = rest_pairs[pieces[0] // 2][:, lo : lo + len(pieces) * BANK]
            nc.gpsimd.tensor_tensor(runs(h_halves[:, cols]), runs(gated[:, cols]), runs(rest_part), ALU.add)

        def weave(k, count):
            halves = h_halves[:, 2 * k * BANK : 2 * (k + 1) * BANK].bitcast(U32).rearrange("p (u s) -> p s u", u=2)
            nc.scalar.copy(rows(k * BLOCK, count).bitcast(U32).rearrange("p (s u) -> p s u", u=2), halves[:, :count])

        def blend_summed(i):
            nc.vector.scalar_tensor_tensor(
                by_token(rows(i * TAIL, TAIL), i), acc["b", i], -2.0, by_token(gated_rows(i), i), ALU.mult, ALU.add
            )

        def quantise_h(first, width):
            cols = slice(first, first + width)
            nc.vector.quantize_mx(out=h_codes[:, cols].bitcast(FP8X4), scales=h_scales[:, cols], in_=rows(first, width))

        def second_product(first, width, pair_banks, shared_end=False):
            cols = slice(first, first + width)
            for pair in range(2):
                staged = ring.tile([P, 2, width], F32, name="staged", tag="staged%d" % pair, align_bytes=ALIGN)
                acc_y = psum.tile([P, 2, width], F32, name="acc_y", tag="bank%d" % pair_banks[pair])
                for e in range(2):
                    c = 2 * pair + e
                    nc.tensor.matmul_mx(
                        out=acc_y[:, e, :],
                        lhsT=wo_codes[:, c * P : (c + 1) * P].bitcast(FP8X4),
                        lhsT_scale=wo_scale_tile[:, c * P : (c + 1) * P],
                        rhs=h_codes[:, cols].bitcast(FP8X4),
                        rhs_scale=h_scales[:, cols],
                        start=True,
                        stop=True,
                    )
                if shared_end and pair == 1:
                    spread = bias[:, 2:].unsqueeze(2).to_broadcast([P, 2, width])
                    nc.vector.scalar_tensor_tensor(staged[:], acc_y[:], -0.5, spread, ALU.mult, ALU.add)
                else:
                    for e in range(2):
                        c = 2 * pair + e
                        nc.scalar.activation(
                            staged[:, e, :], acc_y[:, e, :], ACT.Identity, bias=bias[:, c : c + 1], scale=-0.5
                        )
                        if width == BLOCK:
                            nc.sync.dma_start(out_rows[:, c, cols], staged[:, e, :])
                if width < BLOCK:
                    nc.sync.dma_start(out_rows[:, 2 * pair : 2 * pair + 2, cols], staged[:])

        def second_product_by_rows(first, four_banks):
            cols = slice(first, first + BLOCK)
            for c in range(N // P):
                staged = ring.tile([P, BLOCK], F32, name="row_staged", tag="row_staged", align_bytes=ALIGN)
                acc_y = psum.tile([P, BLOCK], F32, name="acc_row", tag="bank%d" % four_banks[c])
                nc.tensor.matmul_mx(
                    out=acc_y[:],
                    lhsT=wo_codes[:, c * P : (c + 1) * P].bitcast(FP8X4),
                    lhsT_scale=wo_scale_tile[:, c * P : (c + 1) * P],
                    rhs=h_codes[:, cols].bitcast(FP8X4),
                    rhs_scale=h_scales[:, cols],
                    start=True,
                    stop=True,
                )
                nc.scalar.activation(staged[:], acc_y[:], ACT.Identity, bias=bias[:, c : c + 1], scale=-0.5)
                nc.sync.dma_start(out_rows[:, c, cols], staged[:])

        part_words(late[:, :BLOCK], 2)
        part_words(late[:, BLOCK:], 3)
        for bank, i in enumerate(FIRST_GATES):
            open_product("b", i, bank, left=1)
        cast_weight(0)
        quantise_weight(0)
        for bank, i in enumerate(FIRST_GATES):
            open_product("p", i, 4 + bank, left=1, order=(1, 0))
        cast_weight(1)
        quantise_weight(1)
        with nc.allow_non_contiguous_dma(reason="one bias value for each partition and block of 128 outputs"):
            nc.sync.dma_start(bias[:], bo.rearrange("(c p) -> p c", p=P))
        for i in FIRST_GATES:
            run_pass("p", i)
        for i in FIRST_GATES:
            run_pass("b", i)
        cast_weight(2)
        gate(2)
        open_product("p", 4, 4)
        gate(0)
        open_product("b", 4, 5)
        gate(1)
        open_product("p", 5, 6)
        gate(3)
        open_product("b", 5, 7)
        rest(2)
        quantise_weight(2)
        open_product("a", 0, 0, left=1)
        rest(1)
        open_product("ba", 6, 2, left=2, order=(1, 0))
        rest(0)
        open_product("a", 1, 1, left=1)
        cast_weight(3)
        rest(3)
        gate(4)
        quantise_weight(3)
        run_pass("a", 0)
        run_pass("a", 1)
        open_product("a", 2, 3, order=(1, 0))
        gate(5)
        open_product("a", 3, 4)
        rest(4)
        open_product("p", 6, 6)
        open_product("a", 4, 5)
        run_pass("ba", 6)
        run_pass("ba", 6)
        gate_a(0)
        blend_apart((0,), BLOCK)
        open_product("a", 5, 0)
        gate_a(1)
        blend_apart((1,), BLOCK)
        gate(6)
        rest(5)
        open_product("p", 7, 1)
        open_product("b", 6, 7)
        gate_a(3)
        gate_a(2)
        blend_apart((2, 3), POOL)
        weave(0, BLOCK)
        gate(7)
        weave(1, POOL)
        gate_a(4)
        gate_a(6, "ba")
        gate_a(5)
        quantise_h(0, BLOCK)
        second_product(0, BLOCK, (4, 3))
        open_product("ba", 7, 6)
        blend_block(1, nc.vector, POOL, BLOCK)
        blend_summed(6)
        quantise_h(BLOCK, BLOCK)
        second_product(BLOCK, BLOCK, (5, 2))
        open_product("b", 7, 3)
        blend_block(2, nc.vector)
        quantise_h(3 * BLOCK, TAIL)
        second_product(3 * BLOCK, TAIL, (1, 0))
        gate_a(7, "ba")
        quantise_h(2 * BLOCK, BLOCK)
        second_product_by_rows(2 * BLOCK, (4, 7, 5, 2))
        blend_summed(7)
        quantise_h(3 * BLOCK + TAIL, TAIL)
        second_product(3 * BLOCK + TAIL, TAIL, (6, 3), True)
